import numpy as np, ml_dtypes
CORES = [2,6,10,14,18,22,26,30]
N = 8
import mx_ref
BF = ml_dtypes.bfloat16
def pick(q, e):
    c = np.concatenate([q[0].reshape(128, -1, 4), np.zeros((128, 1, 4), np.uint8)], axis=1); s = np.concatenate([q[1], np.ones((16, 1), np.uint8)], axis=1)
    return (np.ascontiguousarray(c[:, e].reshape(128, -1)), np.ascontiguousarray(s[:, e]))
def join(*qs):
    return (np.concatenate([q[0] for q in qs], axis=1), np.concatenate([q[1] for q in qs], axis=1))
def put(q, e, v):
    c, s = q[0].reshape(128, -1, 4).copy(), q[1].copy(); c[:, e] = v[0].reshape(128, -1, 4); s[:, e] = v[1]
    return (c.reshape(128, -1), s)
def pk(c, s):
    return (np.ascontiguousarray(c), mx_ref.live(s))
def emit(q):
    return q[0], q[1]
def cols(t, e):
    v = np.concatenate([t.reshape(128, -1, 4), np.zeros((128, 1, 4), BF)], axis=1)
    return np.ascontiguousarray(v[:, e]).reshape(128, -1)
def tile(rs):
    return np.stack(rs, axis=2).reshape(128, -1).astype(BF)
def cut(t, i, w=512):
    return t[:, w * i:w * i + w]
def f(rng, *shape):
    return mx_ref.flush((rng.standard_normal(shape, dtype=np.float32) * np.exp2(rng.integers(-2, 3, shape[:-1] + (1,)))).astype(BF))
def wide(rng, *shape, cols=0):
    v = rng.standard_normal(shape, dtype=np.float32) * np.exp2(rng.integers(-12, 13, shape)).astype(np.float32)
    if cols: v *= np.repeat(np.exp2(rng.integers(-cols, cols + 1, shape[:-2] + (1, shape[-1] // 4))) * (rng.random(shape[:-2] + (1, shape[-1] // 4)) > 0.0625), 4, axis=-1).astype(np.float32)
    return mx_ref.flush(v.astype(BF))
P, K, O = 192, 64, 1
E = P + 2 * K // N
def play(x, u, a, b):
    row = mx_ref.quantize(np.concatenate([x[r] for r in range(N)], axis=1))
    num = 4 * np.arange(N * P)
    k = mx_ref.quantize(np.ascontiguousarray(u[0]))
    high = []
    for t in range(2):
        n = num.size
        s = mx_ref.matmul(k, row)[0] + np.float32(0)
        split = np.sort(np.argsort(-s, kind="stable")[:K])
        parents = pick(row, split)
        kids = []
        for m in (a[0], b[0]):
            kids.append(tile([mx_ref.matmul(mx_ref.quantize(np.ascontiguousarray(cut(m, i))), parents) * np.float32(0.0625) for i in range(4)]))
        size = np.max(np.abs(np.stack(kids).astype(np.float32)).reshape(2, 16, 8, K, 4), axis=(2, 4))
        high.append((np.max(np.abs(s)), np.max(size), np.min(np.where(size == 0, np.float32(1), size))))
        e = np.repeat(np.arange(n), 1 + np.isin(np.arange(n), split))
        first = split + np.arange(K)
        num = num[e]
        num[first + 1] += 2 - t
        e[first] = n + np.arange(K)
        e[first + 1] = n + K + np.arange(K)
        row = pick(join(row, mx_ref.quantize(kids[0]), mx_ref.quantize(kids[1])), e)
    return row, num, high
def times(t, v):
    return mx_ref.flush((t.astype(np.float32) * np.float32(v)).astype(BF))
def lift(d, r, e, v):
    s = np.where(d["u"][0][:, None, :4].astype(np.float32) < 0, -v, v)
    x = np.array(d["x"][r].astype(np.float32)).reshape(128, P, 4)
    x[:, e] = np.abs(x[:, e]) * s
    d["x"][r] = mx_ref.flush(x.reshape(128, -1).astype(BF))
def setup_inputs(rng):
    u = np.array(f(rng, 128, 512))
    u[:, 4:] = 0
    return {"x": np.array(f(rng, N, 128, 4 * P)), "u": np.stack([u] * N), "a": np.stack([f(rng, 128, 2048)] * N), "b": np.stack([f(rng, 128, 2048)] * N), "w": f(rng, N, 128, 512 * O)}
def setup_inputs_below(rng):
    d = setup_inputs(rng)
    d["x"] = np.array(times(d["x"], 2.0 ** 20))
    for r in range(N): lift(d, r, np.arange(P), -1)
    lift(d, N - 1, rng.permutation(P)[:K], -2.0 ** -6)
    v, p = d["a"][0].astype(np.float32) * np.float32(2.0 ** -6), np.arange(128)
    for i in range(4): v[p, 512 * i + 4 * p + i] = 128
    d["a"] = np.stack([mx_ref.flush(v.astype(BF))] * N)
    d["b"] = times(d["a"], 2.0 ** -4)
    return d
def setup_inputs_edge(rng):
    d = setup_inputs(rng)
    d["a"], d["b"], d["x"] = times(d["a"], 2.0 ** -12), times(d["b"], 2.0 ** -12), np.array(times(d["x"], 64))
    lift(d, int(rng.integers(1, N - 1)), rng.permutation(P)[:K], 4096)
    lift(d, N - 1, rng.permutation(P)[:K], 64)
    return d
def setup_inputs_spread(rng):
    return {**setup_inputs(rng), "x": wide(rng, N, 128, 4 * P, cols=6)}
def setup_inputs_ties(rng):
    d = setup_inputs(rng)
    v, e = times(f(rng, 128, 24), 2.0 ** 14), (rng.permutation(N * P) % 6).reshape(N, P)
    d["x"] = np.stack([cols(v, e[r]) for r in range(N)])
    lift(d, N - 1, rng.permutation(P)[:K // 8], 64)
    return {**d, "b": d["a"].copy()}
def setup_inputs_zero(rng):
    d = setup_inputs(rng)
    d["u"][:, 64:] = 0
    for r in range(N):
        kind = rng.permutation(P) % 3
        lift(d, r, np.flatnonzero(kind == 2), -1)
        x = np.array(d["x"][r]).reshape(128, P, 4)
        x[:, kind == 0] = 0
        x[:64, kind == 1] = 0
        d["x"][r] = x.reshape(128, -1)
    return d
def check_inputs(d):
    b = []
    for k in ("x", "u", "a", "b", "w"):
        v = np.abs(d[k].astype(np.float32))
        if not (np.isfinite(v).all() and ((v == 0) | (v >= 2.0 ** -30) & (v <= 2.0 ** 30)).all()): b.append("a value of " + k)
    if (d["u"][:, :, 4:].astype(np.float32) != 0).any(): b.append("u has numbers behind its column 0")
    for k in ("u", "a", "b"):
        v = d[k].astype(np.float32)
        if (v != v[:1]).any(): b.append(k + " differs between ranks")
    if not b:
        try:
            high = play(d["x"], d["u"], d["a"], d["b"])[2]
            if not all(np.isfinite(s) for s, c, m in high): b.append("a score")
            if not all(c <= 2.0 ** 30 and m >= 2.0 ** -30 for s, c, m in high): b.append("a number of a child")
        except Exception:
            b.append("a number of a child")
    return b
def reference(x, u, a, b, w):
    row, num, _ = play(x, u, a, b)
    oc, osc = np.zeros((N, 128, 4 * E), np.uint8), np.zeros((N, 16, E), np.uint8)
    hs, y = np.zeros((N, 1, E), np.float32), np.zeros((N, 128, O * E), np.float32)
    for r in range(N):
        q = pick(row, np.arange(r * E, r * E + E))
        oc[r], osc[r] = emit(q)
        hs[r, 0] = num[r * E:r * E + E]
        for o in range(O):
            y[r, :, o * E:o * E + E] = mx_ref.matmul(mx_ref.quantize(np.ascontiguousarray(cut(w[r], o))), q)
    return {"oc": oc, "osc": osc, "hs": hs, "y": y}

@@ -1,0 +1,464 @@
+from concourse.bass import DstId, RemoteDMATransfer
+from concourse.mybir import dt, AluOpType, AxisListType, ActivationFunctionType
+
+ALU = AluOpType
+ACT = ActivationFunctionType
+N, P, K, E = 8, 192, 64, 208
+WMAX = 336
+TAU = 1e-32
+UNIT = 2048
+MK = 4 * UNIT + 1
+
+SMALL = {}
+for _n, _w in dict(PL=6, PR=6, PT=6, PB=6, PZ=6, RK=6, KEYC=6, V2C=6, RED=3, VV=3, K2=1, H2=1, CC=12, R1=1, R2=1, FF=2, FL=1, FC=8,
+                   S1=1, S2=1, OPC=3, NPC=3, PK1=3, PK2=3, OO=1, AL=3, BC=3, BE=3, BT=3, BF=3, BE2=3, ON3=3, KK3=3, WT1=3, WT2=3, PID=1,
+                   IC=1, PM16=1, QO=1, ISC=1, CK=1, I2=1, NT=1, C1=1, C2=1, RB=7, B0=7, B7=7, ZS=7, Z7=7, Z7B=7, Z7C=7, SRC7=7, HS7=7, GV=4,
+                   GT4=4, GW=8).items():
+    SMALL[_n] = (8 * sum((w + 7) // 8 for _, w in SMALL.values()), _w)
+
+
+def _scratch():
+    f, h, q, s = "float32", "bfloat16", "float8_e4m3fn_x4", "uint8"
+    d = {}
+
+    def sb(dtype, **kw):
+        for name, n in kw.items():
+            d[name] = ("sbuf", [128, n], dtype)
+    sb(h, XB=4 * P, U4=4, UB=512, AB=2048, BB=2048, WB=512, KH1=4 * P, KH2=4 * P, FH1=4 * WMAX, FH2=4 * WMAX,
+       GH1=512, GH2=512, CL=384, CM=6 * 448, J1=448, M1=192, M2=128)
+    for name, n in dict(UQ=128, AQ=512, BQ=512, WQ=128, W1=3 * WMAX, KO1=P, KO2=P, PK=128, W2=3 * WMAX + 256, FQ=E).items():
+        d[name] = ("sbuf", [128, n], q)
+        d[name + "S"] = ("sbuf", [128, n], s)
+    sb(f, Z0=128, OC=2, OCB=64, TOWN=64, SR=192, ST0=192, DL=384, TI0=384, TIE=384, land1=14, LB=448, LT=448, RM=32,
+       SLT=32, SLT2=32, VALR=192, VALT=192, EV=576, ET=576, V3=3, land2=21, CB=384, RR=384, E1=192, E2=128, NK1=192,
+       NK2=128, FB=192, FR=192, L1=192, L2=192, Q1=192, Q2=192, SB7=224, SROW=224, SD=416, STT=416, HB7=224, HROW=224,
+       GD=128, GT=128, YS=E, J3=192, J4=192, SM=8 * sum((w + 7) // 8 for _, w in SMALL.values()))
+    sb("int32", OI=90, OJ=26, PIN=1, PA=3, ZI=7, SI7=7, HI7=7)
+    sb("uint16", OU=64, OD=26, OFFG=8, OFFL=14)
+    for n, w in dict(IP=32, SP=192, SPT=192).items():
+        d[n] = ("sbuf", [128, 7, w], f)
+    d["PS"] = ("psum", [128, 4096], f)
+    return d
+
+
+SCRATCH = _scratch()
+SEMAPHORES = ["cv", "cs", "ct", "cg", "loc", "ar1", "ar2", "arh"] + ["d%d" % i for i in range(16)]
+
+
+def _halo(r):
+    return (0 if r == 0 else 128 - 16 * r), (0 if r == N - 1 else 16 + 16 * r)
+
+
+def rank_program(g, core, T, topo):
+    r = T.rank_of(core)
+    if r is None:
+        return
+    hL, hR = _halo(r)
+    Wn = hL + P + hR
+    ws = P * r - hL
+    G1, G2 = 3 * Wn, 3 * Wn + 128
+    q_of = {"v": g.vector, "s": g.scalar, "t": g.tensor, "g": g, "y": g.sync}
+    cnt = {"cv": 0, "cs": 0, "ct": 0, "cg": 0}
+    known = {k: {} for k in q_of}
+    recs = {}
+    total = {}
+    ndma, loc = [0], [0]
+
+    def C(name, c0=0, c1=None, p0=0, p1=128, step=1):
+        if name in SMALL:
+            o, w = SMALL[name]
+            c0, c1, name = o + c0, o + (w if c1 is None else c1), "SM"
+        elif c1 is None:
+            c1 = SCRATCH[name][1][-1]
+        ap = T[name][p0:p1, c0:c1] if step == 1 else T[name][p0:p1, c0:c1:step]
+        return (ap, name, p0, p1, c0, c1)
+
+    def H(name, c0=0, c1=None):
+        return C(name, c0, c1, 0, 64)
+
+    def B3(name, c0, c1, p0=0, p1=128):
+        return (T[name][p0:p1, :, c0:c1], name, p0, p1, 0, 7 * SCRATCH[name][1][2])
+
+    def B1(name, b):
+        w = SCRATCH[name][1][2]
+        return (T[name][:, b, :], name, 0, 128, b * w, b * w + w)
+
+    def bank(k, n, p0=0, p1=128):
+        return (T.PS[p0:p1, 512 * k:512 * k + n], "PS", 0, 128, 512 * k, 512 * k + 512)
+
+    def ext(ap):
+        return (ap, None, 0, 0, 0, 0)
+
+    def need(q, sem, val, snap):
+        if known[q].get(sem, 0) >= val:
+            return
+        q_of[q].wait_ge(T.sem[sem], val)
+        for k, x in list(snap.items()) + [(sem, val)]:
+            known[q][k] = max(known[q].get(k, 0), x)
+
+    def deps(q, reads, writes):
+        todo = {}
+        for view, wr in [(x, False) for x in reads] + [(x, True) for x in writes]:
+            _, name, p0, p1, c0, c1 = view
+            for (a0, a1, b0, b1, kind, rq, sem, val, snap) in recs.get(name, []):
+                if a0 >= p1 or p0 >= a1 or b0 >= c1 or c0 >= b1:
+                    continue
+                if name != "PS" and not kind and (not wr or rq == q):
+                    continue
+                if val > todo.get(sem, (0, 0))[0]:
+                    todo[sem] = (val, snap)
+        for sem in sorted(todo, key=lambda k: -len(todo[k][1])):
+            need(q, sem, todo[sem][0], todo[sem][1])
+
+    def note(q, rq, sem, val, reads, writes):
+        snap = dict(known[q])
+        snap[sem] = val
+        for view, wr in [(x, False) for x in reads] + [(x, True) for x in writes]:
+            _, name, p0, p1, c0, c1 = view
+            lst = recs.setdefault(name, [])
+            if wr:
+                lst[:] = [x for x in lst if not (x[0] >= p0 and x[1] <= p1 and x[2] >= c0 and x[3] <= c1)]
+            lst.append((p0, p1, c0, c1, wr, rq, sem, val, snap))
+        total[sem] = val
+
+    def run(q, f, reads, writes):
+        deps(q, reads, writes)
+        sem = "c" + q
+        cnt[sem] += 1
+        f().then_inc(T.sem[sem], 1)
+        note(q, q, sem, cnt[sem], reads, writes)
+
+    def dma(q, out, in_, bits=0):
+        w, x = [out] if out[1] else [], [in_] if in_[1] else []
+        deps(q, x, w)
+        sem = "d%d" % ndma[0]
+        ndma[0] += 1
+        o = out[0].bitcast(dt.uint8) if bits & 1 else out[0]
+        i = in_[0].bitcast(dt.uint8) if bits & 2 else in_[0]
+        q_of[q].dma_start(o, i).then_inc(T.sem[sem], 16)
+        note(q, "dma", sem, 16, x, w)
+
+    def memset(o, val):
+        run("v", lambda: g.vector.memset(o[0], val), [], [o])
+
+    def copy(q, o, i):
+        run(q, (lambda: g.vector.tensor_copy(o[0], i[0])) if q == "v" else (lambda: g.scalar.activation(o[0], i[0], ACT.Copy)), [i], [o])
+
+    def scaled(q, o, i, f):
+        run(q, (lambda: g.vector.tensor_scalar(o[0], i[0], f, None, ALU.mult)) if q == "v" else
+            (lambda: g.scalar.activation(o[0], i[0], ACT.Copy, scale=f)), [i], [o])
+
+    def ts(o, i, s1, op0, s2=None, op1=None):
+        rd = [i] + [x for x in (s1, s2) if isinstance(x, tuple)]
+        a = s1[0] if isinstance(s1, tuple) else s1
+        b = s2[0] if isinstance(s2, tuple) else s2
+        run("v", (lambda: g.vector.tensor_scalar(o[0], i[0], a, None, op0)) if op1 is None else
+            (lambda: g.vector.tensor_scalar(o[0], i[0], a, b, op0, op1)), rd, [o])
+
+    def tt(o, a, b, op):
+        run("v", lambda: g.vector.tensor_tensor(o[0], a[0], b[0], op), [a, b], [o])
+
+    def tr(o, i):
+        run("v", lambda: g.vector.transpose(o[0], i[0]), [i], [o])
+
+    def total_of(q, o, i, junk=None):
+        if q == "v":
+            run("v", lambda: g.vector.tensor_reduce(o[0], i[0], AxisListType.X, ALU.add), [i], [o])
+        else:
+            run("s", lambda: g.scalar.activation(junk[0], i[0], ACT.Copy, accum_out=o[0]), [i], [o, junk])
+
+    def minus(o, i, col):
+        run("s", lambda: g.scalar.activation(o[0], i[0], ACT.Identity, bias=col[0], scale=-1.0), [i, col], [o])
+
+    def gather(q, o, win, off):
+        src = win[0].indirect(off[0])
+        run(q, (lambda: g.vector.tensor_copy(o[0], src)) if q == "v" else (lambda: g.scalar.activation(o[0], src, ACT.Copy)), [win, off], [o])
+
+    def quant(name, c0, c1, src):
+        o, s = C(name, c0, c1), C(name + "S", c0, c1)
+        run("v", lambda: g.vector.quantize_mx(o[0], s[0], src[0]), [src], [o, s])
+
+    def mm(o, l, lc, x, x0, x1):
+        a, b, c, d = C(l, lc, lc + 128), C(l + "S", lc, lc + 128), C(x, x0, x1), C(x + "S", x0, x1)
+        run("t", lambda: g.tensor.matmul_mx(o[0], a[0], b[0], c[0], d[0], True, True), [a, b, c, d], [o])
+
+    def iota(o, pattern, base, cm, whole=False):
+        run("g", (lambda: g.iota(o[0], pattern, base, cm)) if whole else
+            (lambda: g.iota(o[0], pattern, base, cm, allow_small_or_imprecise_dtypes=True)), [], [o])
+
+    def pick(o, src, c1, off):
+        a, w = C(o), C(src, 0, c1)
+        run("v", lambda: g.vector.tensor_copy(a[0].bitcast(dt.uint32), w[0].bitcast(dt.uint32).indirect(off[0])), [w, off], [a])
+        gather("s", C(o + "S"), C(src + "S", 0, c1), off)
+
+    def cross(o, w, i, pat):
+        for b in range(4):
+            for q in range(4):
+                copy(pat[(4 * b + q) % len(pat)], C(o, w * b, w * b + w, 32 * q, 32 * q + 32), C(i, 0, w, 32 * b, 32 * b + 32))
+
+    def quadsum(o, h, i, n):
+        for a in (0, 64):
+            tt(C(h, 0, n, a, a + 64), C(i, 0, n, a, a + 64), C(i, 0, n, 64 - a, 128 - a), ALU.add)
+        for q in range(4):
+            a, b = 32 * q, 32 * (q ^ 1)
+            tt(C(o, 0, n, a, a + 32), C(h, 0, n, a, a + 32), C(h, 0, n, b, b + 32), ALU.add)
+
+    def kids(src, c0, n, t1, t2, first, pat):
+        for i in range(8):
+            k = (first + i) % 8
+            mm(bank(k, n), "AQ" if i < 4 else "BQ", 128 * (i % 4), src, c0, c0 + n)
+            scaled(pat[i], C(t1 if i < 4 else t2, i % 4, 4 * n, step=4), bank(k, n), 0.0625)
+
+    def fan(src, dst, width, arr):
+        deps("g", [src], [])
+        others = [c for c in T.cores if c != core]
+        far = [c for c in others if topo.chip(c) != topo.chip(core)]
+        near = [c for c in others if topo.chip(c) == topo.chip(core)]
+        fe = topo.engines(core, far[0])
+        ne = [e for e in topo.engines(core, near[0]) if e not in fe]
+
+        def tf(dsts, eng):
+            ids, aps = [], []
+            for c in dsts:
+                d = T.rank_of(c)
+                k = width * (r if r < d else r - 1)
+                rid, pid, _ = topo.addr(c)
+                ids.append(DstId(rid=rid, pnc=pid))
+                aps.append(T[dst][:, k:k + width])
+            return RemoteDMATransfer(dst_ids=ids, dma_engine_mask=sum(1 << e for e in eng), remote_sem=T.sem[arr], srcs=[src[0]], dsts=aps)
+        g.remote_dma_fused([tf(far, fe), tf(near, ne)], local_sem=T.sem.loc)
+        loc[0] += len(fe) + len(ne)
+
+    def halo(d, c0, c1, at):
+        c = T.cores[d]
+        rid, pid, _ = topo.addr(c)
+        for name in ("W1", "W1S"):
+            s = C(name, hL + c0, hL + c1)
+            deps("g", [s], [])
+            o, i = T[name][:, at:at + c1 - c0], s[0]
+            if name == "W1":
+                o, i = o.bitcast(dt.uint8), i.bitcast(dt.uint8)
+            g.remote_dma(o, i, T.sem.arh, T.sem.loc, pid, rid, topo.mask(core, c))
+            loc[0] += len(topo.engines(core, c))
+
+    def arrive(sem, val, writes):
+        for _, name, p0, p1, c0, c1 in writes:
+            recs.setdefault(name, []).append((p0, p1, c0, c1, True, "far", sem, val, {sem: val}))
+        total[sem] = val
+
+    dma("s", C("U4"), ext(T.u[:, 0:4]))
+    dma("y", C("XB"), ext(T.x[:, :]))
+    dma("s", C("AB"), ext(T.a[:, :]))
+    dma("y", C("BB"), ext(T.b[:, :]))
+    dma("y", C("WB"), ext(T.w[:, :]))
+
+    memset(C("Z0"), 0.0)
+    memset(C("OC", 1, 2, 0, 64), -9e29)
+    memset((T.SP[64:128, :, 96:192], "SP", 64, 128, 0, 7 * 192), 0.0)
+    memset(C("AL"), 0.0)
+    memset(C("FF"), 0.0)
+    for k, v in enumerate((Wn, Wn + UNIT - MK, -(2 * Wn + UNIT))):
+        memset(C("BE2", k, k + 1), float(v))
+    iota(C("PIN"), [[0, 1]], 0, 1, True)
+    iota(C("PID"), [[0, 1]], 0, 1)
+    iota(C("OI", 0, 28), [[1, 14], [0, 2]], 0, 0, True)
+    iota(C("RK"), [[64, 6]], 2 * P * r, 0)
+    iota(C("RM"), [[1, 32]], 0, 0)
+    iota(C("TI0"), [[-32, 6], [64, 2], [1, 32]], 0, 0)
+    for k, m in enumerate((31, 15, 32)):
+        ts(C("PA", k, k + 1), C("PIN"), m, ALU.bitwise_and)
+        copy("v", C(("IC", "PM16", "QO")[k]), C("PA", k, k + 1))
+    ts(C("ISC"), C("PID"), 64.0, ALU.is_ge)
+    ts(C("I2"), C("IC"), 2.0, ALU.mult)
+    ts(C("CK"), C("I2"), C("ISC"), ALU.add)
+    ts(C("NT"), C("I2"), C("PID"), ALU.subtract)
+
+    for t in range(4):
+        ts(C("UB", t, 512, step=4), C("Z0"), C("U4", t, t + 1), ALU.add)
+    quant("UQ", 0, 128, C("UB"))
+    quant("W1", hL, hL + P, C("XB"))
+    mm(bank(1, 128), "W1", hL, "UQ", 0, 128)
+    mm(bank(2, 128), "W1", hL + 64, "UQ", 0, 128)
+    mm(bank(0, P), "UQ", 0, "W1", hL, hL + P)
+    copy("v", C("OC", 0, 1), bank(1, 1))
+    copy("v", C("OC", 1, 2, 64, 128), bank(2, 1, 64, 128))
+    fan(C("OC"), "land1", 2, "ar1")
+    arrive("ar1", 8 * 7, [C("land1")])
+    if r + 1 < N:
+        halo(r + 1, P - _halo(r + 1)[0], P, 0)
+    if r > 0:
+        halo(r - 1, 0, _halo(r - 1)[1], _halo(r - 1)[0] + P)
+    want = sum(2 * len(topo.engines(T.cores[d], core)) for d in (r - 1, r + 1) if 0 <= d < N)
+    arrive("arh", want, [C(n, a, b) for n in ("W1", "W1S") for a, b in ((0, hL), (hL + P, Wn)) if b > a])
+    iota(C("OI", 28, 36), [[3, 4], [0, 2]], 0, 0, True)
+    iota(C("OI", 36, 40), [[3, 2], [0, 2]], 2, 0, True)
+    iota(C("OI", 40, 48), [[3, 4], [0, 2]], 1, 0, True)
+    iota(C("OI", 48, 52), [[3, 2], [0, 2]], 8, 0, True)
+    iota(C("OI", 52, 60), [[2, 4], [0, 2]], 0, 0, True)
+    iota(C("OI", 60, 64), [[2, 2], [0, 2]], 1, 0, True)
+    iota(C("OI", 64, 90), [[16, 13], [0, 2]], 0, 0, True)
+    iota(C("RB"), [[32, 7]], E * r, 0)
+    iota(C("ON3"), [[1, 3]], -1, 0)
+    iota(C("KK3"), [[1, 3]], 0, 0)
+    iota((T.IP[:, :, :], "IP", 0, 128, 0, 224), [[32, 7], [1, 32]], E * r, 0)
+
+    copy("s", C("SR"), bank(0, P))
+    copy("v", C("OU", 0, 28), C("OI", 0, 28))
+    gather("v", C("OCB"), C("OC"), C("OU", 0, 4))
+    ts(C("TIE"), C("TI0"), C("NT"), ALU.is_lt, -TAU, ALU.mult)
+    tr(C("TOWN"), C("OCB"))
+    tr(C("ST0"), C("SR"))
+    for k in range(6):
+        ts(C("DL", 64 * k, 64 * k + 64), C("TOWN"), C("ST0", 32 * k, 32 * k + 1), ALU.subtract)
+    tt(C("CL"), C("DL"), C("TIE"), ALU.is_gt)
+
+    quant("AQ", 0, 512, C("AB"))
+    kids_pat = "ssssssss"
+    quant("BQ", 0, 512, C("BB"))
+    kids("W1", hL, P, "KH1", "KH2", 3, kids_pat)
+    for k in range(6):
+        total_of("v", C("PL", k, k + 1), C("CL", 64 * k, 64 * k + 64))
+    ts(C("SLT"), C("RM"), C("QO"), ALU.add)
+    ts(C("SLT2"), C("SLT"), 64.0, ALU.add)
+    ts(C("KEYC"), C("RK"), C("CK"), ALU.add)
+    copy("v", C("V2C", 0, 6, 0, 64), C("ST0", 0, 192, 0, 64, 32))
+    ts(C("V2C", 0, 6, 64, 128), C("RK", 0, 6, 64, 128), C("I2", 0, 1, 64, 128), ALU.add)
+
+    gather("v", C("LB"), C("land1"), C("OU", 0, 28))
+    tr(C("LT"), C("LB"))
+
+    def against(ks):
+        for k in ks:
+            sc = C("ST0", 32 * k, 32 * k + 1)
+            if r > 0:
+                ts(C("CM", 448 * k, 448 * k + 64 * r), C("LT", 0, 64 * r), sc, ALU.is_ge)
+            if r < N - 1:
+                ts(C("CM", 448 * k + 64 * r, 448 * k + 448), C("LT", 64 * r, 448), sc, ALU.is_gt)
+            total_of("s", C("PR", k, k + 1), C("CM", 448 * k, 448 * k + 448), C("J1"))
+    against((0, 1, 2))
+    quant("KO1", 0, P, C("KH1"))
+    quant("KO2", 0, P, C("KH2"))
+    mm(bank(3, P), "UQ", 0, "KO1", 0, P)
+    mm(bank(4, P), "UQ", 0, "KO2", 0, P)
+    against((3, 4, 5))
+    copy("v", C("VALR", p0=0, p1=64), bank(3, P, 0, 64))
+    copy("v", C("VALR", p0=64, p1=128), bank(4, P, 64, 128))
+    tr(C("VALT"), C("VALR"))
+    tt(C("PT"), C("PR"), C("PL"), ALU.add)
+    quadsum("PZ", "PB", "PT", 6)
+    for v in range(3):
+        for k in range(6):
+            val = (C("KEYC", k, k + 1), C("V2C", k, k + 1), C("VALT", 32 * k, 32 * k + 1))[v]
+            ts(C("EV", 192 * v + 32 * k, 192 * v + 32 * k + 32), C("SLT2" if v == 1 else "SLT"), C("PZ", k, k + 1), ALU.is_equal, val, ALU.mult)
+        tr(C("ET", 192 * v, 192 * v + 192), C("EV", 192 * v, 192 * v + 192))
+        c = (1, 2, 0)[v]
+        total_of("ssv"[v], C("V3", c, c + 1), C("ET", 192 * v, 192 * v + 192), C("J3"))
+    fan(C("V3"), "land2", 3, "ar2")
+    arrive("ar2", 8 * 7, [C("land2")])
+
+    copy("v", C("OU", 28, 64), C("OI", 28, 64))
+    ts(C("OJ"), C("OI", 64, 90), C("PM16"), ALU.add)
+    copy("v", C("OD"), C("OJ"))
+    ts(C("B0"), C("RB"), C("IC"), ALU.add, float(MK), ALU.mult)
+    ts(C("B7"), C("B0"), float(-ws), ALU.add)
+    c1, cc = float(Wn), float(Wn + 2 * UNIT)
+    ts(C("AL", 0, 1), C("ISC"), cc - MK, ALU.mult, c1, ALU.add)
+    ts(C("AL", 1, 2), C("ISC"), -cc, ALU.mult, -c1, ALU.add)
+    ts(C("C1"), C("ISC"), 2.0 * UNIT - cc, ALU.mult, G1 + ws - c1, ALU.add)
+    ts(C("BC", 0, 1), C("C1"), C("PID"), ALU.add)
+    ts(C("BC", 1, 2), C("ISC"), cc, ALU.mult, c1 + G2 - G1 + UNIT - MK, ALU.add)
+    ts(C("C2"), C("ISC"), -2.0 * UNIT, ALU.mult, float(-(G2 + ws + UNIT)), ALU.add)
+    ts(C("BC", 2, 3), C("C2"), C("PID"), ALU.subtract)
+    kids("W1", 0, Wn, "FH1", "FH2", 5, "svsvsvsv")
+    quant("W1", Wn, 2 * Wn, C("FH1", 0, 4 * Wn))
+    quant("W1", 2 * Wn, 3 * Wn, C("FH2", 0, 4 * Wn))
+    dma("y", C("W2", 0, 3 * Wn), C("W1", 0, 3 * Wn), bits=3)
+    dma("y", C("W2S", 0, 3 * Wn), C("W1S", 0, 3 * Wn))
+    quant("WQ", 0, 128, C("WB"))
+
+    for k in range(3):
+        total_of("v", C("RED", k, k + 1), C("land2", k, 21, step=3))
+    tt(C("VV"), C("RED"), C("V3"), ALU.add)
+    cross("CC", 3, "VV", "vs")
+    copy("v", C("K2", 0, 1, 0, 64), C("VV", 2, 3, 64, 128))
+    gather("v", C("CB"), C("CC"), C("OU", 28, 52))
+    tr(C("RR"), C("CB"))
+    minus(C("E1"), C("RR", 0, 192), C("VV", 0, 1))
+    minus(H("E2"), H("RR", 0, 128), H("VV", 2, 3))
+    ts(C("NK1"), C("RR", 192, 384), C("VV", 1, 2), ALU.subtract, -TAU, ALU.mult)
+    ts(H("NK2"), H("RR", 192, 320), H("K2"), ALU.subtract, -TAU, ALU.mult)
+    tt(C("M1"), C("E1"), C("NK1"), ALU.is_lt)
+    tt(H("M2"), H("E2"), H("NK2"), ALU.is_lt)
+    total_of("v", C("R1"), C("M1"))
+    total_of("v", H("R2"), H("M2"))
+    ts(C("FF", 0, 1), C("R1"), 64.0, ALU.is_lt, C("ISC"), ALU.add)
+    ts(H("FF", 1, 2), H("R2"), H("PID"), ALU.add, 64.0, ALU.is_lt)
+    cross("FC", 2, "FF", "vs")
+    ts(C("L1"), C("RR", 192, 384), C("VV", 1, 2), ALU.is_lt)
+    gather("v", C("FB"), C("FC"), C("OU", 52, 64))
+    tr(C("FR"), C("FB"))
+    ts(H("L2"), H("RR", 192, 384), H("K2"), ALU.is_lt)
+    tt(C("Q1"), C("L1"), C("FR"), ALU.mult)
+    total_of("s", C("S1"), C("Q1"), C("J3"))
+    tt(H("Q2"), H("L2"), H("FR"), ALU.mult)
+    total_of("s", H("S2"), H("Q2"), H("J4"))
+
+    gather("v", C("GD"), C("RR", 192, 256), C("OD", 0, 8))
+    tr(C("GT"), C("GD"))
+    ts(C("GV"), C("GT", 0, 128, step=32), 0.5, ALU.mult, float(-ws), ALU.add)
+    ts(C("GT4"), C("GV"), 0.0, ALU.max, float(Wn - 1), ALU.min)
+    ts(C("OFFG", 0, 4), C("GT4"), float(Wn), ALU.add)
+    ts(C("OFFG", 4, 8), C("GT4"), float(2 * Wn), ALU.add)
+    pick("PK", "W1", 3 * Wn, C("OFFG"))
+
+    ts(C("FL"), C("R1"), 64.0, ALU.is_lt)
+    ts(C("OO"), C("VV", 1, 2), C("ISC"), ALU.subtract, 0.5, ALU.mult)
+    ts(C("BE"), C("ON3"), C("OO"), ALU.mult)
+    tt(C("BT"), C("BE"), C("BC"), ALU.add)
+    ts(C("BF"), C("BT"), C("FL"), ALU.mult)
+    tt(C("WT1"), C("BF"), C("AL"), ALU.add)
+    ts(H("WT2"), H("BE2"), H("FF", 1, 2), ALU.mult)
+    ts(C("OPC"), C("KK3"), C("OO"), ALU.add, C("ISC"), ALU.add)
+    ts(H("H2"), H("K2"), 0.5, ALU.mult)
+    ts(H("NPC"), H("KK3"), H("H2"), ALU.add)
+    ts(C("PK1"), C("OPC"), C("S1"), ALU.add)
+    ts(H("PK2"), H("NPC"), H("S2"), ALU.add)
+    kids("PK", 0, 128, "GH1", "GH2", 5, "ssssssss")
+
+    for k in range(3):
+        ts(B3("SP", 32 * k, 32 * k + 32), (T.IP[:, :, :], "IP", 0, 128, 0, 224), C("PK1", k, k + 1), ALU.is_ge, C("WT1", k, k + 1), ALU.mult)
+        ts(B3("SP", 96 + 32 * k, 128 + 32 * k, 0, 64), (T.IP[0:64, :, :], "IP", 0, 64, 0, 224), H("PK2", k, k + 1), ALU.is_ge, H("WT2", k, k + 1), ALU.mult)
+    for b in range(7):
+        tr(B1("SPT", b), B1("SP", b))
+        total_of("svsvsvv"[b], C("ZS", b, b + 1), B1("SPT", b), C("J3"))
+    quant("W2", G1, G1 + 128, C("GH1"))
+    quant("W2", G2, G2 + 128, C("GH2"))
+    quadsum("Z7B", "Z7", "ZS", 7)
+    tt(C("Z7C"), C("Z7B"), C("B7"), ALU.add)
+    copy("v", C("ZI"), C("Z7C"))
+    ts(C("SI7"), C("ZI"), UNIT - 1, ALU.bitwise_and)
+    copy("v", C("SRC7"), C("SI7"))
+    gather("v", C("SB7"), C("SRC7"), C("OU", 0, 14))
+    tr(C("SROW"), C("SB7"))
+    gather("v", C("SD", 0, 208), C("SROW"), C("OD", 0, 13))
+    gather("s", C("SD", 208, 416), C("SROW"), C("OD", 13, 26)) if False else gather("v", C("SD", 208, 416), C("SROW"), C("OD", 13, 26)) if False else None
+    gather("v", C("SD", 192, 416), C("SROW"), C("OD", 12, 26))
+    tr(C("STT"), C("SD"))
+    copy("v", C("OFFL", 0, 13), C("STT", 0, 416, step=32))
+    pick("FQ", "W2", 3 * Wn + 256, C("OFFL", 0, 13))
+    mm(bank(0, E), "WQ", 0, "FQ", 0, E)
+    dma("y", ext(T.oc[:, :]), C("FQ"), bits=2)
+    for k in range(4):
+        dma("ys"[k % 2], ext(T.osc[4 * k:4 * k + 4, :]), C("FQS", 0, E, 32 * k, 32 * k + 4))
+    copy("v", C("YS"), bank(0, E))
+    dma("y", ext(T.y[:, :]), C("YS"))
+    ts(C("HI7"), C("ZI"), 11, ALU.logical_shift_right)
+    copy("v", C("HS7"), C("HI7"))
+    gather("v", C("HB7"), C("HS7"), C("OU", 0, 14))
+    tr(C("HROW"), C("HB7"))
+    dma("s", ext(T.hs[:, :]), C("HROW", 0, E, 0, 1))
+
+    total["loc"] = loc[0]
+    for sem in SEMAPHORES:
+        if total.get(sem):
+            need("g", sem, total[sem], {})

@@ -6,14 +6,14 @@ ACT = ActivationFunctionType
 N, P, K, E = 8, 192, 64, 208
 WMAX = 336
 TAU = 1e-32
+BIG = 65536.0
 UNIT = 2048
 MK = 4 * UNIT + 1
 
 SMALL = {}
-for _n, _w in dict(PL=6, PR=6, PT=6, PB=6, PZ=6, RK=6, KEYC=6, V2C=6, RED=3, VV=3, K2=1, H2=1, CC=12, R1=1, R2=1, FF=2, FL=1, FC=8,
-                   S1=1, S2=1, OPC=3, NPC=3, PK1=3, PK2=3, OO=1, AL=3, BC=3, BE=3, BT=3, BF=3, BE2=3, ON3=3, KK3=3, WT1=3, WT2=3, PID=1,
-                   IC=1, PM16=1, QO=1, ISC=1, CK=1, I2=1, NT=1, C1=1, C2=1, RB=7, B0=7, B7=7, ZS=7, Z7=7, Z7B=7, Z7C=7, SRC7=7, HS7=7, GV=4,
-                   GT4=4, GW=8).items():
+for _n, _w in dict(PL=6, PR=6, PT=6, PB=6, PZ=6, RK=6, KEYC=6, KEYN=6, V2C=6, RED=3, VV=3, NS=1, NC=1, CC=12, R1=1, R2=1, FF=2, FL=1, F2=1, FC=8,
+                   S1=1, S2=1, OO=1, AL=3, BC=3, BT=3, BEA=1, BEB=1, WTA=1, WTB=1, WT1=3, PID=1, KB=1, NB=1, TH=1, HIS=1, NIS=1,
+                   IC=1, PM16=1, QO=1, P63=1, ISC=1, E64=1, CK=1, I2=1, NT=1, C1=1, C2=1, ZS=7, Z7=7, HS7=7, GV=4, GT4=4).items():
     SMALL[_n] = (8 * sum((w + 7) // 8 for _, w in SMALL.values()), _w)
 
 
@@ -25,17 +25,17 @@ def _scratch():
         for name, n in kw.items():
             d[name] = ("sbuf", [128, n], dtype)
     sb(h, XB=4 * P, U4=4, UB=512, AB=2048, BB=2048, WB=512, KH1=4 * P, KH2=4 * P, FH1=4 * WMAX, FH2=4 * WMAX,
-       GH1=512, GH2=512, CL=384, CM=6 * 448, J1=448, M1=192, M2=128)
+       GH1=512, GH2=512, CL=384, CM=6 * 352, J1=352, M1=192, M2=128)
     for name, n in dict(UQ=128, AQ=512, BQ=512, WQ=128, W1=3 * WMAX, KO1=P, KO2=P, PK=128, W2=3 * WMAX + 256, FQ=E).items():
         d[name] = ("sbuf", [128, n], q)
         d[name + "S"] = ("sbuf", [128, n], s)
-    sb(f, Z0=128, OC=2, OCB=64, TOWN=64, SR=192, ST0=192, DL=384, TI0=384, TIE=384, land1=14, LB=448, LT=448, RM=32,
-       SLT=32, SLT2=32, VALR=192, VALT=192, EV=576, ET=576, V3=3, land2=21, CB=384, RR=384, E1=192, E2=128, NK1=192,
-       NK2=128, FB=192, FR=192, L1=192, L2=192, Q1=192, Q2=192, SB7=224, SROW=224, SD=416, STT=416, HB7=224, HROW=224,
-       GD=128, GT=128, YS=E, J3=192, J4=192, SM=8 * sum((w + 7) // 8 for _, w in SMALL.values()))
-    sb("int32", OI=90, OJ=26, PIN=1, PA=3, ZI=7, SI7=7, HI7=7)
-    sb("uint16", OU=64, OD=26, OFFG=8, OFFL=14)
-    for n, w in dict(IP=32, SP=192, SPT=192).items():
+    sb(f, Z0=128, OC=3, OCB=64, TOWN=64, ST0=192, DL=384, TI0=384, TIE=384, land1=21, LB=352, LT=352, RM=32,
+       SLT=32, SLT2=32, VALT=192, AD=192, EV=576, ET=576, V3=3, land2=21, CB=384, RR=384, E1=192, E2=128, NK1=192,
+       NK2=128, FB=192, FR=256, Q1=257, Q2=257, SB7=224, SROW=224, SD=416, STT=416, HB7=224, HROW=224,
+       GD=128, GT=128, YS=E, J3=257, SM=8 * sum((w + 7) // 8 for _, w in SMALL.values()))
+    sb("int32", OI=102, OJ=26, PIN=1, PA=4, ZI=7, SI7=7, HI7=7)
+    sb("uint16", OU=76, OD=26, OFFG=8, OFFL=14)
+    for n, w in dict(IP0=32, IP1=32, IP2=32, SP=160, SPT=160).items():
         d[n] = ("sbuf", [128, 7, w], f)
     d["PS"] = ("psum", [128, 4096], f)
     return d
@@ -76,6 +76,9 @@ def rank_program(g, core, T, topo):
     def H(name, c0=0, c1=None):
         return C(name, c0, c1, 0, 64)
 
+    def U(name, c0=0, c1=None):
+        return C(name, c0, c1, 64, 128)
+
     def B3(name, c0, c1, p0=0, p1=128):
         return (T[name][p0:p1, :, c0:c1], name, p0, p1, 0, 7 * SCRATCH[name][1][2])
 
@@ -83,8 +86,8 @@ def rank_program(g, core, T, topo):
         w = SCRATCH[name][1][2]
         return (T[name][:, b, :], name, 0, 128, b * w, b * w + w)
 
-    def bank(k, n, p0=0, p1=128):
-        return (T.PS[p0:p1, 512 * k:512 * k + n], "PS", 0, 128, 512 * k, 512 * k + 512)
+    def bank(k, n, p0=0, p1=128, c0=0):
+        return (T.PS[p0:p1, 512 * k + c0:512 * k + n], "PS", 0, 128, 512 * k, 512 * k + 512)
 
     def ext(ap):
         return (ap, None, 0, 0, 0, 0)
@@ -167,8 +170,11 @@ def rank_program(g, core, T, topo):
         else:
             run("s", lambda: g.scalar.activation(junk[0], i[0], ACT.Copy, accum_out=o[0]), [i], [o, junk])
 
-    def minus(o, i, col):
-        run("s", lambda: g.scalar.activation(o[0], i[0], ACT.Identity, bias=col[0], scale=-1.0), [i, col], [o])
+    def affine(o, i, bias, scale, func=ACT.Identity):
+        rd = [i] + [x for x in (bias, scale) if isinstance(x, tuple)]
+        b = bias[0] if isinstance(bias, tuple) else bias
+        a = scale[0] if isinstance(scale, tuple) else scale
+        run("s", lambda: g.scalar.activation(o[0], i[0], func, bias=b, scale=a), rd, [o])
 
     def gather(q, o, win, off):
         src = win[0].indirect(off[0])
@@ -182,7 +188,13 @@ def rank_program(g, core, T, topo):
         a, b, c, d = C(l, lc, lc + 128), C(l + "S", lc, lc + 128), C(x, x0, x1), C(x + "S", x0, x1)
         run("t", lambda: g.tensor.matmul_mx(o[0], a[0], b[0], c[0], d[0], True, True), [a, b, c, d], [o])
 
+    part = [False]
+
     def iota(o, pattern, base, cm, whole=False):
+        now = o[3] - o[2] < 128
+        if now or part[0]:
+            need("g", "cg", cnt["cg"], {})
+        part[0] = now
         run("g", (lambda: g.iota(o[0], pattern, base, cm)) if whole else
             (lambda: g.iota(o[0], pattern, base, cm, allow_small_or_imprecise_dtypes=True)), [], [o])
 
@@ -191,10 +203,10 @@ def rank_program(g, core, T, topo):
         run("v", lambda: g.vector.tensor_copy(a[0].bitcast(dt.uint32), w[0].bitcast(dt.uint32).indirect(off[0])), [w, off], [a])
         gather("s", C(o + "S"), C(src + "S", 0, c1), off)
 
-    def cross(o, w, i, pat):
+    def cross(o, w, i):
         for b in range(4):
             for q in range(4):
-                copy(pat[(4 * b + q) % len(pat)], C(o, w * b, w * b + w, 32 * q, 32 * q + 32), C(i, 0, w, 32 * b, 32 * b + 32))
+                copy("vs"[q % 2], C(o, w * b, w * b + w, 32 * q, 32 * q + 32), C(i, 0, w, 32 * b, 32 * b + 32))
 
     def quadsum(o, h, i, n):
         for a in (0, 64):
@@ -247,27 +259,44 @@ def rank_program(g, core, T, topo):
         total[sem] = val
 
     dma("s", C("U4"), ext(T.u[:, 0:4]))
-    dma("y", C("XB"), ext(T.x[:, :]))
-    dma("s", C("AB"), ext(T.a[:, :]))
-    dma("y", C("BB"), ext(T.b[:, :]))
-    dma("y", C("WB"), ext(T.w[:, :]))
+    for name, t in (("XB", T.x), ("AB", T.a), ("BB", T.b), ("WB", T.w)):
+        dma("y", C(name), ext(t[:, :]))
 
-    memset(C("Z0"), 0.0)
-    memset(C("OC", 1, 2, 0, 64), -9e29)
-    memset((T.SP[64:128, :, 96:192], "SP", 64, 128, 0, 7 * 192), 0.0)
-    memset(C("AL"), 0.0)
-    memset(C("FF"), 0.0)
-    for k, v in enumerate((Wn, Wn + UNIT - MK, -(2 * Wn + UNIT))):
-        memset(C("BE2", k, k + 1), float(v))
     iota(C("PIN"), [[0, 1]], 0, 1, True)
     iota(C("PID"), [[0, 1]], 0, 1)
-    iota(C("OI", 0, 28), [[1, 14], [0, 2]], 0, 0, True)
-    iota(C("RK"), [[64, 6]], 2 * P * r, 0)
-    iota(C("RM"), [[1, 32]], 0, 0)
+    iota(C("OI", 0, 14), [[1, 7], [0, 2]], 0, 0, True)
+    iota(C("OI", 14, 16), [[0, 2]], 0, 0, True)
     iota(C("TI0"), [[-32, 6], [64, 2], [1, 32]], 0, 0)
-    for k, m in enumerate((31, 15, 32)):
+    iota(C("RM"), [[1, 32]], 0, 0)
+    iota(C("RK"), [[64, 6]], 2 * P * r, 0)
+    at, nb, na, last = 18, r, N - 1 - r, []
+    for what, s0, n in (("main", 0, nb), ("rest", 0, nb), ("rest", nb, na), ("main", nb, na)):
+        if what == "main" and n:
+            iota(C("OI", at, at + 2 * n), [[3, n], [0, 2]], 3 * s0, 0, True)
+            at += 2 * n
+        elif n:
+            last.append((at, s0, n))
+            at += 2 * ((n + 1) // 2)
+    iota(H("OI", 16, 18), [[0, 2]], 2, 0, True)
+    iota(U("OI", 16, 18), [[0, 2]], 1, 0, True)
+    for at, s0, n in last:
+        m = (n + 1) // 2
+        iota(H("OI", at, at + 2 * m), [[6, m], [0, 2]], 3 * s0 + 1, 0, True)
+        if n // 2:
+            iota(U("OI", at, at + 2 * (n // 2)), [[6, n // 2], [0, 2]], 3 * s0 + 4, 0, True)
+        if n % 2:
+            iota(U("OI", at + n - 1, at + n + 1), [[0, 2]], 2, 0, True)
+    cut = 32 * (nb + (nb + 1) // 2)
+    memset(C("Z0"), 0.0)
+    memset(C("OC", 2, 3), -9e29)
+    memset(H("BEA"), float(Wn))
+    memset(U("BEA"), float(Wn + UNIT - MK))
+    memset(C("BEB"), -float(2 * Wn + UNIT))
+    memset(C("AL"), 0.0)
+    for k, m in enumerate((31, 15, 32, 63)):
         ts(C("PA", k, k + 1), C("PIN"), m, ALU.bitwise_and)
-        copy("v", C(("IC", "PM16", "QO")[k]), C("PA", k, k + 1))
+    for k, n in enumerate(("IC", "PM16", "QO", "P63")):
+        copy("v", C(n), C("PA", k, k + 1))
     ts(C("ISC"), C("PID"), 64.0, ALU.is_ge)
     ts(C("I2"), C("IC"), 2.0, ALU.mult)
     ts(C("CK"), C("I2"), C("ISC"), ALU.add)
@@ -280,9 +309,10 @@ def rank_program(g, core, T, topo):
     mm(bank(1, 128), "W1", hL, "UQ", 0, 128)
     mm(bank(2, 128), "W1", hL + 64, "UQ", 0, 128)
     mm(bank(0, P), "UQ", 0, "W1", hL, hL + P)
-    copy("v", C("OC", 0, 1), bank(1, 1))
-    copy("v", C("OC", 1, 2, 64, 128), bank(2, 1, 64, 128))
-    fan(C("OC"), "land1", 2, "ar1")
+    copy("s", C("OC", 0, 1), bank(1, 1))
+    copy("v", U("OC", 1, 2), bank(2, 1, 64, 128))
+    copy("v", H("OC", 1, 2), bank(2, 1, 64, 128))
+    fan(C("OC"), "land1", 3, "ar1")
     arrive("ar1", 8 * 7, [C("land1")])
     if r + 1 < N:
         halo(r + 1, P - _halo(r + 1)[0], P, 0)
@@ -290,86 +320,92 @@ def rank_program(g, core, T, topo):
         halo(r - 1, 0, _halo(r - 1)[1], _halo(r - 1)[0] + P)
     want = sum(2 * len(topo.engines(T.cores[d], core)) for d in (r - 1, r + 1) if 0 <= d < N)
     arrive("arh", want, [C(n, a, b) for n in ("W1", "W1S") for a, b in ((0, hL), (hL + P, Wn)) if b > a])
-    iota(C("OI", 28, 36), [[3, 4], [0, 2]], 0, 0, True)
-    iota(C("OI", 36, 40), [[3, 2], [0, 2]], 2, 0, True)
-    iota(C("OI", 40, 48), [[3, 4], [0, 2]], 1, 0, True)
-    iota(C("OI", 48, 52), [[3, 2], [0, 2]], 8, 0, True)
-    iota(C("OI", 52, 60), [[2, 4], [0, 2]], 0, 0, True)
-    iota(C("OI", 60, 64), [[2, 2], [0, 2]], 1, 0, True)
-    iota(C("OI", 64, 90), [[16, 13], [0, 2]], 0, 0, True)
-    iota(C("RB"), [[32, 7]], E * r, 0)
-    iota(C("ON3"), [[1, 3]], -1, 0)
-    iota(C("KK3"), [[1, 3]], 0, 0)
-    iota((T.IP[:, :, :], "IP", 0, 128, 0, 224), [[32, 7], [1, 32]], E * r, 0)
+    for c0, c1, st, base in ((40, 48, 3, 0), (48, 52, 3, 2), (52, 60, 3, 1), (60, 64, 3, 8), (64, 72, 2, 0), (72, 76, 2, 1), (76, 102, 16, 0)):
+        iota(C("OI", c0, c1), [[st, (c1 - c0) // 2], [0, 2]], base, 0, True)
+    for k in range(3):
+        n = "IP%d" % k
+        iota((T[n][:, :, :], n, 0, 128, 0, 224), [[32, 7], [1, 32]], E * r - k, 0)
 
-    copy("s", C("SR"), bank(0, P))
-    copy("v", C("OU", 0, 28), C("OI", 0, 28))
-    gather("v", C("OCB"), C("OC"), C("OU", 0, 4))
+    copy("v", C("OU", 0, 40), C("OI", 0, 40))
+    tr(C("ST0"), bank(0, P))
+    gather("s", C("OCB"), C("OC"), C("OU", 14, 18))
     ts(C("TIE"), C("TI0"), C("NT"), ALU.is_lt, -TAU, ALU.mult)
     tr(C("TOWN"), C("OCB"))
-    tr(C("ST0"), C("SR"))
     for k in range(6):
         ts(C("DL", 64 * k, 64 * k + 64), C("TOWN"), C("ST0", 32 * k, 32 * k + 1), ALU.subtract)
     tt(C("CL"), C("DL"), C("TIE"), ALU.is_gt)
 
     quant("AQ", 0, 512, C("AB"))
-    kids_pat = "ssssssss"
     quant("BQ", 0, 512, C("BB"))
-    kids("W1", hL, P, "KH1", "KH2", 3, kids_pat)
+    kids("W1", hL, P, "KH1", "KH2", 3, "ssssssss")
     for k in range(6):
         total_of("v", C("PL", k, k + 1), C("CL", 64 * k, 64 * k + 64))
     ts(C("SLT"), C("RM"), C("QO"), ALU.add)
     ts(C("SLT2"), C("SLT"), 64.0, ALU.add)
     ts(C("KEYC"), C("RK"), C("CK"), ALU.add)
-    copy("v", C("V2C", 0, 6, 0, 64), C("ST0", 0, 192, 0, 64, 32))
-    ts(C("V2C", 0, 6, 64, 128), C("RK", 0, 6, 64, 128), C("I2", 0, 1, 64, 128), ALU.add)
+    ts(C("KEYN"), C("KEYC"), -1.0, ALU.mult)
+    copy("v", H("V2C"), C("ST0", 0, 192, 0, 64, 32))
+    ts(U("V2C"), U("RK"), U("I2"), ALU.add)
+    ts(C("TH"), C("P63"), -1.0, ALU.mult, 64.0, ALU.add)
 
-    gather("v", C("LB"), C("land1"), C("OU", 0, 28))
-    tr(C("LT"), C("LB"))
+    gather("s", C("LB", 192, 352), C("land1"), C("OU", 30, 40))
+    gather("v", C("LB", 0, 192), C("land1"), C("OU", 18, 30))
+    tr(C("LT", 0, 192), C("LB", 0, 192))
+    tr(C("LT", 192, 352), C("LB", 192, 352))
 
     def against(ks):
         for k in ks:
             sc = C("ST0", 32 * k, 32 * k + 1)
-            if r > 0:
-                ts(C("CM", 448 * k, 448 * k + 64 * r), C("LT", 0, 64 * r), sc, ALU.is_ge)
-            if r < N - 1:
-                ts(C("CM", 448 * k + 64 * r, 448 * k + 448), C("LT", 64 * r, 448), sc, ALU.is_gt)
-            total_of("s", C("PR", k, k + 1), C("CM", 448 * k, 448 * k + 448), C("J1"))
+            if cut > 0:
+                ts(C("CM", 352 * k, 352 * k + cut), C("LT", 0, cut), sc, ALU.is_ge)
+            if cut < 352:
+                ts(C("CM", 352 * k + cut, 352 * k + 352), C("LT", cut, 352), sc, ALU.is_gt)
+            total_of("s", C("PR", k, k + 1), C("CM", 352 * k, 352 * k + 352), C("J1"))
     against((0, 1, 2))
     quant("KO1", 0, P, C("KH1"))
     quant("KO2", 0, P, C("KH2"))
     mm(bank(3, P), "UQ", 0, "KO1", 0, P)
     mm(bank(4, P), "UQ", 0, "KO2", 0, P)
     against((3, 4, 5))
-    copy("v", C("VALR", p0=0, p1=64), bank(3, P, 0, 64))
-    copy("v", C("VALR", p0=64, p1=128), bank(4, P, 64, 128))
-    tr(C("VALT"), C("VALR"))
+    tr(H("VALT"), bank(3, P, 0, 64))
+    tr(U("VALT"), bank(4, P, 64, 128))
     tt(C("PT"), C("PR"), C("PL"), ALU.add)
     quadsum("PZ", "PB", "PT", 6)
-    for v in range(3):
+    for k in range(6):
+        affine(C("AD", 32 * k, 32 * k + 32), C("SLT"), C("PZ", k, k + 1), -1.0, ACT.Abs)
+    for k in range(6):
+        affine(C("EV", 32 * k, 32 * k + 32), C("AD", 32 * k, 32 * k + 32), C("KEYC", k, k + 1), C("KEYN", k, k + 1), ACT.Relu)
+    for v in (1, 2):
         for k in range(6):
-            val = (C("KEYC", k, k + 1), C("V2C", k, k + 1), C("VALT", 32 * k, 32 * k + 1))[v]
+            val = C("V2C", k, k + 1) if v == 1 else C("VALT", 32 * k, 32 * k + 1)
             ts(C("EV", 192 * v + 32 * k, 192 * v + 32 * k + 32), C("SLT2" if v == 1 else "SLT"), C("PZ", k, k + 1), ALU.is_equal, val, ALU.mult)
         tr(C("ET", 192 * v, 192 * v + 192), C("EV", 192 * v, 192 * v + 192))
-        c = (1, 2, 0)[v]
-        total_of("ssv"[v], C("V3", c, c + 1), C("ET", 192 * v, 192 * v + 192), C("J3"))
+        if v == 1:
+            total_of("s", C("V3", 2, 3), C("ET", 192, 384), C("J3", 0, 192))
+    tr(C("ET", 0, 192), C("EV", 0, 192))
+    total_of("s", C("V3", 1, 2), C("ET", 0, 192), C("J3", 0, 192))
+    total_of("v", C("V3", 0, 1), C("ET", 384, 576))
     fan(C("V3"), "land2", 3, "ar2")
     arrive("ar2", 8 * 7, [C("land2")])
 
-    copy("v", C("OU", 28, 64), C("OI", 28, 64))
-    ts(C("OJ"), C("OI", 64, 90), C("PM16"), ALU.add)
+    copy("v", C("OU", 40, 76), C("OI", 40, 76))
+    ts(C("OJ"), C("OI", 76, 102), C("PM16"), ALU.add)
     copy("v", C("OD"), C("OJ"))
-    ts(C("B0"), C("RB"), C("IC"), ALU.add, float(MK), ALU.mult)
-    ts(C("B7"), C("B0"), float(-ws), ALU.add)
     c1, cc = float(Wn), float(Wn + 2 * UNIT)
     ts(C("AL", 0, 1), C("ISC"), cc - MK, ALU.mult, c1, ALU.add)
     ts(C("AL", 1, 2), C("ISC"), -cc, ALU.mult, -c1, ALU.add)
     ts(C("C1"), C("ISC"), 2.0 * UNIT - cc, ALU.mult, G1 + ws - c1, ALU.add)
-    ts(C("BC", 0, 1), C("C1"), C("PID"), ALU.add)
-    ts(C("BC", 1, 2), C("ISC"), cc, ALU.mult, c1 + G2 - G1 + UNIT - MK, ALU.add)
     ts(C("C2"), C("ISC"), -2.0 * UNIT, ALU.mult, float(-(G2 + ws + UNIT)), ALU.add)
+    ts(C("BT", 1, 2), C("ISC"), cc, ALU.mult, c1 + G2 - G1 + UNIT - MK, ALU.add)
+    ts(C("E64"), C("PID"), 64.0, ALU.is_equal)
+    ts(C("HIS"), C("ISC"), 0.5, ALU.mult)
+    ts(C("NIS"), C("ISC"), -0.5, ALU.mult)
+    ts(C("BC", 0, 1), C("C1"), C("PID"), ALU.add)
     ts(C("BC", 2, 3), C("C2"), C("PID"), ALU.subtract)
+    ub = B3("SP", 128, 160, 64, 128)
+    ts(ub, (T.IP0[64:128, :, :], "IP0", 64, 128, 0, 224), float(MK), ALU.mult, float(-ws), ALU.add)
     kids("W1", 0, Wn, "FH1", "FH2", 5, "svsvsvsv")
+    ts(ub, ub, U("E64"), ALU.mult)
     quant("W1", Wn, 2 * Wn, C("FH1", 0, 4 * Wn))
     quant("W1", 2 * Wn, 3 * Wn, C("FH2", 0, 4 * Wn))
     dma("y", C("W2", 0, 3 * Wn), C("W1", 0, 3 * Wn), bits=3)
@@ -379,84 +415,86 @@ def rank_program(g, core, T, topo):
     for k in range(3):
         total_of("v", C("RED", k, k + 1), C("land2", k, 21, step=3))
     tt(C("VV"), C("RED"), C("V3"), ALU.add)
-    cross("CC", 3, "VV", "vs")
-    copy("v", C("K2", 0, 1, 0, 64), C("VV", 2, 3, 64, 128))
-    gather("v", C("CB"), C("CC"), C("OU", 28, 52))
-    tr(C("RR"), C("CB"))
-    minus(C("E1"), C("RR", 0, 192), C("VV", 0, 1))
-    minus(H("E2"), H("RR", 0, 128), H("VV", 2, 3))
+    cross("CC", 3, "VV")
+    gather("s", C("CB", 192, 384), C("CC"), C("OU", 52, 64))
+    gather("v", C("CB", 0, 192), C("CC"), C("OU", 40, 52))
+    copy("s", H("NC"), U("VV", 2, 3))
+    copy("s", U("NC"), U("VV", 2, 3))
+    copy("s", U("NS"), H("VV", 2, 3))
+    copy("s", H("NS"), H("VV", 2, 3))
+    tr(C("RR", 0, 192), C("CB", 0, 192))
+    tr(C("RR", 192, 384), C("CB", 192, 384))
+    affine(C("E1"), C("RR", 0, 192), C("VV", 0, 1), -1.0)
+    affine(C("E2"), C("RR", 0, 128), C("NS"), -1.0)
     ts(C("NK1"), C("RR", 192, 384), C("VV", 1, 2), ALU.subtract, -TAU, ALU.mult)
-    ts(H("NK2"), H("RR", 192, 320), H("K2"), ALU.subtract, -TAU, ALU.mult)
+    ts(C("NK2"), C("RR", 192, 320), C("NC"), ALU.subtract, -TAU, ALU.mult)
     tt(C("M1"), C("E1"), C("NK1"), ALU.is_lt)
-    tt(H("M2"), H("E2"), H("NK2"), ALU.is_lt)
-    total_of("v", C("R1"), C("M1"))
-    total_of("v", H("R2"), H("M2"))
-    ts(C("FF", 0, 1), C("R1"), 64.0, ALU.is_lt, C("ISC"), ALU.add)
-    ts(H("FF", 1, 2), H("R2"), H("PID"), ALU.add, 64.0, ALU.is_lt)
-    cross("FC", 2, "FF", "vs")
-    ts(C("L1"), C("RR", 192, 384), C("VV", 1, 2), ALU.is_lt)
-    gather("v", C("FB"), C("FC"), C("OU", 52, 64))
-    tr(C("FR"), C("FB"))
-    ts(H("L2"), H("RR", 192, 384), H("K2"), ALU.is_lt)
-    tt(C("Q1"), C("L1"), C("FR"), ALU.mult)
-    total_of("s", C("S1"), C("Q1"), C("J3"))
-    tt(H("Q2"), H("L2"), H("FR"), ALU.mult)
-    total_of("s", H("S2"), H("Q2"), H("J4"))
-
-    gather("v", C("GD"), C("RR", 192, 256), C("OD", 0, 8))
+    affine(C("KB"), C("VV", 1, 2), -BIG, 1.0)
+    affine(C("NB"), C("NC"), -BIG, 1.0)
+    affine(C("FR", 192, 256), C("RR", 256, 320), -BIG, 1.0)
+    total_of("s", C("R1"), C("M1"), C("J3", 0, 192))
+    tt(C("M2"), C("E2"), C("NK2"), ALU.is_lt)
+    gather("s", C("GD"), C("RR", 192, 256), C("OD", 0, 8))
+    total_of("v", C("R2"), C("M2"))
+    ts(C("FF", 0, 1), C("R1"), 64.0, ALU.is_lt, C("KB"), ALU.mult)
+    ts(C("FF", 1, 2), C("R2"), C("TH"), ALU.is_lt, C("NB"), ALU.mult)
+    cross("FC", 2, "FF")
+    gather("s", C("FB", 96, 192), C("FC"), C("OU", 70, 76))
+    gather("v", C("FB", 0, 96), C("FC"), C("OU", 64, 70))
+    affine(C("Q1", 256, 257), C("VV", 1, 2), C("HIS"), 0.5)
     tr(C("GT"), C("GD"))
-    ts(C("GV"), C("GT", 0, 128, step=32), 0.5, ALU.mult, float(-ws), ALU.add)
-    ts(C("GT4"), C("GV"), 0.0, ALU.max, float(Wn - 1), ALU.min)
-    ts(C("OFFG", 0, 4), C("GT4"), float(Wn), ALU.add)
-    ts(C("OFFG", 4, 8), C("GT4"), float(2 * Wn), ALU.add)
+    tr(C("FR", 0, 192), C("FB"))
+    affine(C("Q2", 256, 257), C("NC"), C("ISC"), 0.5)
+    affine(C("GV"), C("GT", 0, 128, step=32), float(-ws), 0.5, ACT.Relu)
+    affine(C("GT4"), C("GV"), float(Wn - 1), -1.0, ACT.Relu)
+    ts(C("Q1", 0, 256), C("FR"), C("KB"), ALU.is_lt)
+    total_of("s", C("S1"), C("Q1"), C("J3"))
+    ts(C("Q2", 0, 256), C("FR"), C("NB"), ALU.is_lt)
+    ts(C("OFFG", 0, 4), C("GT4"), -1.0, ALU.mult, float(2 * Wn - 1), ALU.add)
+    ts(C("OFFG", 4, 8), C("GT4"), -1.0, ALU.mult, float(3 * Wn - 1), ALU.add)
+    affine(C("OO"), C("VV", 1, 2), C("NIS"), 0.5)
+    affine(C("FL"), C("FF", 0, 1), 0.0, -1.0, ACT.Sign)
+    affine(C("F2"), C("FF", 1, 2), 0.0, -1.0, ACT.Sign)
+    affine(C("BT", 0, 1), C("OO"), C("BC", 0, 1), -1.0)
+    affine(C("BT", 2, 3), C("OO"), C("BC", 2, 3), 1.0)
+    for k in range(3):
+        affine(C("WT1", k, k + 1), C("FL"), C("AL", k, k + 1), C("BT", k, k + 1))
+    affine(C("WTA"), C("F2"), 0.0, C("BEA"))
+    affine(C("WTB"), C("F2"), 0.0, C("BEB"))
+    total_of("v", C("S2"), C("Q2"))
     pick("PK", "W1", 3 * Wn, C("OFFG"))
-
-    ts(C("FL"), C("R1"), 64.0, ALU.is_lt)
-    ts(C("OO"), C("VV", 1, 2), C("ISC"), ALU.subtract, 0.5, ALU.mult)
-    ts(C("BE"), C("ON3"), C("OO"), ALU.mult)
-    tt(C("BT"), C("BE"), C("BC"), ALU.add)
-    ts(C("BF"), C("BT"), C("FL"), ALU.mult)
-    tt(C("WT1"), C("BF"), C("AL"), ALU.add)
-    ts(H("WT2"), H("BE2"), H("FF", 1, 2), ALU.mult)
-    ts(C("OPC"), C("KK3"), C("OO"), ALU.add, C("ISC"), ALU.add)
-    ts(H("H2"), H("K2"), 0.5, ALU.mult)
-    ts(H("NPC"), H("KK3"), H("H2"), ALU.add)
-    ts(C("PK1"), C("OPC"), C("S1"), ALU.add)
-    ts(H("PK2"), H("NPC"), H("S2"), ALU.add)
     kids("PK", 0, 128, "GH1", "GH2", 5, "ssssssss")
 
     for k in range(3):
-        ts(B3("SP", 32 * k, 32 * k + 32), (T.IP[:, :, :], "IP", 0, 128, 0, 224), C("PK1", k, k + 1), ALU.is_ge, C("WT1", k, k + 1), ALU.mult)
-        ts(B3("SP", 96 + 32 * k, 128 + 32 * k, 0, 64), (T.IP[0:64, :, :], "IP", 0, 64, 0, 224), H("PK2", k, k + 1), ALU.is_ge, H("WT2", k, k + 1), ALU.mult)
+        ts(B3("SP", 32 * k, 32 * k + 32), B3("IP%d" % k, 0, 32), C("S1"), ALU.is_ge, C("WT1", k, k + 1), ALU.mult)
+    ts(B3("SP", 96, 128), B3("IP0", 0, 32), C("S2"), ALU.is_ge, C("WTA"), ALU.mult)
+    ts(B3("SP", 128, 160, 0, 64), B3("IP2", 0, 32, 0, 64), H("S2"), ALU.is_ge, H("WTB"), ALU.mult)
     for b in range(7):
         tr(B1("SPT", b), B1("SP", b))
-        total_of("svsvsvv"[b], C("ZS", b, b + 1), B1("SPT", b), C("J3"))
-    quant("W2", G1, G1 + 128, C("GH1"))
-    quant("W2", G2, G2 + 128, C("GH2"))
-    quadsum("Z7B", "Z7", "ZS", 7)
-    tt(C("Z7C"), C("Z7B"), C("B7"), ALU.add)
-    copy("v", C("ZI"), C("Z7C"))
+        total_of("svsvssv"[b], C("ZS", b, b + 1), B1("SPT", b), C("J3", 0, 160))
+    quadsum("ZI", "Z7", "ZS", 7)
     ts(C("SI7"), C("ZI"), UNIT - 1, ALU.bitwise_and)
-    copy("v", C("SRC7"), C("SI7"))
-    gather("v", C("SB7"), C("SRC7"), C("OU", 0, 14))
+    ts(C("HI7"), C("ZI"), 11, ALU.logical_shift_right)
+    gather("v", C("SB7"), C("SI7"), C("OU", 0, 14))
+    copy("v", C("HS7"), C("HI7"))
     tr(C("SROW"), C("SB7"))
-    gather("v", C("SD", 0, 208), C("SROW"), C("OD", 0, 13))
-    gather("s", C("SD", 208, 416), C("SROW"), C("OD", 13, 26)) if False else gather("v", C("SD", 208, 416), C("SROW"), C("OD", 13, 26)) if False else None
-    gather("v", C("SD", 192, 416), C("SROW"), C("OD", 12, 26))
+    quant("W2", G1, G1 + 128, C("GH1"))
+    gather("s", C("SD", 192, 416), C("SROW"), C("OD", 12, 26))
+    gather("v", C("SD", 0, 192), C("SROW"), C("OD", 0, 12))
+    gather("s", C("HB7"), C("HS7"), C("OU", 0, 14))
+    quant("W2", G2, G2 + 128, C("GH2"))
     tr(C("STT"), C("SD"))
     copy("v", C("OFFL", 0, 13), C("STT", 0, 416, step=32))
     pick("FQ", "W2", 3 * Wn + 256, C("OFFL", 0, 13))
     mm(bank(0, E), "WQ", 0, "FQ", 0, E)
-    dma("y", ext(T.oc[:, :]), C("FQ"), bits=2)
-    for k in range(4):
-        dma("ys"[k % 2], ext(T.osc[4 * k:4 * k + 4, :]), C("FQS", 0, E, 32 * k, 32 * k + 4))
-    copy("v", C("YS"), bank(0, E))
-    dma("y", ext(T.y[:, :]), C("YS"))
-    ts(C("HI7"), C("ZI"), 11, ALU.logical_shift_right)
-    copy("v", C("HS7"), C("HI7"))
-    gather("v", C("HB7"), C("HS7"), C("OU", 0, 14))
     tr(C("HROW"), C("HB7"))
-    dma("s", ext(T.hs[:, :]), C("HROW", 0, E, 0, 1))
+    dma("y", ext(T.oc[:, :]), C("FQ"), bits=2)
+    copy("s", C("YS", 0, 104), bank(0, 104))
+    copy("v", C("YS", 104, E), bank(0, E, c0=104))
+    dma("s", ext(T.y[:, :]), C("YS"))
+    dma("y", ext(T.hs[:, :]), C("HROW", 0, E, 0, 1))
+    for k in range(4):
+        dma("ysys"[k], ext(T.osc[4 * k:4 * k + 4, :]), C("FQS", 0, E, 32 * k, 32 * k + 4))
 
     total["loc"] = loc[0]
     for sem in SEMAPHORES:

@@ -7,13 +7,14 @@ N, P, K, E = 8, 192, 64, 208
 WMAX = 336
 TAU = 1e-32
 BIG = 65536.0
-UNIT = 2048
-MK = 4 * UNIT + 1
+DUMP = 1720
+ROW = 8 + 4 * DUMP
 
 SMALL = {}
-for _n, _w in dict(PL=6, PR=6, PT=6, PB=6, PZ=6, RK=6, KEYC=6, KEYN=6, V2C=6, RED=3, VV=3, NS=1, NC=1, CC=12, R1=1, R2=1, FF=2, FL=1, F2=1, FC=8,
-                   S1=1, S2=1, OO=1, AL=3, BC=3, BT=3, BEA=1, BEB=1, WTA=1, WTB=1, WT1=3, PID=1, KB=1, NB=1, TH=1, HIS=1, NIS=1,
-                   IC=1, PM16=1, QO=1, P63=1, ISC=1, E64=1, CK=1, I2=1, NT=1, C1=1, C2=1, ZS=7, Z7=7, HS7=7, GV=4, GT4=4).items():
+for _n, _w in dict(NST=6, PL=6, PR=6, PT=6, PB=6, PZ=6, RK=6, KEYC=6, KEYN=6, V2C=6, VV=4, R1=1, R2=1, FF=2, FL=1, F2=1, TH=1, KB=1, NB=1,
+                   PID=1, BITS=4, SG=1, ISC=1, CK=1, I2=1, NT=1, KE=3, DB=3, DBN=1, NKE=1, CN=1, BN=1, EB=1, S1=1, C2=1, A12=1,
+                   SB1=1, SGN=1, AN=1, INI=1, CLA=1, CLB=1, BL1=1, BL2=1, GRP=1, GR=1, ZS=8, HS=8, GV=4, GT4=4, GO=8, JJ=8,
+                   JK=8).items():
     SMALL[_n] = (8 * sum((w + 7) // 8 for _, w in SMALL.values()), _w)
 
 
@@ -24,29 +25,32 @@ def _scratch():
     def sb(dtype, **kw):
         for name, n in kw.items():
             d[name] = ("sbuf", [128, n], dtype)
-    sb(h, XB=4 * P, U4=4, UB=512, AB=2048, BB=2048, WB=512, KH1=4 * P, KH2=4 * P, FH1=4 * WMAX, FH2=4 * WMAX,
-       GH1=512, GH2=512, CL=384, CM=6 * 352, J1=352, M1=192, M2=128)
-    for name, n in dict(UQ=128, AQ=512, BQ=512, WQ=128, W1=3 * WMAX, KO1=P, KO2=P, PK=128, W2=3 * WMAX + 256, FQ=E).items():
+    sb(h, XB=4 * P, U4=4, UB=512, AB=2048, BB=2048, WB=512, KH1=4 * P, KH2=4 * P, FH1=576, FH2=576,
+       GH1=512, GH2=512, CL=384, CM=6 * 352, J1=352, M1=192, M2=160)
+    for name, n in dict(UQ=128, AQ=512, BQ=512, WQ=128, W1=3 * WMAX, HQ=144, HK1=144, HK2=144, PK=128, W2=4 * WMAX + 256, FQ=E).items():
         d[name] = ("sbuf", [128, n], q)
         d[name + "S"] = ("sbuf", [128, n], s)
-    sb(f, Z0=128, OC=3, OCB=64, TOWN=64, ST0=192, DL=384, TI0=384, TIE=384, land1=21, LB=352, LT=352, RM=32,
-       SLT=32, SLT2=32, VALT=192, AD=192, EV=576, ET=576, V3=3, land2=21, CB=384, RR=384, E1=192, E2=128, NK1=192,
-       NK2=128, FB=192, FR=256, Q1=257, Q2=257, SB7=224, SROW=224, SD=416, STT=416, HB7=224, HROW=224,
-       GD=128, GT=128, YS=E, J3=257, SM=8 * sum((w + 7) // 8 for _, w in SMALL.values()))
-    sb("int32", OI=102, OJ=26, PIN=1, PA=4, ZI=7, SI7=7, HI7=7)
-    sb("uint16", OU=76, OD=26, OFFG=8, OFFL=14)
-    for n, w in dict(IP0=32, IP1=32, IP2=32, SP=160, SPT=160).items():
-        d[n] = ("sbuf", [128, 7, w], f)
+    sb(f, Z0=128, OC=8, OCB=64, TOWN=64, ST0=192, DL=384, TI0=384, TIE=384, land1=24, LB=352, LT=352, RM=32,
+       SLT=32, SLT2=32, VALT=192, AD=192, EV=576, ET=576, land2=32, RBS=64, RBK=64, SC=192, KY=192, E1=192, E2=160, NK1=192,
+       NK2=160, FB=64, FR=256, Q1=256, Q2=256, VA=64, VB=64, CTI=32, CT=32, SEC=32, RA=ROW, RB=ROW, XS=256, XT=256, ZT=32, XR=32,
+       YY=64, YT=64, HT=4 * WMAX + 256, HR=E, GD=128, GT=128, YS=E, J3=256, OI2=22, SM=8 * sum((w + 7) // 8 for _, w in SMALL.values()))
+    sb("int32", OI=34, PIN=1, PA=4)
+    sb("uint16", OU=34, OD=20, OV=2, OFF=4, OFFG=8, OFFL=14)
     d["PS"] = ("psum", [128, 4096], f)
     return d
 
 
 SCRATCH = _scratch()
-SEMAPHORES = ["cv", "cs", "ct", "cg", "loc", "ar1", "ar2", "arh"] + ["d%d" % i for i in range(16)]
+SEMAPHORES = ["cv", "cs", "ct", "cg", "loc", "ar1", "ar2", "arh"] + ["d%d" % i for i in range(40)]
 
 
 def _halo(r):
     return (0 if r == 0 else 128 - 16 * r), (0 if r == N - 1 else 16 + 16 * r)
+
+
+def _land(r):
+    hL, hR = _halo(r)
+    return ("HQ", 0, hL) if hL and hR else ("W1", 0, hL + P)
 
 
 def rank_program(g, core, T, topo):
@@ -56,7 +60,8 @@ def rank_program(g, core, T, topo):
     hL, hR = _halo(r)
     Wn = hL + P + hR
     ws = P * r - hL
-    G1, G2 = 3 * Wn, 3 * Wn + 128
+    G1, G2, G3 = 3 * Wn, 3 * Wn + 128, 3 * Wn + 256
+    e0 = E * r + 8
     q_of = {"v": g.vector, "s": g.scalar, "t": g.tensor, "g": g, "y": g.sync}
     cnt = {"cv": 0, "cs": 0, "ct": 0, "cg": 0}
     known = {k: {} for k in q_of}
@@ -79,12 +84,12 @@ def rank_program(g, core, T, topo):
     def U(name, c0=0, c1=None):
         return C(name, c0, c1, 64, 128)
 
-    def B3(name, c0, c1, p0=0, p1=128):
-        return (T[name][p0:p1, :, c0:c1], name, p0, p1, 0, 7 * SCRATCH[name][1][2])
+    def Q(name, q, c0=0, c1=None):
+        return C(name, c0, c1, 32 * q, 32 * q + 32)
 
-    def B1(name, b):
-        w = SCRATCH[name][1][2]
-        return (T[name][:, b, :], name, 0, 128, b * w, b * w + w)
+    def part_of(name, i, n, step):
+        w = n // step
+        return (T[name][:, i:n:step], name, 0, 128, i * w, i * w + w)
 
     def bank(k, n, p0=0, p1=128, c0=0):
         return (T.PS[p0:p1, 512 * k + c0:512 * k + n], "PS", 0, 128, 512 * k, 512 * k + 512)
@@ -141,6 +146,11 @@ def rank_program(g, core, T, topo):
         q_of[q].dma_start(o, i).then_inc(T.sem[sem], 16)
         note(q, "dma", sem, 16, x, w)
 
+    def move(dst, d0, src, s0, n):
+        if n:
+            dma("y", C(dst, d0, d0 + n), C(src, s0, s0 + n), bits=3)
+            dma("y", C(dst + "S", d0, d0 + n), C(src + "S", s0, s0 + n))
+
     def memset(o, val):
         run("v", lambda: g.vector.memset(o[0], val), [], [o])
 
@@ -170,15 +180,21 @@ def rank_program(g, core, T, topo):
         else:
             run("s", lambda: g.scalar.activation(junk[0], i[0], ACT.Copy, accum_out=o[0]), [i], [o, junk])
 
-    def affine(o, i, bias, scale, func=ACT.Identity):
+    def affine(o, i, bias, scale, func=ACT.Identity, acc=None):
         rd = [i] + [x for x in (bias, scale) if isinstance(x, tuple)]
         b = bias[0] if isinstance(bias, tuple) else bias
         a = scale[0] if isinstance(scale, tuple) else scale
-        run("s", lambda: g.scalar.activation(o[0], i[0], func, bias=b, scale=a), rd, [o])
+        if acc is None:
+            run("s", lambda: g.scalar.activation(o[0], i[0], func, bias=b, scale=a), rd, [o])
+        else:
+            run("s", lambda: g.scalar.activation(o[0], i[0], func, bias=b, scale=a, accum_out=acc[0]), rd, [o, acc])
 
     def gather(q, o, win, off):
         src = win[0].indirect(off[0])
         run(q, (lambda: g.vector.tensor_copy(o[0], src)) if q == "v" else (lambda: g.scalar.activation(o[0], src, ACT.Copy)), [win, off], [o])
+
+    def scatter(win, off, i):
+        run("v", lambda: g.vector.tensor_copy(win[0].indirect(off[0]), i[0]), [i, off], [win])
 
     def quant(name, c0, c1, src):
         o, s = C(name, c0, c1), C(name + "S", c0, c1)
@@ -203,23 +219,25 @@ def rank_program(g, core, T, topo):
         run("v", lambda: g.vector.tensor_copy(a[0].bitcast(dt.uint32), w[0].bitcast(dt.uint32).indirect(off[0])), [w, off], [a])
         gather("s", C(o + "S"), C(src + "S", 0, c1), off)
 
-    def cross(o, w, i):
-        for b in range(4):
-            for q in range(4):
-                copy("vs"[q % 2], C(o, w * b, w * b + w, 32 * q, 32 * q + 32), C(i, 0, w, 32 * b, 32 * b + 32))
-
     def quadsum(o, h, i, n):
-        for a in (0, 64):
-            tt(C(h, 0, n, a, a + 64), C(i, 0, n, a, a + 64), C(i, 0, n, 64 - a, 128 - a), ALU.add)
+        tt(H(h, 0, n), H(i, 0, n), U(i, 0, n), ALU.add)
+        for q in (0, 1):
+            tt(Q(o, q, 0, n), Q(h, 0, 0, n), Q(h, 1, 0, n), ALU.add)
+        copy("v", U(o, 0, n), H(o, 0, n))
+
+    def swap(name):
+        copy("s", H(name, 64, 96), U(name, 32, 64))
+        copy("v", U(name, 64, 96), H(name, 32, 64))
+
+    def pairs(name, order):
         for q in range(4):
-            a, b = 32 * q, 32 * (q ^ 1)
-            tt(C(o, 0, n, a, a + 32), C(h, 0, n, a, a + 32), C(h, 0, n, b, b + 32), ALU.add)
+            copy(order[q], Q(name, q, 96, 192), Q(name, q ^ 1, 0, 96))
 
     def kids(src, c0, n, t1, t2, first, pat):
         for i in range(8):
             k = (first + i) % 8
             mm(bank(k, n), "AQ" if i < 4 else "BQ", 128 * (i % 4), src, c0, c0 + n)
-            scaled(pat[i], C(t1 if i < 4 else t2, i % 4, 4 * n, step=4), bank(k, n), 0.0625)
+            scaled(pat[i], part_of(t1 if i < 4 else t2, i % 4, 4 * n, 4), bank(k, n), 0.0625)
 
     def fan(src, dst, width, arr):
         deps("g", [src], [])
@@ -241,14 +259,16 @@ def rank_program(g, core, T, topo):
         g.remote_dma_fused([tf(far, fe), tf(near, ne)], local_sem=T.sem.loc)
         loc[0] += len(fe) + len(ne)
 
-    def halo(d, c0, c1, at):
+    def halo(d, c0, c1, behind):
         c = T.cores[d]
+        dst, a, b = _land(d)
+        at = b if behind else a
         rid, pid, _ = topo.addr(c)
-        for name in ("W1", "W1S"):
-            s = C(name, hL + c0, hL + c1)
+        for sfx in ("", "S"):
+            s = C("W1" + sfx, hL + c0, hL + c1)
             deps("g", [s], [])
-            o, i = T[name][:, at:at + c1 - c0], s[0]
-            if name == "W1":
+            o, i = T[dst + sfx][:, at:at + c1 - c0], s[0]
+            if not sfx:
                 o, i = o.bitcast(dt.uint8), i.bitcast(dt.uint8)
             g.remote_dma(o, i, T.sem.arh, T.sem.loc, pid, rid, topo.mask(core, c))
             loc[0] += len(topo.engines(core, c))
@@ -264,46 +284,39 @@ def rank_program(g, core, T, topo):
 
     iota(C("PIN"), [[0, 1]], 0, 1, True)
     iota(C("PID"), [[0, 1]], 0, 1)
-    iota(C("OI", 0, 14), [[1, 7], [0, 2]], 0, 0, True)
-    iota(C("OI", 14, 16), [[0, 2]], 0, 0, True)
-    iota(C("TI0"), [[-32, 6], [64, 2], [1, 32]], 0, 0)
-    iota(C("RM"), [[1, 32]], 0, 0)
-    iota(C("RK"), [[64, 6]], 2 * P * r, 0)
-    at, nb, na, last = 18, r, N - 1 - r, []
+    iota(C("OI", 0, 2), [[0, 2]], 0, 0, True)
+    iota(H("OI", 2, 4), [[0, 2]], 4, 0, True)
+    iota(U("OI", 2, 4), [[0, 2]], 1, 0, True)
+    at, nb, na = 4, r, N - 1 - r
     for what, s0, n in (("main", 0, nb), ("rest", 0, nb), ("rest", nb, na), ("main", nb, na)):
         if what == "main" and n:
-            iota(C("OI", at, at + 2 * n), [[3, n], [0, 2]], 3 * s0, 0, True)
+            iota(C("OI", at, at + 2 * n), [[2, n], [0, 2]], 2 * s0, 0, True)
             at += 2 * n
         elif n:
-            last.append((at, s0, n))
-            at += 2 * ((n + 1) // 2)
-    iota(H("OI", 16, 18), [[0, 2]], 2, 0, True)
-    iota(U("OI", 16, 18), [[0, 2]], 1, 0, True)
-    for at, s0, n in last:
-        m = (n + 1) // 2
-        iota(H("OI", at, at + 2 * m), [[6, m], [0, 2]], 3 * s0 + 1, 0, True)
-        if n // 2:
-            iota(U("OI", at, at + 2 * (n // 2)), [[6, n // 2], [0, 2]], 3 * s0 + 4, 0, True)
-        if n % 2:
-            iota(U("OI", at + n - 1, at + n + 1), [[0, 2]], 2, 0, True)
+            m = (n + 1) // 2
+            iota(H("OI", at, at + 2 * m), [[4, m], [0, 2]], 2 * s0 + 1, 0, True)
+            if n // 2:
+                iota(U("OI", at, at + 2 * (n // 2)), [[4, n // 2], [0, 2]], 2 * s0 + 3, 0, True)
+            if n % 2:
+                iota(U("OI", at + n - 1, at + n + 1), [[0, 2]], 16, 0, True)
+            at += 2 * m
+    iota(C("OI", 26, 34), [[1, 4], [0, 2]], 0, 0, True)
     cut = 32 * (nb + (nb + 1) // 2)
     memset(C("Z0"), 0.0)
-    memset(C("OC", 2, 3), -9e29)
-    memset(H("BEA"), float(Wn))
-    memset(U("BEA"), float(Wn + UNIT - MK))
-    memset(C("BEB"), -float(2 * Wn + UNIT))
-    memset(C("AL"), 0.0)
-    for k, m in enumerate((31, 15, 32, 63)):
+    memset(C("OC"), -9e29)
+    memset(C("land1", 16, 20), -9e29)
+    for k, m in enumerate((31, 15, 32, 112)):
         ts(C("PA", k, k + 1), C("PIN"), m, ALU.bitwise_and)
-    for k, n in enumerate(("IC", "PM16", "QO", "P63")):
-        copy("v", C(n), C("PA", k, k + 1))
-    ts(C("ISC"), C("PID"), 64.0, ALU.is_ge)
-    ts(C("I2"), C("IC"), 2.0, ALU.mult)
-    ts(C("CK"), C("I2"), C("ISC"), ALU.add)
-    ts(C("NT"), C("I2"), C("PID"), ALU.subtract)
+    copy("v", C("BITS"), C("PA"))
+    IC, PM16, QO, GR = [C("BITS", k, k + 1) for k in range(4)]
+    affine(C("SG"), C("PID"), -63.5, 1.0, ACT.Sign)
+    affine(C("I2"), IC, 0.0, 2.0)
+    affine(C("ISC"), C("SG"), 0.0, 1.0, ACT.Relu)
+    affine(C("NT"), C("PID"), C("I2"), -1.0)
+    affine(C("CK"), C("I2"), C("ISC"), 1.0)
 
     for t in range(4):
-        ts(C("UB", t, 512, step=4), C("Z0"), C("U4", t, t + 1), ALU.add)
+        ts(part_of("UB", t, 512, 4), C("Z0"), C("U4", t, t + 1), ALU.add)
     quant("UQ", 0, 128, C("UB"))
     quant("W1", hL, hL + P, C("XB"))
     mm(bank(1, 128), "W1", hL, "UQ", 0, 128)
@@ -312,46 +325,70 @@ def rank_program(g, core, T, topo):
     copy("s", C("OC", 0, 1), bank(1, 1))
     copy("v", U("OC", 1, 2), bank(2, 1, 64, 128))
     copy("v", H("OC", 1, 2), bank(2, 1, 64, 128))
-    fan(C("OC"), "land1", 3, "ar1")
-    arrive("ar1", 8 * 7, [C("land1")])
+    fan(C("OC", 0, 2), "land1", 2, "ar1")
+    arrive("ar1", 8 * 7, [C("land1", 0, 14)])
+    iota(C("TI0"), [[-32, 6], [64, 2], [1, 32]], 0, 0)
     if r + 1 < N:
-        halo(r + 1, P - _halo(r + 1)[0], P, 0)
+        halo(r + 1, P - _halo(r + 1)[0], P, False)
     if r > 0:
-        halo(r - 1, 0, _halo(r - 1)[1], _halo(r - 1)[0] + P)
+        halo(r - 1, 0, _halo(r - 1)[1], True)
     want = sum(2 * len(topo.engines(T.cores[d], core)) for d in (r - 1, r + 1) if 0 <= d < N)
-    arrive("arh", want, [C(n, a, b) for n in ("W1", "W1S") for a, b in ((0, hL), (hL + P, Wn)) if b > a])
-    for c0, c1, st, base in ((40, 48, 3, 0), (48, 52, 3, 2), (52, 60, 3, 1), (60, 64, 3, 8), (64, 72, 2, 0), (72, 76, 2, 1), (76, 102, 16, 0)):
-        iota(C("OI", c0, c1), [[st, (c1 - c0) // 2], [0, 2]], base, 0, True)
+    hq, hl, hr = _land(r)
+    arrive("arh", want, [C(hq + x, a, b) for x in ("", "S") for a, b in ((hl, hl + hL), (hr, hr + hR)) if b > a])
+    iota(C("RM"), [[1, 32]], 0, 0)
+    iota(C("RK"), [[64, 6]], 2 * P * r, 0)
+    iota(C("OI2", 0, 4), [[16, 2], [0, 2]], 0, 0)
+    for q in range(4):
+        st, sh = (96 if q % 2 == 0 else -96), (32 if q < 2 else -32)
+        iota(Q("OI2", q, 4, 12), [[st, 2], [16, 2], [0, 2]], 96 * (q % 2) + 32 + 32 * (q // 2), 0)
+        iota(Q("OI2", q, 12, 20), [[sh, 2], [st, 2], [16, 2]], 96 * (q % 2) + 32 + 32 * (q // 2), 0)
+    iota(C("OI2", 20, 22), [[0, 2]], 32, 0)
+    iota(C("CTI"), [[2 * (G2 - G1) - 2, 2], [2, 16]], 2 * (G1 + ws), 0)
+    iota(C("RA", e0 - 8, e0 + 232), [[0, 240]], 0, 0)
+    iota(C("RB", e0 - 8, e0 + 232), [[0, 240]], 0, 0)
+    iota(C("RA", e0 - 8, e0 + 232, 0, 16), [[0, 240]], -2, 0)
+    iota(C("INI"), [[0, 1]], 0, 0)
+    iota(C("INI", 0, 1, 0, 16), [[0, 1]], 320 - 2 * (E * r - ws - 1), 0)
+    for t, x in (("VA", 1), ("VB", 0)):
+        iota(H(t, 0, 32), [[0, 32]], -2 * Wn, 0)
+        iota(U(t, 0, 32), [[2 * G3 - 4 * Wn, 2], [0, 16]], -2 * G3 + 2 * x, 0)
+    iota(C("VA", 0, 32, 0, 16), [[0, 32]], -2 * Wn - 2, 0)
+    iota(H("SEC"), [[0, 32]], 0, 0)
+    iota(U("SEC"), [[0, 32]], 1, 0)
+    iota(C("ZT"), [[0, 32]], 0, 0)
     for k in range(3):
-        n = "IP%d" % k
-        iota((T[n][:, :, :], n, 0, 128, 0, 224), [[32, 7], [1, 32]], E * r - k, 0)
+        iota(C("HT", k * Wn, k * Wn + Wn), [[4, Wn]], 4 * ws + 2 * (k // 2), 0)
+    iota(C("HT", G3, G3 + Wn), [[4, Wn]], 4 * ws + 1, 0)
 
-    copy("v", C("OU", 0, 40), C("OI", 0, 40))
+    copy("v", C("OU"), C("OI"))
     tr(C("ST0"), bank(0, P))
-    gather("s", C("OCB"), C("OC"), C("OU", 14, 18))
+    gather("s", C("OCB"), C("OC"), C("OU", 0, 4))
     ts(C("TIE"), C("TI0"), C("NT"), ALU.is_lt, -TAU, ALU.mult)
     tr(C("TOWN"), C("OCB"))
+    copy("s", H("V2C"), C("ST0", 0, 192, 0, 64, 32))
     for k in range(6):
-        ts(C("DL", 64 * k, 64 * k + 64), C("TOWN"), C("ST0", 32 * k, 32 * k + 1), ALU.subtract)
+        if k % 2:
+            ts(C("DL", 64 * k, 64 * k + 64), C("TOWN"), C("ST0", 32 * k, 32 * k + 1), ALU.subtract)
+        else:
+            scaled("s", C("NST", k, k + 1), C("ST0", 32 * k, 32 * k + 1), -1.0)
+            affine(C("DL", 64 * k, 64 * k + 64), C("TOWN"), C("NST", k, k + 1), 1.0)
+    quant("AQ", 0, 512, C("AB"))
     tt(C("CL"), C("DL"), C("TIE"), ALU.is_gt)
 
-    quant("AQ", 0, 512, C("AB"))
-    quant("BQ", 0, 512, C("BB"))
-    kids("W1", hL, P, "KH1", "KH2", 3, "ssssssss")
+    gather("v", C("LB", 0, 192), C("land1", 0, 20), C("OU", 4, 16))
+    gather("s", C("LB", 192, 352), C("land1", 0, 20), C("OU", 16, 26))
+    affine(C("SLT"), C("RM"), QO, 1.0)
+    affine(C("KEYC"), C("RK"), C("CK"), 1.0)
+    affine(U("V2C"), U("RK"), U("I2"), 1.0)
+    affine(C("SLT2"), C("SLT"), 64.0, 1.0)
+    affine(C("KEYN"), C("KEYC"), 0.0, -1.0)
     for k in range(6):
-        total_of("v", C("PL", k, k + 1), C("CL", 64 * k, 64 * k + 64))
-    ts(C("SLT"), C("RM"), C("QO"), ALU.add)
-    ts(C("SLT2"), C("SLT"), 64.0, ALU.add)
-    ts(C("KEYC"), C("RK"), C("CK"), ALU.add)
-    ts(C("KEYN"), C("KEYC"), -1.0, ALU.mult)
-    copy("v", H("V2C"), C("ST0", 0, 192, 0, 64, 32))
-    ts(U("V2C"), U("RK"), U("I2"), ALU.add)
-    ts(C("TH"), C("P63"), -1.0, ALU.mult, 64.0, ALU.add)
-
-    gather("s", C("LB", 192, 352), C("land1"), C("OU", 30, 40))
-    gather("v", C("LB", 0, 192), C("land1"), C("OU", 18, 30))
+        total_of("s", C("PL", k, k + 1), C("CL", 64 * k, 64 * k + 64), C("J1", 0, 64))
     tr(C("LT", 0, 192), C("LB", 0, 192))
     tr(C("LT", 192, 352), C("LB", 192, 352))
+    quant("BQ", 0, 512, C("BB"))
+    ts(C("OD"), C("OI2", 0, 20), PM16, ALU.add)
+    ts(C("OV"), C("OI2", 20, 22), IC, ALU.add)
 
     def against(ks):
         for k in ks:
@@ -360,17 +397,28 @@ def rank_program(g, core, T, topo):
                 ts(C("CM", 352 * k, 352 * k + cut), C("LT", 0, cut), sc, ALU.is_ge)
             if cut < 352:
                 ts(C("CM", 352 * k + cut, 352 * k + 352), C("LT", cut, 352), sc, ALU.is_gt)
-            total_of("s", C("PR", k, k + 1), C("CM", 352 * k, 352 * k + 352), C("J1"))
+            total_of("v" if k == 5 else "s", C("PR", k, k + 1), C("CM", 352 * k, 352 * k + 352), C("J1"))
+    kids("W1", hL, P, "KH1", "KH2", 3, "ssssssss")
     against((0, 1, 2))
-    quant("KO1", 0, P, C("KH1"))
-    quant("KO2", 0, P, C("KH2"))
-    mm(bank(3, P), "UQ", 0, "KO1", 0, P)
-    mm(bank(4, P), "UQ", 0, "KO2", 0, P)
+    quant("W1", Wn + hL, Wn + hL + P, C("KH1"))
+    quant("W1", 2 * Wn + hL, 2 * Wn + hL + P, C("KH2"))
+    mm(bank(3, P), "UQ", 0, "W1", Wn + hL, Wn + hL + P)
+    mm(bank(4, P), "UQ", 0, "W1", 2 * Wn + hL, 2 * Wn + hL + P)
     against((3, 4, 5))
     tr(H("VALT"), bank(3, P, 0, 64))
     tr(U("VALT"), bank(4, P, 64, 128))
     tt(C("PT"), C("PR"), C("PL"), ALU.add)
     quadsum("PZ", "PB", "PT", 6)
+    affine(C("TH"), IC, 64.0, -1.0)
+    affine(C("CN"), C("ISC"), float(272 + 6 * DUMP), 2.0)
+    affine(C("GR"), GR, 0.0, 1.0, ACT.Sign)
+    affine(C("CLA"), PM16, C("PID"), -1.0)
+    affine(C("GRP"), C("GR"), 2.0, -2.0)
+    affine(C("CLA"), C("CLA"), C("GRP"), 2.0)
+    affine(C("CLB"), C("ISC"), C("CLA"), 1.0)
+    affine(C("CLA"), C("ISC"), C("CLA"), -1.0)
+    affine(C("BL1"), C("ISC"), C("GRP"), -2.0)
+    affine(C("BL2"), C("GRP"), -2.0, 1.0)
     for k in range(6):
         affine(C("AD", 32 * k, 32 * k + 32), C("SLT"), C("PZ", k, k + 1), -1.0, ACT.Abs)
     for k in range(6):
@@ -381,118 +429,122 @@ def rank_program(g, core, T, topo):
             ts(C("EV", 192 * v + 32 * k, 192 * v + 32 * k + 32), C("SLT2" if v == 1 else "SLT"), C("PZ", k, k + 1), ALU.is_equal, val, ALU.mult)
         tr(C("ET", 192 * v, 192 * v + 192), C("EV", 192 * v, 192 * v + 192))
         if v == 1:
-            total_of("s", C("V3", 2, 3), C("ET", 192, 384), C("J3", 0, 192))
+            total_of("s", H("land2", 28, 29), H("ET", 192, 384), H("J3", 0, 192))
+            total_of("s", U("land2", 30, 31), U("ET", 192, 384), U("J3", 0, 192))
+            copy("s", U("land2", 28, 29), H("land2", 28, 29))
+            copy("s", H("land2", 30, 31), U("land2", 30, 31))
     tr(C("ET", 0, 192), C("EV", 0, 192))
-    total_of("s", C("V3", 1, 2), C("ET", 0, 192), C("J3", 0, 192))
-    total_of("v", C("V3", 0, 1), C("ET", 384, 576))
-    fan(C("V3"), "land2", 3, "ar2")
-    arrive("ar2", 8 * 7, [C("land2")])
+    total_of("s", C("land2", 31, 32), C("ET", 0, 192), C("J3", 0, 192))
+    total_of("v", C("land2", 29, 30), C("ET", 384, 576))
+    fan(C("land2", 28, 32), "land2", 4, "ar2")
+    arrive("ar2", 8 * 7, [C("land2", 0, 28)])
 
-    copy("v", C("OU", 40, 76), C("OI", 40, 76))
-    ts(C("OJ"), C("OI", 76, 102), C("PM16"), ALU.add)
-    copy("v", C("OD"), C("OJ"))
-    c1, cc = float(Wn), float(Wn + 2 * UNIT)
-    ts(C("AL", 0, 1), C("ISC"), cc - MK, ALU.mult, c1, ALU.add)
-    ts(C("AL", 1, 2), C("ISC"), -cc, ALU.mult, -c1, ALU.add)
-    ts(C("C1"), C("ISC"), 2.0 * UNIT - cc, ALU.mult, G1 + ws - c1, ALU.add)
-    ts(C("C2"), C("ISC"), -2.0 * UNIT, ALU.mult, float(-(G2 + ws + UNIT)), ALU.add)
-    ts(C("BT", 1, 2), C("ISC"), cc, ALU.mult, c1 + G2 - G1 + UNIT - MK, ALU.add)
-    ts(C("E64"), C("PID"), 64.0, ALU.is_equal)
-    ts(C("HIS"), C("ISC"), 0.5, ALU.mult)
-    ts(C("NIS"), C("ISC"), -0.5, ALU.mult)
-    ts(C("BC", 0, 1), C("C1"), C("PID"), ALU.add)
-    ts(C("BC", 2, 3), C("C2"), C("PID"), ALU.subtract)
-    ub = B3("SP", 128, 160, 64, 128)
-    ts(ub, (T.IP0[64:128, :, :], "IP0", 64, 128, 0, 224), float(MK), ALU.mult, float(-ws), ALU.add)
-    kids("W1", 0, Wn, "FH1", "FH2", 5, "svsvsvsv")
-    ts(ub, ub, U("E64"), ALU.mult)
-    quant("W1", Wn, 2 * Wn, C("FH1", 0, 4 * Wn))
-    quant("W1", 2 * Wn, 3 * Wn, C("FH2", 0, 4 * Wn))
-    dma("y", C("W2", 0, 3 * Wn), C("W1", 0, 3 * Wn), bits=3)
-    dma("y", C("W2S", 0, 3 * Wn), C("W1S", 0, 3 * Wn))
+    ks, kn = (0, hL + hR) if hq == "HQ" else (0 if hL else Wn - 128, 128)
+    kids(hq, ks, kn, "FH1", "FH2", 5, "ssvsvssv")
+    affine(C("CT", 0, 16), C("CTI", 0, 16), C("CLA"), 1.0)
+    affine(C("CT", 16, 32), C("CTI", 16, 32), C("CLB"), 1.0)
+    quant("HK1", 0, kn, C("FH1", 0, 4 * kn))
+    quant("HK2", 0, kn, C("FH2", 0, 4 * kn))
+    if hq == "HQ":
+        move("W1", 0, "HQ", 0, hL)
+        move("W1", hL + P, "HQ", hL, hR)
+    for k in (1, 2):
+        move("W1", k * Wn, "HK%d" % k, 0, hL)
+        move("W1", k * Wn + hL + P, "HK%d" % k, kn - hR, hR)
+    move("W2", 0, "W1", 0, 3 * Wn)
+    move("W2", G3, "W1", 2 * Wn, Wn)
     quant("WQ", 0, 128, C("WB"))
 
-    for k in range(3):
-        total_of("v", C("RED", k, k + 1), C("land2", k, 21, step=3))
-    tt(C("VV"), C("RED"), C("V3"), ALU.add)
-    cross("CC", 3, "VV")
-    gather("s", C("CB", 192, 384), C("CC"), C("OU", 52, 64))
-    gather("v", C("CB", 0, 192), C("CC"), C("OU", 40, 52))
-    copy("s", H("NC"), U("VV", 2, 3))
-    copy("s", U("NC"), U("VV", 2, 3))
-    copy("s", U("NS"), H("VV", 2, 3))
-    copy("s", H("NS"), H("VV", 2, 3))
-    tr(C("RR", 0, 192), C("CB", 0, 192))
-    tr(C("RR", 192, 384), C("CB", 192, 384))
-    affine(C("E1"), C("RR", 0, 192), C("VV", 0, 1), -1.0)
-    affine(C("E2"), C("RR", 0, 128), C("NS"), -1.0)
-    ts(C("NK1"), C("RR", 192, 384), C("VV", 1, 2), ALU.subtract, -TAU, ALU.mult)
-    ts(C("NK2"), C("RR", 192, 320), C("NC"), ALU.subtract, -TAU, ALU.mult)
+    for k in range(2):
+        total_of("s", C("VV", k + 2, k + 3), C("land2", k + 2, 32, step=4), C("JJ"))
+        total_of("v", C("VV", k, k + 1), C("land2", k, 32, step=4))
+    gather("v", C("RBS"), C("VV"), C("OU", 26, 30))
+    gather("s", C("RBK"), C("VV"), C("OU", 30, 34))
+    tr(C("SC", 0, 64), C("RBS"))
+    tr(C("KY", 0, 64), C("RBK"))
+    swap("SC")
+    swap("KY")
+    pairs("SC", "vsvs")
+    pairs("KY", "vsvs")
+    affine(C("E1"), C("SC"), C("VV", 1, 2), -1.0)
+    ts(C("NK1"), C("KY"), C("VV", 3, 4), ALU.subtract, -TAU, ALU.mult)
+    affine(C("E2"), C("SC", 32, 192), C("VV", 0, 1), -1.0)
     tt(C("M1"), C("E1"), C("NK1"), ALU.is_lt)
-    affine(C("KB"), C("VV", 1, 2), -BIG, 1.0)
-    affine(C("NB"), C("NC"), -BIG, 1.0)
-    affine(C("FR", 192, 256), C("RR", 256, 320), -BIG, 1.0)
+    ts(C("NK2"), C("KY", 32, 192), C("VV", 2, 3), ALU.subtract, -TAU, ALU.mult)
+    affine(C("KB"), C("VV", 3, 4), -BIG, 1.0)
+    affine(C("NB"), C("VV", 2, 3), -BIG, 1.0)
+    affine(C("NKE"), C("VV", 2, 3), C("CN"), 1.0)
+    for k in range(3):
+        affine(C("KE", k, k + 1), C("VV", 3, 4), float(272 + 2 * k * DUMP), 1.0)
     total_of("s", C("R1"), C("M1"), C("J3", 0, 192))
     tt(C("M2"), C("E2"), C("NK2"), ALU.is_lt)
-    gather("s", C("GD"), C("RR", 192, 256), C("OD", 0, 8))
     total_of("v", C("R2"), C("M2"))
-    ts(C("FF", 0, 1), C("R1"), 64.0, ALU.is_lt, C("KB"), ALU.mult)
-    ts(C("FF", 1, 2), C("R2"), C("TH"), ALU.is_lt, C("NB"), ALU.mult)
-    cross("FC", 2, "FF")
-    gather("s", C("FB", 96, 192), C("FC"), C("OU", 70, 76))
-    gather("v", C("FB", 0, 96), C("FC"), C("OU", 64, 70))
-    affine(C("Q1", 256, 257), C("VV", 1, 2), C("HIS"), 0.5)
+    gather("s", C("GD"), C("KY"), C("OD", 4, 12))
+    ts(C("FF", 1, 2), C("R1"), 64.0, ALU.is_lt, C("KB"), ALU.mult)
+    ts(C("FF", 0, 1), C("R2"), C("TH"), ALU.is_lt, C("NB"), ALU.mult)
+    gather("v", C("FB"), C("FF"), C("OU", 26, 30))
+    for f, a in ((H, 64), (U, 32)):
+        affine(f("FR", 192, 224), f("KY", a, a + 32), -BIG, 1.0)
+        affine(f("FR", 224, 256), f("KY", a + 96, a + 128), -BIG, 1.0)
+    affine(C("FL"), C("FF", 1, 2), 0.0, -1.0, ACT.Sign)
+    affine(C("F2"), C("FF", 0, 1), 0.0, -1.0, ACT.Sign)
+    tr(C("FR", 0, 64), C("FB"))
+    swap("FR")
+    pairs("FR", "vsvs")
+    affine(C("Q1"), C("FR"), C("KB"), -1.0, ACT.Sign, C("S1"))
+    affine(C("Q2"), C("FR"), C("NB"), -1.0, ACT.Sign, C("C2"))
+    for k, x in enumerate((2 * DUMP - 1, -2 * DUMP - 1, 1 - 4 * DUMP)):
+        ts(C("DB", k, k + 1), C("FL"), float(x), ALU.mult, C("KE", k, k + 1), ALU.add)
+    ts(C("DBN"), C("F2"), -6.0 * DUMP - 1, ALU.mult, C("NKE"), ALU.add)
+    win, off, ct = C("KY", 0, 96), C("OV"), C("CT")
+    run("v", lambda: g.vector.tensor_tensor(T.VA[:, 32:64], win[0].indirect(off[0]), ct[0], ALU.subtract), [win, off, ct], [C("VA", 32, 64)])
+    affine(C("VB", 32, 48), C("VA", 32, 48), C("BL1"), 1.0)
+    affine(C("VB", 48, 64), C("VA", 48, 64), C("BL2"), 1.0)
     tr(C("GT"), C("GD"))
-    tr(C("FR", 0, 192), C("FB"))
-    affine(C("Q2", 256, 257), C("NC"), C("ISC"), 0.5)
+    ts(C("OFF", 1, 4), C("DB"), C("S1"), ALU.add, 0.5, ALU.mult)
+    ts(C("OFF", 0, 1), C("C2"), C("DBN"), ALU.add, 0.5, ALU.mult)
+
+    scatter(C("RB"), C("OFF"), C("VB"))
+    scatter(C("RA"), C("OFF"), C("VA"))
+    affine(C("EB"), C("S1"), float(2 * e0 - 1), -1.0)
+    affine(C("JK", 0, 2), C("DB", 0, 2), C("EB"), -1.0, ACT.Sign, C("A12"))
+    affine(C("SB1"), C("DB", 2, 3), C("EB"), -1.0, ACT.Sign)
+    affine(C("BN"), C("DBN"), float(2 * e0 - 1), -1.0)
+    affine(C("SGN"), C("C2"), C("BN"), -1.0, ACT.Sign)
+    scaled("s", C("RB", e0 - 1, e0), C("RB", e0 - 1, e0), 0.0)
+    affine(C("AN"), C("SGN"), C("A12"), 1.0)
+    affine(C("XS", 224, 256), C("SEC"), C("SB1"), C("AN"))
+    xa, xb, x0, xo = C("RA", e0, e0 + 224), C("RB", e0 - 1, e0 + 223), C("INI"), C("XS", 0, 224)
+    run("v", lambda: g.vector.tensor_tensor_scan(xo[0], xa[0], xb[0], x0[0], ALU.add, ALU.subtract), [xa, xb, x0], [xo])
     affine(C("GV"), C("GT", 0, 128, step=32), float(-ws), 0.5, ACT.Relu)
     affine(C("GT4"), C("GV"), float(Wn - 1), -1.0, ACT.Relu)
-    ts(C("Q1", 0, 256), C("FR"), C("KB"), ALU.is_lt)
-    total_of("s", C("S1"), C("Q1"), C("J3"))
-    ts(C("Q2", 0, 256), C("FR"), C("NB"), ALU.is_lt)
-    ts(C("OFFG", 0, 4), C("GT4"), -1.0, ALU.mult, float(2 * Wn - 1), ALU.add)
-    ts(C("OFFG", 4, 8), C("GT4"), -1.0, ALU.mult, float(3 * Wn - 1), ALU.add)
-    affine(C("OO"), C("VV", 1, 2), C("NIS"), 0.5)
-    affine(C("FL"), C("FF", 0, 1), 0.0, -1.0, ACT.Sign)
-    affine(C("F2"), C("FF", 1, 2), 0.0, -1.0, ACT.Sign)
-    affine(C("BT", 0, 1), C("OO"), C("BC", 0, 1), -1.0)
-    affine(C("BT", 2, 3), C("OO"), C("BC", 2, 3), 1.0)
-    for k in range(3):
-        affine(C("WT1", k, k + 1), C("FL"), C("AL", k, k + 1), C("BT", k, k + 1))
-    affine(C("WTA"), C("F2"), 0.0, C("BEA"))
-    affine(C("WTB"), C("F2"), 0.0, C("BEB"))
-    total_of("v", C("S2"), C("Q2"))
+    for k in (0, 1):
+        affine(C("GO", 4 * k, 4 * k + 4), C("GT4"), float((2 + k) * Wn - 1), -1.0)
+    tr(C("XT"), C("XS"))
+    copy("v", C("OFFG"), C("GO"))
     pick("PK", "W1", 3 * Wn, C("OFFG"))
+    total_of("s", C("ZS", 7, 8), C("XT", 224, 256), C("J3", 0, 32))
+    tt(C("ZS", 0, 7), C("XT", 0, 224, step=32), C("XT", 16, 224, step=32), ALU.add)
     kids("PK", 0, 128, "GH1", "GH2", 5, "ssssssss")
-
-    for k in range(3):
-        ts(B3("SP", 32 * k, 32 * k + 32), B3("IP%d" % k, 0, 32), C("S1"), ALU.is_ge, C("WT1", k, k + 1), ALU.mult)
-    ts(B3("SP", 96, 128), B3("IP0", 0, 32), C("S2"), ALU.is_ge, C("WTA"), ALU.mult)
-    ts(B3("SP", 128, 160, 0, 64), B3("IP2", 0, 32, 0, 64), H("S2"), ALU.is_ge, H("WTB"), ALU.mult)
-    for b in range(7):
-        tr(B1("SPT", b), B1("SP", b))
-        total_of("svsvssv"[b], C("ZS", b, b + 1), B1("SPT", b), C("J3", 0, 160))
-    quadsum("ZI", "Z7", "ZS", 7)
-    ts(C("SI7"), C("ZI"), UNIT - 1, ALU.bitwise_and)
-    ts(C("HI7"), C("ZI"), 11, ALU.logical_shift_right)
-    gather("v", C("SB7"), C("SI7"), C("OU", 0, 14))
-    copy("v", C("HS7"), C("HI7"))
-    tr(C("SROW"), C("SB7"))
+    quadsum("ZT", "HS", "ZS", 8)
+    tr(C("XR"), C("ZT"))
+    gather("v", C("YY"), C("XR"), C("OD", 0, 4))
+    tr(C("YT"), C("YY"))
+    for h in (0, 1):
+        ts(part_of("OFFL", h, 14, 2), C("YT", 32 * h, 32 * h + 7), C("ZT", 7, 8), ALU.add, -0.5, ALU.mult)
     quant("W2", G1, G1 + 128, C("GH1"))
-    gather("s", C("SD", 192, 416), C("SROW"), C("OD", 12, 26))
-    gather("v", C("SD", 0, 192), C("SROW"), C("OD", 0, 12))
-    gather("s", C("HB7"), C("HS7"), C("OU", 0, 14))
     quant("W2", G2, G2 + 128, C("GH2"))
-    tr(C("STT"), C("SD"))
-    copy("v", C("OFFL", 0, 13), C("STT", 0, 416, step=32))
-    pick("FQ", "W2", 3 * Wn + 256, C("OFFL", 0, 13))
+    pick("FQ", "W2", G3 + Wn, C("OFFL", 0, 13))
     mm(bank(0, E), "WQ", 0, "FQ", 0, E)
-    tr(C("HROW"), C("HB7"))
     dma("y", ext(T.oc[:, :]), C("FQ"), bits=2)
-    copy("s", C("YS", 0, 104), bank(0, 104))
-    copy("v", C("YS", 104, E), bank(0, E, c0=104))
+    kw, kl = C("KY"), C("OD", 12, 20)
+    for k, at in ((0.0, G1), (1.0, G2)):
+        ho = C("HT", at, at + 128)
+        run("s", lambda: g.scalar.activation(ho[0], kw[0].indirect(kl[0]), ACT.Identity, bias=k, scale=2.0), [kw, kl], [ho])
+    gather("s", C("HR"), C("HT", 0, G3 + Wn), C("OFFL", 0, 13))
+    copy("v", C("YS"), bank(0, E))
     dma("s", ext(T.y[:, :]), C("YS"))
-    dma("y", ext(T.hs[:, :]), C("HROW", 0, E, 0, 1))
+    dma("y", ext(T.hs[:, :]), C("HR", 0, E, 0, 1))
     for k in range(4):
         dma("ysys"[k], ext(T.osc[4 * k:4 * k + 4, :]), C("FQS", 0, E, 32 * k, 32 * k + 4))
 

@@ -9,12 +9,12 @@ TAU = 1e-32
 BIG = 65536.0
 DUMP = 1720
 ROW = 8 + 4 * DUMP
+CW = 360
 
 SMALL = {}
-for _n, _w in dict(NST=6, PL=6, PR=6, PT=6, PB=6, PZ=6, RK=6, KEYC=6, KEYN=6, V2C=6, VV=4, R1=1, R2=1, FF=2, FL=1, F2=1, TH=1, KB=1, NB=1,
-                   PID=1, BITS=4, SG=1, ISC=1, CK=1, I2=1, NT=1, KE=3, DB=3, DBN=1, NKE=1, CN=1, BN=1, EB=1, S1=1, C2=1, A12=1,
-                   SB1=1, SGN=1, AN=1, INI=1, CLA=1, CLB=1, BL1=1, BL2=1, GRP=1, GR=1, ZS=8, HS=8, GV=4, GT4=4, GO=8, JJ=8,
-                   JK=8).items():
+for _n, _w in dict(NST=6, PR=6, PB=6, PZ=6, RK=6, KEYC=6, KEYN=6, V2C=6, VV=4, R1=1, R2=1, FF=2, FL=1, F2=1, TH=1, KB=1, NB=1,
+                   PID=1, BITS=4, SG=1, ISC=1, CK=1, I2=1, NT=1, TN=1, KE=3, DB=3, DBN=1, NKE=1, CN=1, BN=1, EB=1, S1=1, C2=1, A12=1,
+                   SB1=1, SGN=1, AN=1, INI=1, CLA=1, CLB=1, BL1=1, BL2=1, GRP=1, GR=1, ZS=8, HS=8, JJ=8, JK=8).items():
     SMALL[_n] = (8 * sum((w + 7) // 8 for _, w in SMALL.values()), _w)
 
 
@@ -26,14 +26,15 @@ def _scratch():
         for name, n in kw.items():
             d[name] = ("sbuf", [128, n], dtype)
     sb(h, XB=4 * P, U4=4, UB=512, AB=2048, BB=2048, WB=512, KH1=4 * P, KH2=4 * P, FH1=576, FH2=576,
-       GH1=512, GH2=512, CL=384, CM=6 * 352, J1=352, M1=192, M2=160)
+       GH1=512, GH2=512, CL=384, J1=CW, M1=192, M2=160)
     for name, n in dict(UQ=128, AQ=512, BQ=512, WQ=128, W1=3 * WMAX, HQ=144, HK1=144, HK2=144, PK=128, W2=4 * WMAX + 256, FQ=E).items():
         d[name] = ("sbuf", [128, n], q)
         d[name + "S"] = ("sbuf", [128, n], s)
-    sb(f, Z0=128, OC=8, OCB=64, TOWN=64, ST0=192, DL=384, TI0=384, TIE=384, land1=24, LB=352, LT=352, RM=32,
+    sb(f, CM=6 * CW, Z0=128, OC=8, OCB=64, TOWN=64, ST0=192, DL=384, TI0=384, TIE=384, land1=24, LB=352, LT=352, RM=32,
        SLT=32, SLT2=32, VALT=192, AD=192, EV=576, ET=576, land2=32, RBS=64, RBK=64, SC=192, KY=192, E1=192, E2=160, NK1=192,
        NK2=160, FB=64, FR=256, Q1=256, Q2=256, VA=64, VB=64, CTI=32, CT=32, SEC=32, RA=ROW, RB=ROW, XS=256, XT=256, ZT=32, XR=32,
-       YY=64, YT=64, HT=4 * WMAX + 256, HR=E, GD=128, GT=128, YS=E, J3=256, OI2=22, SM=8 * sum((w + 7) // 8 for _, w in SMALL.values()))
+       YY=64, YT=64, HT=4 * WMAX + 256, HR=E, GD=128, GE=128, GT=128, YS=E, J3=256, OI2=22,
+       SM=8 * sum((w + 7) // 8 for _, w in SMALL.values()))
     sb("int32", OI=34, PIN=1, PA=4)
     sb("uint16", OU=34, OD=20, OV=2, OFF=4, OFFG=8, OFFL=14)
     d["PS"] = ("psum", [128, 4096], f)
@@ -193,6 +194,10 @@ def rank_program(g, core, T, topo):
         src = win[0].indirect(off[0])
         run(q, (lambda: g.vector.tensor_copy(o[0], src)) if q == "v" else (lambda: g.scalar.activation(o[0], src, ACT.Copy)), [win, off], [o])
 
+    def gathered(o, win, off, bias, scale, func):
+        src = win[0].indirect(off[0])
+        run("s", lambda: g.scalar.activation(o[0], src, func, bias=bias, scale=scale), [win, off], [o])
+
     def scatter(win, off, i):
         run("v", lambda: g.vector.tensor_copy(win[0].indirect(off[0]), i[0]), [i, off], [win])
 
@@ -239,13 +244,21 @@ def rank_program(g, core, T, topo):
             mm(bank(k, n), "AQ" if i < 4 else "BQ", 128 * (i % 4), src, c0, c0 + n)
             scaled(pat[i], part_of(t1 if i < 4 else t2, i % 4, 4 * n, 4), bank(k, n), 0.0625)
 
+    def split(a, b):
+        if topo.chip(a) != topo.chip(b):
+            return topo.engines(a, b)
+        off = topo.engines(a, [c for c in T.cores if topo.chip(c) != topo.chip(a)][0])
+        return [e for e in topo.engines(a, b) if e not in off][:2]
+
+    def arrivals():
+        return sum(len(split(c, core)) for c in T.cores if c != core)
+
     def fan(src, dst, width, arr):
         deps("g", [src], [])
         others = [c for c in T.cores if c != core]
         far = [c for c in others if topo.chip(c) != topo.chip(core)]
         near = [c for c in others if topo.chip(c) == topo.chip(core)]
-        fe = topo.engines(core, far[0])
-        ne = [e for e in topo.engines(core, near[0]) if e not in fe]
+        fe, ne = split(core, far[0]), split(core, near[0])
 
         def tf(dsts, eng):
             ids, aps = [], []
@@ -313,6 +326,7 @@ def rank_program(g, core, T, topo):
     affine(C("I2"), IC, 0.0, 2.0)
     affine(C("ISC"), C("SG"), 0.0, 1.0, ACT.Relu)
     affine(C("NT"), C("PID"), C("I2"), -1.0)
+    affine(C("TN"), C("NT"), 0.0, TAU)
     affine(C("CK"), C("I2"), C("ISC"), 1.0)
 
     for t in range(4):
@@ -326,7 +340,7 @@ def rank_program(g, core, T, topo):
     copy("v", U("OC", 1, 2), bank(2, 1, 64, 128))
     copy("v", H("OC", 1, 2), bank(2, 1, 64, 128))
     fan(C("OC", 0, 2), "land1", 2, "ar1")
-    arrive("ar1", 8 * 7, [C("land1", 0, 14)])
+    arrive("ar1", arrivals(), [C("land1", 0, 14)])
     iota(C("TI0"), [[-32, 6], [64, 2], [1, 32]], 0, 0)
     if r + 1 < N:
         halo(r + 1, P - _halo(r + 1)[0], P, False)
@@ -338,32 +352,17 @@ def rank_program(g, core, T, topo):
     iota(C("RM"), [[1, 32]], 0, 0)
     iota(C("RK"), [[64, 6]], 2 * P * r, 0)
     iota(C("OI2", 0, 4), [[16, 2], [0, 2]], 0, 0)
+    iota(C("OI2", 20, 22), [[0, 2]], 32, 0)
+    iota(C("CTI"), [[2 * (G2 - G1) - 2, 2], [2, 16]], 2 * (G1 + ws), 0)
     for q in range(4):
         st, sh = (96 if q % 2 == 0 else -96), (32 if q < 2 else -32)
         iota(Q("OI2", q, 4, 12), [[st, 2], [16, 2], [0, 2]], 96 * (q % 2) + 32 + 32 * (q // 2), 0)
         iota(Q("OI2", q, 12, 20), [[sh, 2], [st, 2], [16, 2]], 96 * (q % 2) + 32 + 32 * (q // 2), 0)
-    iota(C("OI2", 20, 22), [[0, 2]], 32, 0)
-    iota(C("CTI"), [[2 * (G2 - G1) - 2, 2], [2, 16]], 2 * (G1 + ws), 0)
-    iota(C("RA", e0 - 8, e0 + 232), [[0, 240]], 0, 0)
-    iota(C("RB", e0 - 8, e0 + 232), [[0, 240]], 0, 0)
-    iota(C("RA", e0 - 8, e0 + 232, 0, 16), [[0, 240]], -2, 0)
-    iota(C("INI"), [[0, 1]], 0, 0)
-    iota(C("INI", 0, 1, 0, 16), [[0, 1]], 320 - 2 * (E * r - ws - 1), 0)
-    for t, x in (("VA", 1), ("VB", 0)):
-        iota(H(t, 0, 32), [[0, 32]], -2 * Wn, 0)
-        iota(U(t, 0, 32), [[2 * G3 - 4 * Wn, 2], [0, 16]], -2 * G3 + 2 * x, 0)
-    iota(C("VA", 0, 32, 0, 16), [[0, 32]], -2 * Wn - 2, 0)
-    iota(H("SEC"), [[0, 32]], 0, 0)
-    iota(U("SEC"), [[0, 32]], 1, 0)
-    iota(C("ZT"), [[0, 32]], 0, 0)
-    for k in range(3):
-        iota(C("HT", k * Wn, k * Wn + Wn), [[4, Wn]], 4 * ws + 2 * (k // 2), 0)
-    iota(C("HT", G3, G3 + Wn), [[4, Wn]], 4 * ws + 1, 0)
 
     copy("v", C("OU"), C("OI"))
     tr(C("ST0"), bank(0, P))
     gather("s", C("OCB"), C("OC"), C("OU", 0, 4))
-    ts(C("TIE"), C("TI0"), C("NT"), ALU.is_lt, -TAU, ALU.mult)
+    ts(C("TIE"), C("TI0"), TAU, ALU.mult, C("TN"), ALU.subtract)
     tr(C("TOWN"), C("OCB"))
     copy("s", H("V2C"), C("ST0", 0, 192, 0, 64, 32))
     for k in range(6):
@@ -383,21 +382,19 @@ def rank_program(g, core, T, topo):
     affine(C("SLT2"), C("SLT"), 64.0, 1.0)
     affine(C("KEYN"), C("KEYC"), 0.0, -1.0)
     for k in range(6):
-        total_of("s", C("PL", k, k + 1), C("CL", 64 * k, 64 * k + 64), C("J1", 0, 64))
+        total_of("s", C("CM", CW * k + 352, CW * k + 353), C("CL", 64 * k, 64 * k + 64), C("J1", 0, 64))
     tr(C("LT", 0, 192), C("LB", 0, 192))
     tr(C("LT", 192, 352), C("LB", 192, 352))
     quant("BQ", 0, 512, C("BB"))
-    ts(C("OD"), C("OI2", 0, 20), PM16, ALU.add)
-    ts(C("OV"), C("OI2", 20, 22), IC, ALU.add)
 
     def against(ks):
         for k in ks:
             sc = C("ST0", 32 * k, 32 * k + 1)
             if cut > 0:
-                ts(C("CM", 352 * k, 352 * k + cut), C("LT", 0, cut), sc, ALU.is_ge)
+                ts(C("CM", CW * k, CW * k + cut), C("LT", 0, cut), sc, ALU.is_ge)
             if cut < 352:
-                ts(C("CM", 352 * k + cut, 352 * k + 352), C("LT", cut, 352), sc, ALU.is_gt)
-            total_of("v" if k == 5 else "s", C("PR", k, k + 1), C("CM", 352 * k, 352 * k + 352), C("J1"))
+                ts(C("CM", CW * k + cut, CW * k + 352), C("LT", cut, 352), sc, ALU.is_gt)
+            total_of("v" if k == 5 else "s", C("PR", k, k + 1), C("CM", CW * k, CW * k + 353), C("J1", 0, 353))
     kids("W1", hL, P, "KH1", "KH2", 3, "ssssssss")
     against((0, 1, 2))
     quant("W1", Wn + hL, Wn + hL + P, C("KH1"))
@@ -407,8 +404,7 @@ def rank_program(g, core, T, topo):
     against((3, 4, 5))
     tr(H("VALT"), bank(3, P, 0, 64))
     tr(U("VALT"), bank(4, P, 64, 128))
-    tt(C("PT"), C("PR"), C("PL"), ALU.add)
-    quadsum("PZ", "PB", "PT", 6)
+    quadsum("PZ", "PB", "PR", 6)
     affine(C("TH"), IC, 64.0, -1.0)
     affine(C("CN"), C("ISC"), float(272 + 6 * DUMP), 2.0)
     affine(C("GR"), GR, 0.0, 1.0, ACT.Sign)
@@ -437,8 +433,23 @@ def rank_program(g, core, T, topo):
     total_of("s", C("land2", 31, 32), C("ET", 0, 192), C("J3", 0, 192))
     total_of("v", C("land2", 29, 30), C("ET", 384, 576))
     fan(C("land2", 28, 32), "land2", 4, "ar2")
-    arrive("ar2", 8 * 7, [C("land2", 0, 28)])
+    arrive("ar2", arrivals(), [C("land2", 0, 28)])
 
+    iota(C("RA", e0 - 8, e0 + 232), [[0, 240]], 0, 0)
+    iota(C("RB", e0 - 8, e0 + 232), [[0, 240]], 0, 0)
+    iota(C("INI"), [[0, 1]], 0, 0)
+    iota(C("RA", e0 - 8, e0 + 232, 0, 16), [[0, 240]], -2, 0)
+    iota(C("INI", 0, 1, 0, 16), [[0, 1]], 320 - 2 * (E * r - ws - 1), 0)
+    for t, x in (("VA", 1), ("VB", 0)):
+        iota(H(t, 0, 32), [[0, 32]], -2 * Wn, 0)
+        iota(U(t, 0, 32), [[2 * G3 - 4 * Wn, 2], [0, 16]], -2 * G3 + 2 * x, 0)
+    iota(C("VA", 0, 32, 0, 16), [[0, 32]], -2 * Wn - 2, 0)
+    iota(H("SEC"), [[0, 32]], 0, 0)
+    iota(U("SEC"), [[0, 32]], 1, 0)
+    iota(C("ZT"), [[0, 32]], 0, 0)
+    for k in range(3):
+        iota(C("HT", k * Wn, k * Wn + Wn), [[4, Wn]], 4 * ws + 2 * (k // 2), 0)
+    iota(C("HT", G3, G3 + Wn), [[4, Wn]], 4 * ws + 1, 0)
     ks, kn = (0, hL + hR) if hq == "HQ" else (0 if hL else Wn - 128, 128)
     kids(hq, ks, kn, "FH1", "FH2", 5, "ssvsvssv")
     affine(C("CT", 0, 16), C("CTI", 0, 16), C("CLA"), 1.0)
@@ -453,6 +464,8 @@ def rank_program(g, core, T, topo):
         move("W1", k * Wn + hL + P, "HK%d" % k, kn - hR, hR)
     move("W2", 0, "W1", 0, 3 * Wn)
     move("W2", G3, "W1", 2 * Wn, Wn)
+    ts(C("OD"), C("OI2", 0, 20), PM16, ALU.add)
+    ts(C("OV"), C("OI2", 20, 22), IC, ALU.add)
     quant("WQ", 0, 128, C("WB"))
 
     for k in range(2):
@@ -479,50 +492,49 @@ def rank_program(g, core, T, topo):
     total_of("s", C("R1"), C("M1"), C("J3", 0, 192))
     tt(C("M2"), C("E2"), C("NK2"), ALU.is_lt)
     total_of("v", C("R2"), C("M2"))
-    gather("s", C("GD"), C("KY"), C("OD", 4, 12))
+    gathered(C("GD"), C("KY"), C("OD", 4, 12), float(-ws), 0.5, ACT.Relu)
     ts(C("FF", 1, 2), C("R1"), 64.0, ALU.is_lt, C("KB"), ALU.mult)
     ts(C("FF", 0, 1), C("R2"), C("TH"), ALU.is_lt, C("NB"), ALU.mult)
     gather("v", C("FB"), C("FF"), C("OU", 26, 30))
     for f, a in ((H, 64), (U, 32)):
         affine(f("FR", 192, 224), f("KY", a, a + 32), -BIG, 1.0)
         affine(f("FR", 224, 256), f("KY", a + 96, a + 128), -BIG, 1.0)
-    affine(C("FL"), C("FF", 1, 2), 0.0, -1.0, ACT.Sign)
-    affine(C("F2"), C("FF", 0, 1), 0.0, -1.0, ACT.Sign)
+    affine(C("GE"), C("GD"), float(Wn - 1), -1.0, ACT.Relu)
     tr(C("FR", 0, 64), C("FB"))
     swap("FR")
     pairs("FR", "vsvs")
+    affine(C("FL"), C("FF", 1, 2), 0.0, -1.0, ACT.Sign)
+    affine(C("F2"), C("FF", 0, 1), 0.0, -1.0, ACT.Sign)
     affine(C("Q1"), C("FR"), C("KB"), -1.0, ACT.Sign, C("S1"))
     affine(C("Q2"), C("FR"), C("NB"), -1.0, ACT.Sign, C("C2"))
+    win, off, ct = C("KY", 0, 96), C("OV"), C("CT")
+    run("v", lambda: g.vector.tensor_tensor(T.VA[:, 32:64], win[0].indirect(off[0]), ct[0], ALU.subtract), [win, off, ct], [C("VA", 32, 64)])
+    tr(C("GT"), C("GE"))
     for k, x in enumerate((2 * DUMP - 1, -2 * DUMP - 1, 1 - 4 * DUMP)):
         ts(C("DB", k, k + 1), C("FL"), float(x), ALU.mult, C("KE", k, k + 1), ALU.add)
     ts(C("DBN"), C("F2"), -6.0 * DUMP - 1, ALU.mult, C("NKE"), ALU.add)
-    win, off, ct = C("KY", 0, 96), C("OV"), C("CT")
-    run("v", lambda: g.vector.tensor_tensor(T.VA[:, 32:64], win[0].indirect(off[0]), ct[0], ALU.subtract), [win, off, ct], [C("VA", 32, 64)])
     affine(C("VB", 32, 48), C("VA", 32, 48), C("BL1"), 1.0)
     affine(C("VB", 48, 64), C("VA", 48, 64), C("BL2"), 1.0)
-    tr(C("GT"), C("GD"))
+    for k in (0, 1):
+        ts(C("OFFG", 4 * k, 4 * k + 4), C("GT", 0, 128, step=32), -1.0, ALU.mult, float((2 + k) * Wn - 1), ALU.add)
     ts(C("OFF", 1, 4), C("DB"), C("S1"), ALU.add, 0.5, ALU.mult)
     ts(C("OFF", 0, 1), C("C2"), C("DBN"), ALU.add, 0.5, ALU.mult)
 
     scatter(C("RB"), C("OFF"), C("VB"))
     scatter(C("RA"), C("OFF"), C("VA"))
     affine(C("EB"), C("S1"), float(2 * e0 - 1), -1.0)
-    affine(C("JK", 0, 2), C("DB", 0, 2), C("EB"), -1.0, ACT.Sign, C("A12"))
-    affine(C("SB1"), C("DB", 2, 3), C("EB"), -1.0, ACT.Sign)
     affine(C("BN"), C("DBN"), float(2 * e0 - 1), -1.0)
+    affine(C("JK", 0, 2), C("DB", 0, 2), C("EB"), -1.0, ACT.Sign, C("A12"))
     affine(C("SGN"), C("C2"), C("BN"), -1.0, ACT.Sign)
-    scaled("s", C("RB", e0 - 1, e0), C("RB", e0 - 1, e0), 0.0)
+    affine(C("SB1"), C("DB", 2, 3), C("EB"), -1.0, ACT.Sign)
     affine(C("AN"), C("SGN"), C("A12"), 1.0)
+    scaled("s", C("RB", e0 - 1, e0), C("RB", e0 - 1, e0), 0.0)
     affine(C("XS", 224, 256), C("SEC"), C("SB1"), C("AN"))
+    pick("PK", "W1", 3 * Wn, C("OFFG"))
     xa, xb, x0, xo = C("RA", e0, e0 + 224), C("RB", e0 - 1, e0 + 223), C("INI"), C("XS", 0, 224)
     run("v", lambda: g.vector.tensor_tensor_scan(xo[0], xa[0], xb[0], x0[0], ALU.add, ALU.subtract), [xa, xb, x0], [xo])
-    affine(C("GV"), C("GT", 0, 128, step=32), float(-ws), 0.5, ACT.Relu)
-    affine(C("GT4"), C("GV"), float(Wn - 1), -1.0, ACT.Relu)
-    for k in (0, 1):
-        affine(C("GO", 4 * k, 4 * k + 4), C("GT4"), float((2 + k) * Wn - 1), -1.0)
     tr(C("XT"), C("XS"))
-    copy("v", C("OFFG"), C("GO"))
-    pick("PK", "W1", 3 * Wn, C("OFFG"))
+    gathered(C("HT", G1, G1 + 128), C("KY"), C("OD", 12, 20), 0.0, 2.0, ACT.Identity)
     total_of("s", C("ZS", 7, 8), C("XT", 224, 256), C("J3", 0, 32))
     tt(C("ZS", 0, 7), C("XT", 0, 224, step=32), C("XT", 16, 224, step=32), ALU.add)
     kids("PK", 0, 128, "GH1", "GH2", 5, "ssssssss")
@@ -537,16 +549,13 @@ def rank_program(g, core, T, topo):
     pick("FQ", "W2", G3 + Wn, C("OFFL", 0, 13))
     mm(bank(0, E), "WQ", 0, "FQ", 0, E)
     dma("y", ext(T.oc[:, :]), C("FQ"), bits=2)
-    kw, kl = C("KY"), C("OD", 12, 20)
-    for k, at in ((0.0, G1), (1.0, G2)):
-        ho = C("HT", at, at + 128)
-        run("s", lambda: g.scalar.activation(ho[0], kw[0].indirect(kl[0]), ACT.Identity, bias=k, scale=2.0), [kw, kl], [ho])
+    affine(C("HT", G2, G2 + 128), C("HT", G1, G1 + 128), 1.0, 1.0)
     gather("s", C("HR"), C("HT", 0, G3 + Wn), C("OFFL", 0, 13))
-    copy("v", C("YS"), bank(0, E))
-    dma("s", ext(T.y[:, :]), C("YS"))
-    dma("y", ext(T.hs[:, :]), C("HR", 0, E, 0, 1))
     for k in range(4):
-        dma("ysys"[k], ext(T.osc[4 * k:4 * k + 4, :]), C("FQS", 0, E, 32 * k, 32 * k + 4))
+        dma("yyss"[k], ext(T.osc[4 * k:4 * k + 4, :]), C("FQS", 0, E, 32 * k, 32 * k + 4))
+    copy("v", C("YS"), bank(0, E))
+    dma("y", ext(T.y[:, :]), C("YS"))
+    dma("s", ext(T.hs[:, :]), C("HR", 0, E, 0, 1))
 
     total["loc"] = loc[0]
     for sem in SEMAPHORES:

@@ -5,16 +5,17 @@ ALU = AluOpType
 ACT = ActivationFunctionType
 N, P, K, E = 8, 192, 64, 208
 WMAX = 336
-TAU = 1e-32
+TAU = 2.0 ** -106
 BIG = 65536.0
 DUMP = 1720
 ROW = 8 + 4 * DUMP
 CW = 360
 
 SMALL = {}
-for _n, _w in dict(NST=6, PR=6, PB=6, PZ=6, RK=6, KEYC=6, KEYN=6, V2C=6, VV=4, R1=1, R2=1, FF=2, FL=1, F2=1, TH=1, KB=1, NB=1,
-                   PID=1, BITS=4, SG=1, ISC=1, CK=1, I2=1, NT=1, TN=1, KE=3, DB=3, DBN=1, NKE=1, CN=1, BN=1, EB=1, S1=1, C2=1, A12=1,
-                   SB1=1, SGN=1, AN=1, INI=1, CLA=1, CLB=1, BL1=1, BL2=1, GRP=1, GR=1, ZS=8, HS=8, JJ=8, JK=8).items():
+for _n, _w in dict(PR=6, PB=6, PZ=6, RK=6, KEYC=6, KEYN=6, V2C=6, VV=4, R1=1, R2=1, FL=1, F2=1, TH=1, KB=1, NB=1, TK=1,
+                   PID=1, BITS=4, SG=1, ISC=1, CK=1, I2=1, NT=1, NTB=1, NTN=6, S1A=1, C2A=1, KES=1, KE=3, DB=3, DBN=1, NKA=1, NKE=1,
+                   CN=1, BN=1, EB=1, S1=1, C2=1, A12=1, SB1=1, SGN=1, AN=1, INI=1, CLA=1, CLP=1, CLM=1, CLB=1, BL1=1, BL2=1, GRP=1,
+                   GR=1, ZS=8, HS=8, JJ=16, JK=8).items():
     SMALL[_n] = (8 * sum((w + 7) // 8 for _, w in SMALL.values()), _w)
 
 
@@ -26,14 +27,14 @@ def _scratch():
         for name, n in kw.items():
             d[name] = ("sbuf", [128, n], dtype)
     sb(h, XB=4 * P, U4=4, UB=512, AB=2048, BB=2048, WB=512, KH1=4 * P, KH2=4 * P, FH1=576, FH2=576,
-       GH1=512, GH2=512, CL=384, J1=CW, M1=192, M2=160)
+       GH1=512, GH2=512, CL=384, J0=384, J1=6 * CW, M1=192, M2=160, Z0=128)
     for name, n in dict(UQ=128, AQ=512, BQ=512, WQ=128, W1=3 * WMAX, HQ=144, HK1=144, HK2=144, PK=128, W2=4 * WMAX + 256, FQ=E).items():
         d[name] = ("sbuf", [128, n], q)
         d[name + "S"] = ("sbuf", [128, n], s)
-    sb(f, CM=6 * CW, Z0=128, OC=8, OCB=64, TOWN=64, ST0=192, DL=384, TI0=384, TIE=384, land1=24, LB=352, LT=352, RM=32,
+    sb(f, CM=6 * CW, C64=32, THT=32, OC=8, OCB=64, TOWN=64, ST0=192, DL=384, TI0=64, TIE=384, land1=24, LB=352, LT=352,
        SLT=32, SLT2=32, VALT=192, AD=192, EV=576, ET=576, land2=32, RBS=64, RBK=64, SC=192, KY=192, E1=192, E2=160, NK1=192,
        NK2=160, FB=64, FR=256, Q1=256, Q2=256, VA=64, VB=64, CTI=32, CT=32, SEC=32, RA=ROW, RB=ROW, XS=256, XT=256, ZT=32, XR=32,
-       YY=64, YT=64, HT=4 * WMAX + 256, HR=E, GD=128, GE=128, GT=128, YS=E, J3=256, OI2=22,
+       YY=64, YT=64, HT=4 * WMAX + 256, HR=E, GD=128, GE=128, GT=128, YS=E, J3=576, OI2=22,
        SM=8 * sum((w + 7) // 8 for _, w in SMALL.values()))
     sb("int32", OI=34, PIN=1, PA=4)
     sb("uint16", OU=34, OD=20, OV=2, OFF=4, OFFG=8, OFFL=14)
@@ -112,7 +113,7 @@ def rank_program(g, core, T, topo):
             for (a0, a1, b0, b1, kind, rq, sem, val, snap) in recs.get(name, []):
                 if a0 >= p1 or p0 >= a1 or b0 >= c1 or c0 >= b1:
                     continue
-                if name != "PS" and not kind and (not wr or rq == q):
+                if not kind and (rq == q or (not wr and name != "PS")):
                     continue
                 if val > todo.get(sem, (0, 0))[0]:
                     todo[sem] = (val, snap)
@@ -219,16 +220,19 @@ def rank_program(g, core, T, topo):
         run("g", (lambda: g.iota(o[0], pattern, base, cm)) if whole else
             (lambda: g.iota(o[0], pattern, base, cm, allow_small_or_imprecise_dtypes=True)), [], [o])
 
-    def pick(o, src, c1, off):
-        a, w = C(o), C(src, 0, c1)
+    def pick_codes(o, c0, c1, src, n, off):
+        a, w = C(o, c0, c1), C(src, 0, n)
         run("v", lambda: g.vector.tensor_copy(a[0].bitcast(dt.uint32), w[0].bitcast(dt.uint32).indirect(off[0])), [w, off], [a])
-        gather("s", C(o + "S"), C(src + "S", 0, c1), off)
 
-    def quadsum(o, h, i, n):
+    def pick_scales(o, c0, c1, src, n, off):
+        gather("s", C(o + "S", c0, c1), C(src + "S", 0, n), off)
+
+    def quadsum(o, h, i, n, between=None):
         tt(H(h, 0, n), H(i, 0, n), U(i, 0, n), ALU.add)
-        for q in (0, 1):
+        if between:
+            between()
+        for q in range(4):
             tt(Q(o, q, 0, n), Q(h, 0, 0, n), Q(h, 1, 0, n), ALU.add)
-        copy("v", U(o, 0, n), H(o, 0, n))
 
     def swap(name):
         copy("s", H(name, 64, 96), U(name, 32, 64))
@@ -238,8 +242,10 @@ def rank_program(g, core, T, topo):
         for q in range(4):
             copy(order[q], Q(name, q, 96, 192), Q(name, q ^ 1, 0, 96))
 
-    def kids(src, c0, n, t1, t2, first, pat):
+    def kids(src, c0, n, t1, t2, first, pat, halfway=None):
         for i in range(8):
+            if i == 4 and halfway:
+                halfway()
             k = (first + i) % 8
             mm(bank(k, n), "AQ" if i < 4 else "BQ", 128 * (i % 4), src, c0, c0 + n)
             scaled(pat[i], part_of(t1 if i < 4 else t2, i % 4, 4 * n, 4), bank(k, n), 0.0625)
@@ -296,10 +302,11 @@ def rank_program(g, core, T, topo):
         dma("y", C(name), ext(t[:, :]))
 
     iota(C("PIN"), [[0, 1]], 0, 1, True)
-    iota(C("PID"), [[0, 1]], 0, 1)
+    iota(C("RK"), [[64, 6]], 2 * P * r, 0)
+    iota(C("TI0"), [[64, 2], [1, 32]], 0, 0)
     iota(C("OI", 0, 2), [[0, 2]], 0, 0, True)
-    iota(H("OI", 2, 4), [[0, 2]], 4, 0, True)
-    iota(U("OI", 2, 4), [[0, 2]], 1, 0, True)
+    iota(C("OI", 2, 4), [[0, 2]], 4, 0, True)
+    upper = [(2, 4, -3)]
     at, nb, na = 4, r, N - 1 - r
     for what, s0, n in (("main", 0, nb), ("rest", 0, nb), ("rest", nb, na), ("main", nb, na)):
         if what == "main" and n:
@@ -307,27 +314,41 @@ def rank_program(g, core, T, topo):
             at += 2 * n
         elif n:
             m = (n + 1) // 2
-            iota(H("OI", at, at + 2 * m), [[4, m], [0, 2]], 2 * s0 + 1, 0, True)
+            iota(C("OI", at, at + 2 * m), [[4, m], [0, 2]], 2 * s0 + 1, 0, True)
             if n // 2:
-                iota(U("OI", at, at + 2 * (n // 2)), [[4, n // 2], [0, 2]], 2 * s0 + 3, 0, True)
+                upper.append((at, at + 2 * (n // 2), 2))
             if n % 2:
-                iota(U("OI", at + n - 1, at + n + 1), [[0, 2]], 16, 0, True)
+                upper.append((at + n - 1, at + n + 1, 16 - (2 * s0 + 1 + 4 * (m - 1))))
             at += 2 * m
     iota(C("OI", 26, 34), [[1, 4], [0, 2]], 0, 0, True)
     cut = 32 * (nb + (nb + 1) // 2)
     memset(C("Z0"), 0.0)
     memset(C("OC"), -9e29)
     memset(C("land1", 16, 20), -9e29)
+    memset(C("C64"), 64.0)
+    copy("v", C("PID"), C("PIN"))
     for k, m in enumerate((31, 15, 32, 112)):
         ts(C("PA", k, k + 1), C("PIN"), m, ALU.bitwise_and)
     copy("v", C("BITS"), C("PA"))
     IC, PM16, QO, GR = [C("BITS", k, k + 1) for k in range(4)]
     affine(C("SG"), C("PID"), -63.5, 1.0, ACT.Sign)
     affine(C("I2"), IC, 0.0, 2.0)
+    affine(C("TH"), IC, 64.0, -1.0)
+    affine(C("GR"), GR, 0.0, 1.0, ACT.Sign)
+    affine(C("SLT"), C("TI0", 0, 32), QO, 1.0)
     affine(C("ISC"), C("SG"), 0.0, 1.0, ACT.Relu)
     affine(C("NT"), C("PID"), C("I2"), -1.0)
-    affine(C("TN"), C("NT"), 0.0, TAU)
+    affine(C("CLA"), PM16, C("PID"), -1.0)
+    affine(C("GRP"), C("GR"), 2.0, -2.0)
+    affine(C("SLT2"), C("SLT"), 64.0, 1.0)
     affine(C("CK"), C("I2"), C("ISC"), 1.0)
+    affine(C("NTB"), C("NT"), P * r * TAU, -TAU)
+    affine(C("THT"), C("TI0", 0, 32), C("TH"), 0.0)
+    affine(C("NTN"), C("RK"), C("NTB"), -0.5 * TAU)
+    affine(C("KEYC"), C("RK"), C("CK"), 1.0)
+    affine(U("V2C"), U("RK"), U("I2"), 1.0)
+    affine(C("CLP"), C("CLA"), C("GRP"), 2.0)
+    affine(C("KEYN"), C("KEYC"), 0.0, -1.0)
 
     for t in range(4):
         ts(part_of("UB", t, 512, 4), C("Z0"), C("U4", t, t + 1), ALU.add)
@@ -336,12 +357,11 @@ def rank_program(g, core, T, topo):
     mm(bank(1, 128), "W1", hL, "UQ", 0, 128)
     mm(bank(2, 128), "W1", hL + 64, "UQ", 0, 128)
     mm(bank(0, P), "UQ", 0, "W1", hL, hL + P)
-    copy("s", C("OC", 0, 1), bank(1, 1))
+    copy("v", C("OC", 0, 1), bank(1, 1))
     copy("v", U("OC", 1, 2), bank(2, 1, 64, 128))
     copy("v", H("OC", 1, 2), bank(2, 1, 64, 128))
     fan(C("OC", 0, 2), "land1", 2, "ar1")
     arrive("ar1", arrivals(), [C("land1", 0, 14)])
-    iota(C("TI0"), [[-32, 6], [64, 2], [1, 32]], 0, 0)
     if r + 1 < N:
         halo(r + 1, P - _halo(r + 1)[0], P, False)
     if r > 0:
@@ -349,8 +369,6 @@ def rank_program(g, core, T, topo):
     want = sum(2 * len(topo.engines(T.cores[d], core)) for d in (r - 1, r + 1) if 0 <= d < N)
     hq, hl, hr = _land(r)
     arrive("arh", want, [C(hq + x, a, b) for x in ("", "S") for a, b in ((hl, hl + hL), (hr, hr + hR)) if b > a])
-    iota(C("RM"), [[1, 32]], 0, 0)
-    iota(C("RK"), [[64, 6]], 2 * P * r, 0)
     iota(C("OI2", 0, 4), [[16, 2], [0, 2]], 0, 0)
     iota(C("OI2", 20, 22), [[0, 2]], 32, 0)
     iota(C("CTI"), [[2 * (G2 - G1) - 2, 2], [2, 16]], 2 * (G1 + ws), 0)
@@ -360,32 +378,28 @@ def rank_program(g, core, T, topo):
         iota(Q("OI2", q, 12, 20), [[sh, 2], [st, 2], [16, 2]], 96 * (q % 2) + 32 + 32 * (q // 2), 0)
 
     copy("v", C("OU"), C("OI"))
-    tr(C("ST0"), bank(0, P))
+    for c0, c1, x in upper:
+        ts(U("OU", c0, c1), U("OI", c0, c1), float(x), ALU.add)
     gather("s", C("OCB"), C("OC"), C("OU", 0, 4))
-    ts(C("TIE"), C("TI0"), TAU, ALU.mult, C("TN"), ALU.subtract)
+    tr(C("ST0"), bank(0, P))
+    for k in range(6):
+        affine(C("TIE", 64 * k, 64 * k + 64), C("TI0"), C("NTN", k, k + 1), TAU)
     tr(C("TOWN"), C("OCB"))
-    copy("s", H("V2C"), C("ST0", 0, 192, 0, 64, 32))
-    for k in range(6):
-        if k % 2:
-            ts(C("DL", 64 * k, 64 * k + 64), C("TOWN"), C("ST0", 32 * k, 32 * k + 1), ALU.subtract)
-        else:
-            scaled("s", C("NST", k, k + 1), C("ST0", 32 * k, 32 * k + 1), -1.0)
-            affine(C("DL", 64 * k, 64 * k + 64), C("TOWN"), C("NST", k, k + 1), 1.0)
     quant("AQ", 0, 512, C("AB"))
-    tt(C("CL"), C("DL"), C("TIE"), ALU.is_gt)
-
-    gather("v", C("LB", 0, 192), C("land1", 0, 20), C("OU", 4, 16))
-    gather("s", C("LB", 192, 352), C("land1", 0, 20), C("OU", 16, 26))
-    affine(C("SLT"), C("RM"), QO, 1.0)
-    affine(C("KEYC"), C("RK"), C("CK"), 1.0)
-    affine(U("V2C"), U("RK"), U("I2"), 1.0)
-    affine(C("SLT2"), C("SLT"), 64.0, 1.0)
-    affine(C("KEYN"), C("KEYC"), 0.0, -1.0)
     for k in range(6):
-        total_of("s", C("CM", CW * k + 352, CW * k + 353), C("CL", 64 * k, 64 * k + 64), C("J1", 0, 64))
-    tr(C("LT", 0, 192), C("LB", 0, 192))
-    tr(C("LT", 192, 352), C("LB", 192, 352))
+        ts(C("DL", 64 * k, 64 * k + 64), C("TOWN"), C("ST0", 32 * k, 32 * k + 1), ALU.subtract)
+    tt(C("CL"), C("DL"), C("TIE"), ALU.is_gt)
     quant("BQ", 0, 512, C("BB"))
+    copy("s", H("V2C"), C("ST0", 0, 192, 0, 64, 32))
+    affine(C("CLB"), C("ISC"), C("CLP"), 1.0)
+    affine(C("CLM"), C("ISC"), C("CLP"), -1.0)
+    affine(C("CN"), C("ISC"), float(272 + 6 * DUMP), 2.0)
+    affine(C("BL1"), C("ISC"), C("GRP"), -2.0)
+    affine(C("BL2"), C("GRP"), -2.0, 1.0)
+
+    def own_counts():
+        for k in range(6):
+            total_of("s", C("CM", CW * k + 352, CW * k + 353), C("CL", 64 * k, 64 * k + 64), C("J0", 64 * k, 64 * k + 64))
 
     def against(ks):
         for k in ks:
@@ -394,42 +408,38 @@ def rank_program(g, core, T, topo):
                 ts(C("CM", CW * k, CW * k + cut), C("LT", 0, cut), sc, ALU.is_ge)
             if cut < 352:
                 ts(C("CM", CW * k + cut, CW * k + 352), C("LT", cut, 352), sc, ALU.is_gt)
-            total_of("v" if k == 5 else "s", C("PR", k, k + 1), C("CM", CW * k, CW * k + 353), C("J1", 0, 353))
-    kids("W1", hL, P, "KH1", "KH2", 3, "ssssssss")
-    against((0, 1, 2))
+            total_of("v" if k == 5 else "s", C("PR", k, k + 1), C("CM", CW * k, CW * k + 353), C("J1", CW * k, CW * k + 353))
+    kids("W1", hL, P, "KH1", "KH2", 3, "ssssssss", own_counts)
     quant("W1", Wn + hL, Wn + hL + P, C("KH1"))
-    quant("W1", 2 * Wn + hL, 2 * Wn + hL + P, C("KH2"))
+    gather("v", C("LB", 0, 192), C("land1", 0, 20), C("OU", 4, 16))
+    gather("s", C("LB", 192, 352), C("land1", 0, 20), C("OU", 16, 26))
+    tr(C("LT", 0, 192), C("LB", 0, 192))
+    tr(C("LT", 192, 352), C("LB", 192, 352))
     mm(bank(3, P), "UQ", 0, "W1", Wn + hL, Wn + hL + P)
+    against((0, 1))
+    quant("W1", 2 * Wn + hL, 2 * Wn + hL + P, C("KH2"))
     mm(bank(4, P), "UQ", 0, "W1", 2 * Wn + hL, 2 * Wn + hL + P)
-    against((3, 4, 5))
-    tr(H("VALT"), bank(3, P, 0, 64))
-    tr(U("VALT"), bank(4, P, 64, 128))
-    quadsum("PZ", "PB", "PR", 6)
-    affine(C("TH"), IC, 64.0, -1.0)
-    affine(C("CN"), C("ISC"), float(272 + 6 * DUMP), 2.0)
-    affine(C("GR"), GR, 0.0, 1.0, ACT.Sign)
-    affine(C("CLA"), PM16, C("PID"), -1.0)
-    affine(C("GRP"), C("GR"), 2.0, -2.0)
-    affine(C("CLA"), C("CLA"), C("GRP"), 2.0)
-    affine(C("CLB"), C("ISC"), C("CLA"), 1.0)
-    affine(C("CLA"), C("ISC"), C("CLA"), -1.0)
-    affine(C("BL1"), C("ISC"), C("GRP"), -2.0)
-    affine(C("BL2"), C("GRP"), -2.0, 1.0)
+    against((2, 3, 4, 5))
+    quadsum("PZ", "PB", "PR", 6, lambda: tr(H("VALT"), bank(3, P, 0, 64)))
     for k in range(6):
         affine(C("AD", 32 * k, 32 * k + 32), C("SLT"), C("PZ", k, k + 1), -1.0, ACT.Abs)
     for k in range(6):
         affine(C("EV", 32 * k, 32 * k + 32), C("AD", 32 * k, 32 * k + 32), C("KEYC", k, k + 1), C("KEYN", k, k + 1), ACT.Relu)
-    for v in (1, 2):
+
+    def slots(v):
         for k in range(6):
             val = C("V2C", k, k + 1) if v == 1 else C("VALT", 32 * k, 32 * k + 1)
             ts(C("EV", 192 * v + 32 * k, 192 * v + 32 * k + 32), C("SLT2" if v == 1 else "SLT"), C("PZ", k, k + 1), ALU.is_equal, val, ALU.mult)
-        tr(C("ET", 192 * v, 192 * v + 192), C("EV", 192 * v, 192 * v + 192))
-        if v == 1:
-            total_of("s", H("land2", 28, 29), H("ET", 192, 384), H("J3", 0, 192))
-            total_of("s", U("land2", 30, 31), U("ET", 192, 384), U("J3", 0, 192))
-            copy("s", U("land2", 28, 29), H("land2", 28, 29))
-            copy("s", H("land2", 30, 31), U("land2", 30, 31))
+    slots(1)
+    tr(U("VALT"), bank(4, P, 64, 128))
+    tr(C("ET", 192, 384), C("EV", 192, 384))
+    slots(2)
     tr(C("ET", 0, 192), C("EV", 0, 192))
+    tr(C("ET", 384, 576), C("EV", 384, 576))
+    total_of("s", H("land2", 28, 29), H("ET", 192, 384), H("J3", 192, 384))
+    total_of("s", U("land2", 30, 31), U("ET", 192, 384), U("J3", 192, 384))
+    copy("s", U("land2", 28, 29), H("land2", 28, 29))
+    copy("s", H("land2", 30, 31), U("land2", 30, 31))
     total_of("s", C("land2", 31, 32), C("ET", 0, 192), C("J3", 0, 192))
     total_of("v", C("land2", 29, 30), C("ET", 384, 576))
     fan(C("land2", 28, 32), "land2", 4, "ar2")
@@ -452,7 +462,7 @@ def rank_program(g, core, T, topo):
     iota(C("HT", G3, G3 + Wn), [[4, Wn]], 4 * ws + 1, 0)
     ks, kn = (0, hL + hR) if hq == "HQ" else (0 if hL else Wn - 128, 128)
     kids(hq, ks, kn, "FH1", "FH2", 5, "ssvsvssv")
-    affine(C("CT", 0, 16), C("CTI", 0, 16), C("CLA"), 1.0)
+    affine(C("CT", 0, 16), C("CTI", 0, 16), C("CLM"), 1.0)
     affine(C("CT", 16, 32), C("CTI", 16, 32), C("CLB"), 1.0)
     quant("HK1", 0, kn, C("FH1", 0, 4 * kn))
     quant("HK2", 0, kn, C("FH2", 0, 4 * kn))
@@ -469,10 +479,12 @@ def rank_program(g, core, T, topo):
     quant("WQ", 0, 128, C("WB"))
 
     for k in range(2):
-        total_of("s", C("VV", k + 2, k + 3), C("land2", k + 2, 32, step=4), C("JJ"))
+        total_of("s", C("VV", k + 2, k + 3), C("land2", k + 2, 32, step=4), C("JJ", 8 * k, 8 * k + 8))
         total_of("v", C("VV", k, k + 1), C("land2", k, 32, step=4))
     gather("v", C("RBS"), C("VV"), C("OU", 26, 30))
     gather("s", C("RBK"), C("VV"), C("OU", 30, 34))
+    affine(C("TK"), C("VV", 2, 3), 0.0, TAU)
+    affine(C("KB"), C("VV", 3, 4), -BIG, 1.0)
     tr(C("SC", 0, 64), C("RBS"))
     tr(C("KY", 0, 64), C("RBK"))
     swap("SC")
@@ -482,42 +494,45 @@ def rank_program(g, core, T, topo):
     affine(C("E1"), C("SC"), C("VV", 1, 2), -1.0)
     ts(C("NK1"), C("KY"), C("VV", 3, 4), ALU.subtract, -TAU, ALU.mult)
     affine(C("E2"), C("SC", 32, 192), C("VV", 0, 1), -1.0)
+    affine(C("NK2"), C("KY", 32, 192), C("TK"), -TAU)
     tt(C("M1"), C("E1"), C("NK1"), ALU.is_lt)
-    ts(C("NK2"), C("KY", 32, 192), C("VV", 2, 3), ALU.subtract, -TAU, ALU.mult)
-    affine(C("KB"), C("VV", 3, 4), -BIG, 1.0)
-    affine(C("NB"), C("VV", 2, 3), -BIG, 1.0)
-    affine(C("NKE"), C("VV", 2, 3), C("CN"), 1.0)
-    for k in range(3):
-        affine(C("KE", k, k + 1), C("VV", 3, 4), float(272 + 2 * k * DUMP), 1.0)
-    total_of("s", C("R1"), C("M1"), C("J3", 0, 192))
     tt(C("M2"), C("E2"), C("NK2"), ALU.is_lt)
     total_of("v", C("R2"), C("M2"))
     gathered(C("GD"), C("KY"), C("OD", 4, 12), float(-ws), 0.5, ACT.Relu)
-    ts(C("FF", 1, 2), C("R1"), 64.0, ALU.is_lt, C("KB"), ALU.mult)
-    ts(C("FF", 0, 1), C("R2"), C("TH"), ALU.is_lt, C("NB"), ALU.mult)
-    gather("v", C("FB"), C("FF"), C("OU", 26, 30))
+    affine(C("NB"), C("VV", 2, 3), -BIG, 1.0)
     for f, a in ((H, 64), (U, 32)):
         affine(f("FR", 192, 224), f("KY", a, a + 32), -BIG, 1.0)
         affine(f("FR", 224, 256), f("KY", a + 96, a + 128), -BIG, 1.0)
+    total_of("s", C("R1"), C("M1"), C("J3", 0, 192))
     affine(C("GE"), C("GD"), float(Wn - 1), -1.0, ACT.Relu)
+    affine(C("Q1", 192, 256), C("FR", 192, 256), C("KB"), -1.0, ACT.Sign, C("S1A"))
+    affine(C("Q2", 192, 256), C("FR", 192, 256), C("NB"), -1.0, ACT.Sign, C("C2A"))
+    affine(C("NKA"), C("VV", 2, 3), C("CN"), 1.0)
+    affine(C("KES"), C("VV", 3, 4), C("S1A"), 1.0)
+    affine(C("NKE"), C("NKA"), C("C2A"), 1.0)
+    for k in range(3):
+        affine(C("KE", k, k + 1), C("KES"), float(272 + 2 * k * DUMP), 1.0)
+    ts(C("FB", 32, 64), C("C64"), C("R1"), ALU.is_gt, C("KB"), ALU.mult)
+    ts(C("FB", 0, 32), C("THT"), C("R2"), ALU.is_gt, C("NB"), ALU.mult)
     tr(C("FR", 0, 64), C("FB"))
+    tr(C("GT"), C("GE"))
     swap("FR")
+    for k in (0, 1):
+        ts(C("OFFG", 4 * k, 4 * k + 4), C("GT", 0, 128, step=32), -1.0, ALU.mult, float((2 + k) * Wn - 1), ALU.add)
     pairs("FR", "vsvs")
-    affine(C("FL"), C("FF", 1, 2), 0.0, -1.0, ACT.Sign)
-    affine(C("F2"), C("FF", 0, 1), 0.0, -1.0, ACT.Sign)
-    affine(C("Q1"), C("FR"), C("KB"), -1.0, ACT.Sign, C("S1"))
-    affine(C("Q2"), C("FR"), C("NB"), -1.0, ACT.Sign, C("C2"))
+    affine(C("FL"), C("FB", 32, 33), 0.0, -1.0, ACT.Sign)
+    affine(C("F2"), C("FB", 0, 1), 0.0, -1.0, ACT.Sign)
+    affine(C("Q1", 0, 192), C("FR", 0, 192), C("KB"), -1.0, ACT.Sign, C("S1"))
+    affine(C("Q2", 0, 192), C("FR", 0, 192), C("NB"), -1.0, ACT.Sign, C("C2"))
     win, off, ct = C("KY", 0, 96), C("OV"), C("CT")
     run("v", lambda: g.vector.tensor_tensor(T.VA[:, 32:64], win[0].indirect(off[0]), ct[0], ALU.subtract), [win, off, ct], [C("VA", 32, 64)])
-    tr(C("GT"), C("GE"))
     for k, x in enumerate((2 * DUMP - 1, -2 * DUMP - 1, 1 - 4 * DUMP)):
         ts(C("DB", k, k + 1), C("FL"), float(x), ALU.mult, C("KE", k, k + 1), ALU.add)
     ts(C("DBN"), C("F2"), -6.0 * DUMP - 1, ALU.mult, C("NKE"), ALU.add)
-    affine(C("VB", 32, 48), C("VA", 32, 48), C("BL1"), 1.0)
-    affine(C("VB", 48, 64), C("VA", 48, 64), C("BL2"), 1.0)
-    for k in (0, 1):
-        ts(C("OFFG", 4 * k, 4 * k + 4), C("GT", 0, 128, step=32), -1.0, ALU.mult, float((2 + k) * Wn - 1), ALU.add)
+    ts(C("VB", 32, 48), C("VA", 32, 48), C("BL1"), ALU.add)
+    ts(C("VB", 48, 64), C("VA", 48, 64), C("BL2"), ALU.add)
     ts(C("OFF", 1, 4), C("DB"), C("S1"), ALU.add, 0.5, ALU.mult)
+    pick_codes("PK", 0, 128, "W1", 3 * Wn, C("OFFG"))
     ts(C("OFF", 0, 1), C("C2"), C("DBN"), ALU.add, 0.5, ALU.mult)
 
     scatter(C("RB"), C("OFF"), C("VB"))
@@ -528,33 +543,39 @@ def rank_program(g, core, T, topo):
     affine(C("SGN"), C("C2"), C("BN"), -1.0, ACT.Sign)
     affine(C("SB1"), C("DB", 2, 3), C("EB"), -1.0, ACT.Sign)
     affine(C("AN"), C("SGN"), C("A12"), 1.0)
+    pick_scales("PK", 0, 128, "W1", 3 * Wn, C("OFFG"))
     scaled("s", C("RB", e0 - 1, e0), C("RB", e0 - 1, e0), 0.0)
     affine(C("XS", 224, 256), C("SEC"), C("SB1"), C("AN"))
-    pick("PK", "W1", 3 * Wn, C("OFFG"))
     xa, xb, x0, xo = C("RA", e0, e0 + 224), C("RB", e0 - 1, e0 + 223), C("INI"), C("XS", 0, 224)
     run("v", lambda: g.vector.tensor_tensor_scan(xo[0], xa[0], xb[0], x0[0], ALU.add, ALU.subtract), [xa, xb, x0], [xo])
     tr(C("XT"), C("XS"))
     gathered(C("HT", G1, G1 + 128), C("KY"), C("OD", 12, 20), 0.0, 2.0, ACT.Identity)
-    total_of("s", C("ZS", 7, 8), C("XT", 224, 256), C("J3", 0, 32))
+    total_of("s", C("ZS", 7, 8), C("XT", 224, 256), C("J3", 192, 224))
     tt(C("ZS", 0, 7), C("XT", 0, 224, step=32), C("XT", 16, 224, step=32), ALU.add)
     kids("PK", 0, 128, "GH1", "GH2", 5, "ssssssss")
     quadsum("ZT", "HS", "ZS", 8)
     tr(C("XR"), C("ZT"))
+    quant("W2", G1, G1 + 128, C("GH1"))
     gather("v", C("YY"), C("XR"), C("OD", 0, 4))
     tr(C("YT"), C("YY"))
+    quant("W2", G2, G2 + 128, C("GH2"))
     for h in (0, 1):
         ts(part_of("OFFL", h, 14, 2), C("YT", 32 * h, 32 * h + 7), C("ZT", 7, 8), ALU.add, -0.5, ALU.mult)
-    quant("W2", G1, G1 + 128, C("GH1"))
-    quant("W2", G2, G2 + 128, C("GH2"))
-    pick("FQ", "W2", G3 + Wn, C("OFFL", 0, 13))
-    mm(bank(0, E), "WQ", 0, "FQ", 0, E)
-    dma("y", ext(T.oc[:, :]), C("FQ"), bits=2)
     affine(C("HT", G2, G2 + 128), C("HT", G1, G1 + 128), 1.0, 1.0)
+    for c0, c1 in ((0, 128), (128, E)):
+        off = C("OFFL", c0 // 16, c1 // 16)
+        pick_codes("FQ", c0, c1, "W2", G3 + Wn, off)
+        pick_scales("FQ", c0, c1, "W2", G3 + Wn, off)
+    mm(bank(0, 128), "WQ", 0, "FQ", 0, 128)
+    mm(bank(1, 128), "WQ", 0, "FQ", E - 128, E)
+    dma("y", ext(T.oc[:, :]), C("FQ"), bits=2)
     gather("s", C("HR"), C("HT", 0, G3 + Wn), C("OFFL", 0, 13))
     for k in range(4):
         dma("yyss"[k], ext(T.osc[4 * k:4 * k + 4, :]), C("FQS", 0, E, 32 * k, 32 * k + 4))
-    copy("v", C("YS"), bank(0, E))
-    dma("y", ext(T.y[:, :]), C("YS"))
+    copy("v", C("YS", 0, 128), bank(0, 128))
+    dma("y", ext(T.y[:, 0:128]), C("YS", 0, 128))
+    copy("v", C("YS", 128, E), bank(1, 128, 0, 128, 256 - E))
+    dma("y", ext(T.y[:, 128:E]), C("YS", 128, E))
     dma("s", ext(T.hs[:, :]), C("HR", 0, E, 0, 1))
 
     total["loc"] = loc[0]

@@ -9,10 +9,12 @@ TAU = 2.0 ** -106
 BIG = 65536.0
 DUMP = 1720
 ROW = 8 + 4 * DUMP
-CW = 360
+CW = 416
+HW = CW // 2
+NV = 4
 
 SMALL = {}
-for _n, _w in dict(PR=6, PB=6, PZ=6, RK=6, KEYC=6, KEYN=6, V2C=6, VV=4, R1=1, R2=1, FL=1, F2=1, TH=1, KB=1, NB=1, TK=1,
+for _n, _w in dict(PB=6, PZ=6, LO=2, HI=2, QOB=1, NST=2, RK=6, KEYC=6, KEYN=6, V2C=6, VV=4, FL=1, F2=1, TH=1, KB=1, NB=1, TK=1,
                    PID=1, BITS=4, SG=1, ISC=1, CK=1, I2=1, NT=1, NTB=1, NTN=6, S1A=1, C2A=1, KES=1, KE=3, DB=3, DBN=1, NKA=1, NKE=1,
                    CN=1, BN=1, EB=1, S1=1, C2=1, A12=1, SB1=1, SGN=1, AN=1, INI=1, CLA=1, CLP=1, CLM=1, CLB=1, BL1=1, BL2=1, GRP=1,
                    GR=1, ZS=8, HS=8, JJ=16, JK=8).items():
@@ -27,17 +29,17 @@ def _scratch():
         for name, n in kw.items():
             d[name] = ("sbuf", [128, n], dtype)
     sb(h, XB=4 * P, U4=4, UB=512, AB=2048, BB=2048, WB=512, KH1=4 * P, KH2=4 * P, FH1=576, FH2=576,
-       GH1=512, GH2=512, CL=384, J0=384, J1=6 * CW, M1=192, M2=160, Z0=128)
+       GH1=512, GH2=512, CM=6 * CW, SCN=6 * HW, J1=2 * CW, M1=192, M2=160, Z0=128)
     for name, n in dict(UQ=128, AQ=512, BQ=512, WQ=128, W1=3 * WMAX, HQ=144, HK1=144, HK2=144, PK=128, W2=4 * WMAX + 256, FQ=E).items():
         d[name] = ("sbuf", [128, n], q)
         d[name + "S"] = ("sbuf", [128, n], s)
-    sb(f, CM=6 * CW, C64=32, THT=32, OC=8, OCB=64, TOWN=64, ST0=192, DL=384, TI0=64, TIE=384, land1=24, LB=352, LT=352,
-       SLT=32, SLT2=32, VALT=192, AD=192, EV=576, ET=576, land2=32, RBS=64, RBK=64, SC=192, KY=192, E1=192, E2=160, NK1=192,
-       NK2=160, FB=64, FR=256, Q1=256, Q2=256, VA=64, VB=64, CTI=32, CT=32, SEC=32, RA=ROW, RB=ROW, XS=256, XT=256, ZT=32, XR=32,
-       YY=64, YT=64, HT=4 * WMAX + 256, HR=E, GD=128, GE=128, GT=128, YS=E, J3=576, OI2=22,
+    sb(f, BLT=32, C64=32, THT=32, OC=8, OCB=64, TOWN=64, ST0=192, DL=384, TI0=64, TIE=384, land1=24, LB=352, LT=352,
+       SLT=32, SLT2=32, VALT=192, AD=192, EV=576, ET=576, land2=412, RBS=64, RBK=64, SC=192, KY=192, E1=192, E2=160, NK1=192,
+       NK2=160, R1=96, R2=80, FB=64, FR=256, Q1=256, Q2=256, VA=64, VB=64, CTI=32, CT=32, SEC=32, RA=ROW, RB=ROW, XS=256, XT=256,
+       ZT=32, XR=32, YY=64, YT=64, HT=4 * WMAX + 256, HR=E, GD=128, GE=128, GT=128, YS=E, J3=416, OI2=22,
        SM=8 * sum((w + 7) // 8 for _, w in SMALL.values()))
-    sb("int32", OI=34, PIN=1, PA=4)
-    sb("uint16", OU=34, OD=20, OV=2, OFF=4, OFFG=8, OFFL=14)
+    sb("int32", OI=26, PIN=1, PA=4)
+    sb("uint16", OU=26, OD=20, OV=2, OFF=4, OFFG=8, OFFL=14)
     d["PS"] = ("psum", [128, 4096], f)
     return d
 
@@ -182,6 +184,9 @@ def rank_program(g, core, T, topo):
         else:
             run("s", lambda: g.scalar.activation(junk[0], i[0], ACT.Copy, accum_out=o[0]), [i], [o, junk])
 
+    def pairsum(o, a, b, start=0.0):
+        run("v", lambda: g.vector.tensor_tensor_scan(o[0], a[0], b[0], start, ALU.add, ALU.add), [a, b], [o])
+
     def affine(o, i, bias, scale, func=ACT.Identity, acc=None):
         rd = [i] + [x for x in (bias, scale) if isinstance(x, tuple)]
         b = bias[0] if isinstance(bias, tuple) else bias
@@ -227,8 +232,8 @@ def rank_program(g, core, T, topo):
     def pick_scales(o, c0, c1, src, n, off):
         gather("s", C(o + "S", c0, c1), C(src + "S", 0, n), off)
 
-    def quadsum(o, h, i, n, between=None):
-        tt(H(h, 0, n), H(i, 0, n), U(i, 0, n), ALU.add)
+    def quadsum(o, h, lo, up, n, between=None):
+        tt(H(h, 0, n), lo, up, ALU.add)
         if between:
             between()
         for q in range(4):
@@ -242,24 +247,26 @@ def rank_program(g, core, T, topo):
         for q in range(4):
             copy(order[q], Q(name, q, 96, 192), Q(name, q ^ 1, 0, 96))
 
-    def kids(src, c0, n, t1, t2, first, pat, halfway=None):
+    def kids(src, c0, n, t1, t2, first, pat, late=None):
         for i in range(8):
-            if i == 4 and halfway:
-                halfway()
             k = (first + i) % 8
             mm(bank(k, n), "AQ" if i < 4 else "BQ", 128 * (i % 4), src, c0, c0 + n)
+            if i == 7 and late:
+                late()
             scaled(pat[i], part_of(t1 if i < 4 else t2, i % 4, 4 * n, 4), bank(k, n), 0.0625)
+
+    def ways(a):
+        return topo.engines(a, [c for c in T.cores if topo.chip(c) != topo.chip(a)][0])
 
     def split(a, b):
         if topo.chip(a) != topo.chip(b):
             return topo.engines(a, b)
-        off = topo.engines(a, [c for c in T.cores if topo.chip(c) != topo.chip(a)][0])
-        return [e for e in topo.engines(a, b) if e not in off][:2]
+        return [e for e in topo.engines(a, b) if e not in ways(a)][:2]
 
     def arrivals():
         return sum(len(split(c, core)) for c in T.cores if c != core)
 
-    def fan(src, dst, width, arr):
+    def fan(src, dst, base, width, arr):
         deps("g", [src], [])
         others = [c for c in T.cores if c != core]
         far = [c for c in others if topo.chip(c) != topo.chip(core)]
@@ -270,7 +277,7 @@ def rank_program(g, core, T, topo):
             ids, aps = [], []
             for c in dsts:
                 d = T.rank_of(c)
-                k = width * (r if r < d else r - 1)
+                k = base + width * (r if r < d else r - 1)
                 rid, pid, _ = topo.addr(c)
                 ids.append(DstId(rid=rid, pnc=pid))
                 aps.append(T[dst][:, k:k + width])
@@ -278,19 +285,18 @@ def rank_program(g, core, T, topo):
         g.remote_dma_fused([tf(far, fe), tf(near, ne)], local_sem=T.sem.loc)
         loc[0] += len(fe) + len(ne)
 
-    def halo(d, c0, c1, behind):
+    def halo(d, sfx):
         c = T.cores[d]
         dst, a, b = _land(d)
-        at = b if behind else a
+        c0, c1, at = (P - _halo(d)[0], P, a) if d > r else (0, _halo(d)[1], b)
         rid, pid, _ = topo.addr(c)
-        for sfx in ("", "S"):
-            s = C("W1" + sfx, hL + c0, hL + c1)
-            deps("g", [s], [])
-            o, i = T[dst + sfx][:, at:at + c1 - c0], s[0]
-            if not sfx:
-                o, i = o.bitcast(dt.uint8), i.bitcast(dt.uint8)
-            g.remote_dma(o, i, T.sem.arh, T.sem.loc, pid, rid, topo.mask(core, c))
-            loc[0] += len(topo.engines(core, c))
+        s = C("W1" + sfx, hL + c0, hL + c1)
+        deps("g", [s], [])
+        o, i = T[dst + sfx][:, at:at + c1 - c0], s[0]
+        if not sfx:
+            o, i = o.bitcast(dt.uint8), i.bitcast(dt.uint8)
+        g.remote_dma(o, i, T.sem.arh, T.sem.loc, pid, rid, sum(1 << e for e in ways(core)))
+        loc[0] += len(ways(core))
 
     def arrive(sem, val, writes):
         for _, name, p0, p1, c0, c1 in writes:
@@ -320,7 +326,6 @@ def rank_program(g, core, T, topo):
             if n % 2:
                 upper.append((at + n - 1, at + n + 1, 16 - (2 * s0 + 1 + 4 * (m - 1))))
             at += 2 * m
-    iota(C("OI", 26, 34), [[1, 4], [0, 2]], 0, 0, True)
     cut = 32 * (nb + (nb + 1) // 2)
     memset(C("Z0"), 0.0)
     memset(C("OC"), -9e29)
@@ -335,15 +340,16 @@ def rank_program(g, core, T, topo):
     affine(C("I2"), IC, 0.0, 2.0)
     affine(C("TH"), IC, 64.0, -1.0)
     affine(C("GR"), GR, 0.0, 1.0, ACT.Sign)
-    affine(C("SLT"), C("TI0", 0, 32), QO, 1.0)
+    affine(C("QOB"), QO, float(-4 * HW), 1.0)
     affine(C("ISC"), C("SG"), 0.0, 1.0, ACT.Relu)
     affine(C("NT"), C("PID"), C("I2"), -1.0)
     affine(C("CLA"), PM16, C("PID"), -1.0)
     affine(C("GRP"), C("GR"), 2.0, -2.0)
-    affine(C("SLT2"), C("SLT"), 64.0, 1.0)
+    affine(C("SLT"), C("TI0", 0, 32), C("QOB"), 1.0)
     affine(C("CK"), C("I2"), C("ISC"), 1.0)
     affine(C("NTB"), C("NT"), P * r * TAU, -TAU)
     affine(C("THT"), C("TI0", 0, 32), C("TH"), 0.0)
+    affine(C("SLT2"), C("SLT"), 64.0, 1.0)
     affine(C("NTN"), C("RK"), C("NTB"), -0.5 * TAU)
     affine(C("KEYC"), C("RK"), C("CK"), 1.0)
     affine(U("V2C"), U("RK"), U("I2"), 1.0)
@@ -354,19 +360,19 @@ def rank_program(g, core, T, topo):
         ts(part_of("UB", t, 512, 4), C("Z0"), C("U4", t, t + 1), ALU.add)
     quant("UQ", 0, 128, C("UB"))
     quant("W1", hL, hL + P, C("XB"))
+    pieces = [(d, sfx) for sfx in ("S", "") for d in (r - 1, r + 1) if 0 <= d < N]
+    halo(*pieces[0])
     mm(bank(1, 128), "W1", hL, "UQ", 0, 128)
     mm(bank(2, 128), "W1", hL + 64, "UQ", 0, 128)
     mm(bank(0, P), "UQ", 0, "W1", hL, hL + P)
     copy("v", C("OC", 0, 1), bank(1, 1))
     copy("v", U("OC", 1, 2), bank(2, 1, 64, 128))
     copy("v", H("OC", 1, 2), bank(2, 1, 64, 128))
-    fan(C("OC", 0, 2), "land1", 2, "ar1")
+    fan(C("OC", 0, 2), "land1", 0, 2, "ar1")
     arrive("ar1", arrivals(), [C("land1", 0, 14)])
-    if r + 1 < N:
-        halo(r + 1, P - _halo(r + 1)[0], P, False)
-    if r > 0:
-        halo(r - 1, 0, _halo(r - 1)[1], True)
-    want = sum(2 * len(topo.engines(T.cores[d], core)) for d in (r - 1, r + 1) if 0 <= d < N)
+    for piece in pieces[1:]:
+        halo(*piece)
+    want = sum(2 * len(ways(T.cores[d])) for d in (r - 1, r + 1) if 0 <= d < N)
     hq, hl, hr = _land(r)
     arrive("arh", want, [C(hq + x, a, b) for x in ("", "S") for a, b in ((hl, hl + hL), (hr, hr + hR)) if b > a])
     iota(C("OI2", 0, 4), [[16, 2], [0, 2]], 0, 0)
@@ -388,7 +394,8 @@ def rank_program(g, core, T, topo):
     quant("AQ", 0, 512, C("AB"))
     for k in range(6):
         ts(C("DL", 64 * k, 64 * k + 64), C("TOWN"), C("ST0", 32 * k, 32 * k + 1), ALU.subtract)
-    tt(C("CL"), C("DL"), C("TIE"), ALU.is_gt)
+    for k in range(6):
+        tt(C("CM", CW * k + 352, CW * k + CW), C("DL", 64 * k, 64 * k + 64), C("TIE", 64 * k, 64 * k + 64), ALU.is_gt)
     quant("BQ", 0, 512, C("BB"))
     copy("s", H("V2C"), C("ST0", 0, 192, 0, 64, 32))
     affine(C("CLB"), C("ISC"), C("CLP"), 1.0)
@@ -396,31 +403,56 @@ def rank_program(g, core, T, topo):
     affine(C("CN"), C("ISC"), float(272 + 6 * DUMP), 2.0)
     affine(C("BL1"), C("ISC"), C("GRP"), -2.0)
     affine(C("BL2"), C("GRP"), -2.0, 1.0)
+    for k in range(NV, 6):
+        scaled("s", C("NST", k - NV, k - NV + 1), C("ST0", 32 * k, 32 * k + 1), -1.0)
+    affine(C("BLT", 0, 16), C("TI0", 0, 16), C("BL1"), 0.0)
+    affine(C("BLT", 16, 32), C("TI0", 0, 16), C("BL2"), 0.0)
 
-    def own_counts():
-        for k in range(6):
-            total_of("s", C("CM", CW * k + 352, CW * k + 353), C("CL", 64 * k, 64 * k + 64), C("J0", 64 * k, 64 * k + 64))
+    def last(k):
+        return C("SCN", HW * k + HW - 1, HW * k + HW)
 
-    def against(ks):
-        for k in ks:
-            sc = C("ST0", 32 * k, 32 * k + 1)
-            if cut > 0:
-                ts(C("CM", CW * k, CW * k + cut), C("LT", 0, cut), sc, ALU.is_ge)
-            if cut < 352:
-                ts(C("CM", CW * k + cut, CW * k + 352), C("LT", cut, 352), sc, ALU.is_gt)
-            total_of("v" if k == 5 else "s", C("PR", k, k + 1), C("CM", CW * k, CW * k + 353), C("J1", CW * k, CW * k + 353))
-    kids("W1", hL, P, "KH1", "KH2", 3, "ssssssss", own_counts)
+    def tally(k):
+        pairsum(C("SCN", HW * k, HW * k + HW), C("CM", CW * k, CW * k + HW), C("CM", CW * k + HW, CW * k + CW), float(-HW))
+
+    def against(k):
+        sc = C("ST0", 32 * k, 32 * k + 1)
+        if cut > 0:
+            ts(C("CM", CW * k, CW * k + cut), C("LT", 0, cut), sc, ALU.is_ge)
+        if cut < 352:
+            ts(C("CM", CW * k + cut, CW * k + 352), C("LT", cut, 352), sc, ALU.is_gt)
+
+    def signs(k):
+        c, i, j = CW * k, k - NV, CW * (k - NV)
+        affine(C("CM", c, c + 352), C("LT"), C("NST", i, i + 1), 1.0, ACT.Sign)
+        if cut > 0:
+            affine(C("J1", j, j + cut), C("CM", c, c + cut), 0.0, -1.0, ACT.Relu, C("LO", i, i + 1))
+        affine(C("J1", j + cut, j + CW), C("CM", c + cut, c + CW), 0.0, 1.0, ACT.Relu, C("HI", i, i + 1))
+
+    kids("W1", hL, P, "KH1", "KH2", 3, "ssssssss", lambda: gather("s", C("LB", 192, 352), C("land1", 0, 20), C("OU", 16, 26)))
     quant("W1", Wn + hL, Wn + hL + P, C("KH1"))
     gather("v", C("LB", 0, 192), C("land1", 0, 20), C("OU", 4, 16))
-    gather("s", C("LB", 192, 352), C("land1", 0, 20), C("OU", 16, 26))
     tr(C("LT", 0, 192), C("LB", 0, 192))
     tr(C("LT", 192, 352), C("LB", 192, 352))
     mm(bank(3, P), "UQ", 0, "W1", Wn + hL, Wn + hL + P)
-    against((0, 1))
+    signs(4)
+    signs(5)
+    against(0)
+    against(1)
+    tally(0)
     quant("W1", 2 * Wn + hL, 2 * Wn + hL + P, C("KH2"))
     mm(bank(4, P), "UQ", 0, "W1", 2 * Wn + hL, 2 * Wn + hL + P)
-    against((2, 3, 4, 5))
-    quadsum("PZ", "PB", "PR", 6, lambda: tr(H("VALT"), bank(3, P, 0, 64)))
+    against(2)
+    tally(1)
+    against(3)
+    tally(2)
+    tally(3)
+    for k in range(NV, 6):
+        i = k - NV
+        if cut > 0:
+            ts(last(k), C("HI", i, i + 1), C("LO", i, i + 1), ALU.subtract, float(cut - HW), ALU.add)
+        else:
+            ts(last(k), C("HI", i, i + 1), float(-HW), ALU.add)
+    quadsum("PZ", "PB", C("SCN", HW - 1, None, 0, 64, HW), C("SCN", HW - 1, None, 64, 128, HW), 6, lambda: tr(H("VALT"), bank(3, P, 0, 64)))
     for k in range(6):
         affine(C("AD", 32 * k, 32 * k + 32), C("SLT"), C("PZ", k, k + 1), -1.0, ACT.Abs)
     for k in range(6):
@@ -436,14 +468,14 @@ def rank_program(g, core, T, topo):
     slots(2)
     tr(C("ET", 0, 192), C("EV", 0, 192))
     tr(C("ET", 384, 576), C("EV", 384, 576))
-    total_of("s", H("land2", 28, 29), H("ET", 192, 384), H("J3", 192, 384))
-    total_of("s", U("land2", 30, 31), U("ET", 192, 384), U("J3", 192, 384))
-    copy("s", U("land2", 28, 29), H("land2", 28, 29))
-    copy("s", H("land2", 30, 31), U("land2", 30, 31))
-    total_of("s", C("land2", 31, 32), C("ET", 0, 192), C("J3", 0, 192))
-    total_of("v", C("land2", 29, 30), C("ET", 384, 576))
-    fan(C("land2", 28, 32), "land2", 4, "ar2")
-    arrive("ar2", arrivals(), [C("land2", 0, 28)])
+    total_of("s", H("land2", 380, 381), H("ET", 192, 384), H("J3", 192, 384))
+    total_of("s", U("land2", 382, 383), U("ET", 192, 384), U("J3", 192, 384))
+    copy("s", U("land2", 380, 381), H("land2", 380, 381))
+    copy("s", H("land2", 382, 383), U("land2", 382, 383))
+    for v, at in ((0, 3), (2, 1)):
+        pairsum((T.land2[:, at:384:4], "land2", 0, 128, 380 + at, 381 + at), C("ET", 192 * v, 192 * v + 96), C("ET", 192 * v + 96, 192 * v + 192))
+    fan(C("land2", 380, 384), "land2", 384, 4, "ar2")
+    arrive("ar2", arrivals(), [C("land2", 384, 412)])
 
     iota(C("RA", e0 - 8, e0 + 232), [[0, 240]], 0, 0)
     iota(C("RB", e0 - 8, e0 + 232), [[0, 240]], 0, 0)
@@ -479,12 +511,14 @@ def rank_program(g, core, T, topo):
     quant("WQ", 0, 128, C("WB"))
 
     for k in range(2):
-        total_of("s", C("VV", k + 2, k + 3), C("land2", k + 2, 32, step=4), C("JJ", 8 * k, 8 * k + 8))
-        total_of("v", C("VV", k, k + 1), C("land2", k, 32, step=4))
-    gather("v", C("RBS"), C("VV"), C("OU", 26, 30))
-    gather("s", C("RBK"), C("VV"), C("OU", 30, 34))
+        total_of("s", C("VV", k + 2, k + 3), C("land2", 382 + k, 412, step=4), C("JJ", 8 * k, 8 * k + 8))
+        total_of("v", C("VV", k, k + 1), C("land2", 380 + k, 412, step=4))
+    for k in range(2):
+        ts(C("RBS", 32 * k, 32 * k + 32), C("C64"), 0.0, ALU.mult, C("VV", k, k + 1), ALU.add)
+        affine(C("RBK", 32 * k, 32 * k + 32), C("C64"), C("VV", k + 2, k + 3), 0.0)
     affine(C("TK"), C("VV", 2, 3), 0.0, TAU)
     affine(C("KB"), C("VV", 3, 4), -BIG, 1.0)
+    affine(C("NB"), C("VV", 2, 3), -BIG, 1.0)
     tr(C("SC", 0, 64), C("RBS"))
     tr(C("KY", 0, 64), C("RBK"))
     swap("SC")
@@ -497,31 +531,31 @@ def rank_program(g, core, T, topo):
     affine(C("NK2"), C("KY", 32, 192), C("TK"), -TAU)
     tt(C("M1"), C("E1"), C("NK1"), ALU.is_lt)
     tt(C("M2"), C("E2"), C("NK2"), ALU.is_lt)
-    total_of("v", C("R2"), C("M2"))
+    pairsum(C("R1"), C("M1", 0, 96), C("M1", 96, 192))
+    pairsum(C("R2"), C("M2", 0, 80), C("M2", 80, 160))
+    R1, R2 = C("R1", 95, 96), C("R2", 79, 80)
     gathered(C("GD"), C("KY"), C("OD", 4, 12), float(-ws), 0.5, ACT.Relu)
-    affine(C("NB"), C("VV", 2, 3), -BIG, 1.0)
     for f, a in ((H, 64), (U, 32)):
         affine(f("FR", 192, 224), f("KY", a, a + 32), -BIG, 1.0)
         affine(f("FR", 224, 256), f("KY", a + 96, a + 128), -BIG, 1.0)
-    total_of("s", C("R1"), C("M1"), C("J3", 0, 192))
     affine(C("GE"), C("GD"), float(Wn - 1), -1.0, ACT.Relu)
+    affine(C("NKA"), C("VV", 2, 3), C("CN"), 1.0)
     affine(C("Q1", 192, 256), C("FR", 192, 256), C("KB"), -1.0, ACT.Sign, C("S1A"))
     affine(C("Q2", 192, 256), C("FR", 192, 256), C("NB"), -1.0, ACT.Sign, C("C2A"))
-    affine(C("NKA"), C("VV", 2, 3), C("CN"), 1.0)
     affine(C("KES"), C("VV", 3, 4), C("S1A"), 1.0)
     affine(C("NKE"), C("NKA"), C("C2A"), 1.0)
     for k in range(3):
         affine(C("KE", k, k + 1), C("KES"), float(272 + 2 * k * DUMP), 1.0)
-    ts(C("FB", 32, 64), C("C64"), C("R1"), ALU.is_gt, C("KB"), ALU.mult)
-    ts(C("FB", 0, 32), C("THT"), C("R2"), ALU.is_gt, C("NB"), ALU.mult)
+    ts(C("FB", 32, 64), C("C64"), R1, ALU.is_gt, C("KB"), ALU.mult)
+    ts(C("FB", 0, 32), C("THT"), R2, ALU.is_gt, C("NB"), ALU.mult)
+    ts(C("FL"), C("C64", 0, 1), R1, ALU.is_gt)
+    ts(C("F2"), C("THT", 0, 1), R2, ALU.is_gt)
     tr(C("FR", 0, 64), C("FB"))
     tr(C("GT"), C("GE"))
     swap("FR")
     for k in (0, 1):
         ts(C("OFFG", 4 * k, 4 * k + 4), C("GT", 0, 128, step=32), -1.0, ALU.mult, float((2 + k) * Wn - 1), ALU.add)
     pairs("FR", "vsvs")
-    affine(C("FL"), C("FB", 32, 33), 0.0, -1.0, ACT.Sign)
-    affine(C("F2"), C("FB", 0, 1), 0.0, -1.0, ACT.Sign)
     affine(C("Q1", 0, 192), C("FR", 0, 192), C("KB"), -1.0, ACT.Sign, C("S1"))
     affine(C("Q2", 0, 192), C("FR", 0, 192), C("NB"), -1.0, ACT.Sign, C("C2"))
     win, off, ct = C("KY", 0, 96), C("OV"), C("CT")
@@ -529,10 +563,9 @@ def rank_program(g, core, T, topo):
     for k, x in enumerate((2 * DUMP - 1, -2 * DUMP - 1, 1 - 4 * DUMP)):
         ts(C("DB", k, k + 1), C("FL"), float(x), ALU.mult, C("KE", k, k + 1), ALU.add)
     ts(C("DBN"), C("F2"), -6.0 * DUMP - 1, ALU.mult, C("NKE"), ALU.add)
-    ts(C("VB", 32, 48), C("VA", 32, 48), C("BL1"), ALU.add)
-    ts(C("VB", 48, 64), C("VA", 48, 64), C("BL2"), ALU.add)
-    ts(C("OFF", 1, 4), C("DB"), C("S1"), ALU.add, 0.5, ALU.mult)
+    tt(C("VB", 32, 64), C("VA", 32, 64), C("BLT"), ALU.add)
     pick_codes("PK", 0, 128, "W1", 3 * Wn, C("OFFG"))
+    ts(C("OFF", 1, 4), C("DB"), C("S1"), ALU.add, 0.5, ALU.mult)
     ts(C("OFF", 0, 1), C("C2"), C("DBN"), ALU.add, 0.5, ALU.mult)
 
     scatter(C("RB"), C("OFF"), C("VB"))
@@ -550,10 +583,10 @@ def rank_program(g, core, T, topo):
     run("v", lambda: g.vector.tensor_tensor_scan(xo[0], xa[0], xb[0], x0[0], ALU.add, ALU.subtract), [xa, xb, x0], [xo])
     tr(C("XT"), C("XS"))
     gathered(C("HT", G1, G1 + 128), C("KY"), C("OD", 12, 20), 0.0, 2.0, ACT.Identity)
-    total_of("s", C("ZS", 7, 8), C("XT", 224, 256), C("J3", 192, 224))
+    total_of("s", C("ZS", 7, 8), C("XT", 224, 256), C("J3", 0, 32))
     tt(C("ZS", 0, 7), C("XT", 0, 224, step=32), C("XT", 16, 224, step=32), ALU.add)
     kids("PK", 0, 128, "GH1", "GH2", 5, "ssssssss")
-    quadsum("ZT", "HS", "ZS", 8)
+    quadsum("ZT", "HS", H("ZS"), U("ZS"), 8)
     tr(C("XR"), C("ZT"))
     quant("W2", G1, G1 + 128, C("GH1"))
     gather("v", C("YY"), C("XR"), C("OD", 0, 4))

from concourse.bass import DstId, RemoteDMATransfer
from concourse.mybir import dt, AluOpType, AxisListType, ActivationFunctionType

ALU = AluOpType
ACT = ActivationFunctionType
N, P, K, E = 8, 192, 64, 208
WMAX = 336
TAU = 2.0 ** -106
BIG = 65536.0
DUMP = 1720
ROW = 8 + 4 * DUMP
CW = 416
HW = CW // 2
NV = 4

SMALL = {}
for _n, _w in dict(PB=6, PZ=6, LO=2, HI=2, QOB=1, NST=2, RK=6, KEYC=6, KEYN=6, V2C=6, VV=4, FL=1, F2=1, TH=1, KB=1, NB=1, TK=1,
                   PID=1, BITS=4, SG=1, ISC=1, CK=1, I2=1, NT=1, NTB=1, NTN=6, S1A=1, C2A=1, KES=1, KE=3, DB=3, DBN=1, NKA=1, NKE=1,
                   CN=1, BN=1, EB=1, S1=1, C2=1, A12=1, SB1=1, SGN=1, AN=1, INI=1, CLA=1, CLP=1, CLM=1, CLB=1, BL1=1, BL2=1, GRP=1,
                   GR=1, ZS=8, HS=8, JJ=16, JK=8).items():
    SMALL[_n] = (8 * sum((w + 7) // 8 for _, w in SMALL.values()), _w)


def _scratch():
    f, h, q, s = "float32", "bfloat16", "float8_e4m3fn_x4", "uint8"
    d = {}

    def sb(dtype, **kw):
        for name, n in kw.items():
            d[name] = ("sbuf", [128, n], dtype)
    sb(h, XB=4 * P, U4=4, UB=512, AB=2048, BB=2048, WB=512, KH1=4 * P, KH2=4 * P, FH1=576, FH2=576,
       GH1=512, GH2=512, CM=6 * CW, SCN=6 * HW, J1=2 * CW, M1=192, M2=160, Z0=128)
    for name, n in dict(UQ=128, AQ=512, BQ=512, WQ=128, W1=3 * WMAX, HQ=144, HK1=144, HK2=144, PK=128, W2=4 * WMAX + 256, FQ=E).items():
        d[name] = ("sbuf", [128, n], q)
        d[name + "S"] = ("sbuf", [128, n], s)
    sb(f, BLT=32, C64=32, THT=32, OC=8, OCB=64, TOWN=64, ST0=192, DL=384, TI0=64, TIE=384, land1=24, LB=352, LT=352,
       SLT=32, SLT2=32, VALT=192, AD=192, EV=576, ET=576, land2=412, RBS=64, RBK=64, SC=192, KY=192, E1=192, E2=160, NK1=192,
       NK2=160, R1=96, R2=80, FB=64, FR=256, Q1=256, Q2=256, VA=64, VB=64, CTI=32, CT=32, SEC=32, RA=ROW, RB=ROW, XS=256, XT=256,
       ZT=32, XR=32, YY=64, YT=64, HT=4 * WMAX + 256, HR=E, GD=128, GE=128, GT=128, YS=E, J3=416, OI2=22,
       SM=8 * sum((w + 7) // 8 for _, w in SMALL.values()))
    sb("int32", OI=26, PIN=1, PA=4)
    sb("uint16", OU=26, OD=20, OV=2, OFF=4, OFFG=8, OFFL=14)
    d["PS"] = ("psum", [128, 4096], f)
    return d


SCRATCH = _scratch()
SEMAPHORES = ["cv", "cs", "ct", "cg", "loc", "ar1", "ar2", "arh"] + ["d%d" % i for i in range(40)]


def _halo(r):
    return (0 if r == 0 else 128 - 16 * r), (0 if r == N - 1 else 16 + 16 * r)


def _land(r):
    hL, hR = _halo(r)
    return ("HQ", 0, hL) if hL and hR else ("W1", 0, hL + P)


def rank_program(g, core, T, topo):
    r = T.rank_of(core)
    if r is None:
        return
    hL, hR = _halo(r)
    Wn = hL + P + hR
    ws = P * r - hL
    G1, G2, G3 = 3 * Wn, 3 * Wn + 128, 3 * Wn + 256
    e0 = E * r + 8
    q_of = {"v": g.vector, "s": g.scalar, "t": g.tensor, "g": g, "y": g.sync}
    cnt = {"cv": 0, "cs": 0, "ct": 0, "cg": 0}
    known = {k: {} for k in q_of}
    recs = {}
    total = {}
    ndma, loc = [0], [0]

    def C(name, c0=0, c1=None, p0=0, p1=128, step=1):
        if name in SMALL:
            o, w = SMALL[name]
            c0, c1, name = o + c0, o + (w if c1 is None else c1), "SM"
        elif c1 is None:
            c1 = SCRATCH[name][1][-1]
        ap = T[name][p0:p1, c0:c1] if step == 1 else T[name][p0:p1, c0:c1:step]
        return (ap, name, p0, p1, c0, c1)

    def H(name, c0=0, c1=None):
        return C(name, c0, c1, 0, 64)

    def U(name, c0=0, c1=None):
        return C(name, c0, c1, 64, 128)

    def Q(name, q, c0=0, c1=None):
        return C(name, c0, c1, 32 * q, 32 * q + 32)

    def part_of(name, i, n, step):
        w = n // step
        return (T[name][:, i:n:step], name, 0, 128, i * w, i * w + w)

    def bank(k, n, p0=0, p1=128, c0=0):
        return (T.PS[p0:p1, 512 * k + c0:512 * k + n], "PS", 0, 128, 512 * k, 512 * k + 512)

    def ext(ap):
        return (ap, None, 0, 0, 0, 0)

    def need(q, sem, val, snap):
        if known[q].get(sem, 0) >= val:
            return
        q_of[q].wait_ge(T.sem[sem], val)
        for k, x in list(snap.items()) + [(sem, val)]:
            known[q][k] = max(known[q].get(k, 0), x)

    def deps(q, reads, writes):
        todo = {}
        for view, wr in [(x, False) for x in reads] + [(x, True) for x in writes]:
            _, name, p0, p1, c0, c1 = view
            for (a0, a1, b0, b1, kind, rq, sem, val, snap) in recs.get(name, []):
                if a0 >= p1 or p0 >= a1 or b0 >= c1 or c0 >= b1:
                    continue
                if not kind and (rq == q or (not wr and name != "PS")):
                    continue
                if val > todo.get(sem, (0, 0))[0]:
                    todo[sem] = (val, snap)
        for sem in sorted(todo, key=lambda k: -len(todo[k][1])):
            need(q, sem, todo[sem][0], todo[sem][1])

    def note(q, rq, sem, val, reads, writes):
        snap = dict(known[q])
        snap[sem] = val
        for view, wr in [(x, False) for x in reads] + [(x, True) for x in writes]:
            _, name, p0, p1, c0, c1 = view
            lst = recs.setdefault(name, [])
            if wr:
                lst[:] = [x for x in lst if not (x[0] >= p0 and x[1] <= p1 and x[2] >= c0 and x[3] <= c1)]
            lst.append((p0, p1, c0, c1, wr, rq, sem, val, snap))
        total[sem] = val

    def run(q, f, reads, writes):
        deps(q, reads, writes)
        sem = "c" + q
        cnt[sem] += 1
        f().then_inc(T.sem[sem], 1)
        note(q, q, sem, cnt[sem], reads, writes)

    def dma(q, out, in_, bits=0):
        w, x = [out] if out[1] else [], [in_] if in_[1] else []
        deps(q, x, w)
        sem = "d%d" % ndma[0]
        ndma[0] += 1
        o = out[0].bitcast(dt.uint8) if bits & 1 else out[0]
        i = in_[0].bitcast(dt.uint8) if bits & 2 else in_[0]
        q_of[q].dma_start(o, i).then_inc(T.sem[sem], 16)
        note(q, "dma", sem, 16, x, w)

    def move(dst, d0, src, s0, n):
        if n:
            dma("y", C(dst, d0, d0 + n), C(src, s0, s0 + n), bits=3)
            dma("y", C(dst + "S", d0, d0 + n), C(src + "S", s0, s0 + n))

    def memset(o, val):
        run("v", lambda: g.vector.memset(o[0], val), [], [o])

    def copy(q, o, i):
        run(q, (lambda: g.vector.tensor_copy(o[0], i[0])) if q == "v" else (lambda: g.scalar.activation(o[0], i[0], ACT.Copy)), [i], [o])

    def scaled(q, o, i, f):
        run(q, (lambda: g.vector.tensor_scalar(o[0], i[0], f, None, ALU.mult)) if q == "v" else
            (lambda: g.scalar.activation(o[0], i[0], ACT.Copy, scale=f)), [i], [o])

    def ts(o, i, s1, op0, s2=None, op1=None):
        rd = [i] + [x for x in (s1, s2) if isinstance(x, tuple)]
        a = s1[0] if isinstance(s1, tuple) else s1
        b = s2[0] if isinstance(s2, tuple) else s2
        run("v", (lambda: g.vector.tensor_scalar(o[0], i[0], a, None, op0)) if op1 is None else
            (lambda: g.vector.tensor_scalar(o[0], i[0], a, b, op0, op1)), rd, [o])

    def tt(o, a, b, op):
        run("v", lambda: g.vector.tensor_tensor(o[0], a[0], b[0], op), [a, b], [o])

    def tr(o, i):
        run("v", lambda: g.vector.transpose(o[0], i[0]), [i], [o])

    def total_of(q, o, i, junk=None):
        if q == "v":
            run("v", lambda: g.vector.tensor_reduce(o[0], i[0], AxisListType.X, ALU.add), [i], [o])
        else:
            run("s", lambda: g.scalar.activation(junk[0], i[0], ACT.Copy, accum_out=o[0]), [i], [o, junk])

    def pairsum(o, a, b, start=0.0):
        run("v", lambda: g.vector.tensor_tensor_scan(o[0], a[0], b[0], start, ALU.add, ALU.add), [a, b], [o])

    def affine(o, i, bias, scale, func=ACT.Identity, acc=None):
        rd = [i] + [x for x in (bias, scale) if isinstance(x, tuple)]
        b = bias[0] if isinstance(bias, tuple) else bias
        a = scale[0] if isinstance(scale, tuple) else scale
        if acc is None:
            run("s", lambda: g.scalar.activation(o[0], i[0], func, bias=b, scale=a), rd, [o])
        else:
            run("s", lambda: g.scalar.activation(o[0], i[0], func, bias=b, scale=a, accum_out=acc[0]), rd, [o, acc])

    def gather(q, o, win, off):
        src = win[0].indirect(off[0])
        run(q, (lambda: g.vector.tensor_copy(o[0], src)) if q == "v" else (lambda: g.scalar.activation(o[0], src, ACT.Copy)), [win, off], [o])

    def gathered(o, win, off, bias, scale, func):
        src = win[0].indirect(off[0])
        run("s", lambda: g.scalar.activation(o[0], src, func, bias=bias, scale=scale), [win, off], [o])

    def scatter(win, off, i):
        run("v", lambda: g.vector.tensor_copy(win[0].indirect(off[0]), i[0]), [i, off], [win])

    def quant(name, c0, c1, src):
        o, s = C(name, c0, c1), C(name + "S", c0, c1)
        run("v", lambda: g.vector.quantize_mx(o[0], s[0], src[0]), [src], [o, s])

    def mm(o, l, lc, x, x0, x1):
        a, b, c, d = C(l, lc, lc + 128), C(l + "S", lc, lc + 128), C(x, x0, x1), C(x + "S", x0, x1)
        run("t", lambda: g.tensor.matmul_mx(o[0], a[0], b[0], c[0], d[0], True, True), [a, b, c, d], [o])

    part = [False]

    def iota(o, pattern, base, cm, whole=False):
        now = o[3] - o[2] < 128
        if now or part[0]:
            need("g", "cg", cnt["cg"], {})
        part[0] = now
        run("g", (lambda: g.iota(o[0], pattern, base, cm)) if whole else
            (lambda: g.iota(o[0], pattern, base, cm, allow_small_or_imprecise_dtypes=True)), [], [o])

    def pick_codes(o, c0, c1, src, n, off):
        a, w = C(o, c0, c1), C(src, 0, n)
        run("v", lambda: g.vector.tensor_copy(a[0].bitcast(dt.uint32), w[0].bitcast(dt.uint32).indirect(off[0])), [w, off], [a])

    def pick_scales(o, c0, c1, src, n, off):
        gather("s", C(o + "S", c0, c1), C(src + "S", 0, n), off)

    def quadsum(o, h, lo, up, n, between=None):
        tt(H(h, 0, n), lo, up, ALU.add)
        if between:
            between()
        for q in range(4):
            tt(Q(o, q, 0, n), Q(h, 0, 0, n), Q(h, 1, 0, n), ALU.add)

    def swap(name):
        copy("s", H(name, 64, 96), U(name, 32, 64))
        copy("v", U(name, 64, 96), H(name, 32, 64))

    def pairs(name, order):
        for q in range(4):
            copy(order[q], Q(name, q, 96, 192), Q(name, q ^ 1, 0, 96))

    def kids(src, c0, n, t1, t2, first, pat, late=None):
        for i in range(8):
            k = (first + i) % 8
            mm(bank(k, n), "AQ" if i < 4 else "BQ", 128 * (i % 4), src, c0, c0 + n)
            if i == 7 and late:
                late()
            scaled(pat[i], part_of(t1 if i < 4 else t2, i % 4, 4 * n, 4), bank(k, n), 0.0625)

    def ways(a):
        return topo.engines(a, [c for c in T.cores if topo.chip(c) != topo.chip(a)][0])

    def split(a, b):
        if topo.chip(a) != topo.chip(b):
            return topo.engines(a, b)
        return [e for e in topo.engines(a, b) if e not in ways(a)][:2]

    def arrivals():
        return sum(len(split(c, core)) for c in T.cores if c != core)

    def fan(src, dst, base, width, arr):
        deps("g", [src], [])
        others = [c for c in T.cores if c != core]
        far = [c for c in others if topo.chip(c) != topo.chip(core)]
        near = [c for c in others if topo.chip(c) == topo.chip(core)]
        fe, ne = split(core, far[0]), split(core, near[0])

        def tf(dsts, eng):
            ids, aps = [], []
            for c in dsts:
                d = T.rank_of(c)
                k = base + width * (r if r < d else r - 1)
                rid, pid, _ = topo.addr(c)
                ids.append(DstId(rid=rid, pnc=pid))
                aps.append(T[dst][:, k:k + width])
            return RemoteDMATransfer(dst_ids=ids, dma_engine_mask=sum(1 << e for e in eng), remote_sem=T.sem[arr], srcs=[src[0]], dsts=aps)
        g.remote_dma_fused([tf(far, fe), tf(near, ne)], local_sem=T.sem.loc)
        loc[0] += len(fe) + len(ne)

    def halo(d, sfx):
        c = T.cores[d]
        dst, a, b = _land(d)
        c0, c1, at = (P - _halo(d)[0], P, a) if d > r else (0, _halo(d)[1], b)
        rid, pid, _ = topo.addr(c)
        s = C("W1" + sfx, hL + c0, hL + c1)
        deps("g", [s], [])
        o, i = T[dst + sfx][:, at:at + c1 - c0], s[0]
        if not sfx:
            o, i = o.bitcast(dt.uint8), i.bitcast(dt.uint8)
        g.remote_dma(o, i, T.sem.arh, T.sem.loc, pid, rid, sum(1 << e for e in ways(core)))
        loc[0] += len(ways(core))

    def arrive(sem, val, writes):
        for _, name, p0, p1, c0, c1 in writes:
            recs.setdefault(name, []).append((p0, p1, c0, c1, True, "far", sem, val, {sem: val}))
        total[sem] = val

    dma("s", C("U4"), ext(T.u[:, 0:4]))
    for name, t in (("XB", T.x), ("AB", T.a), ("BB", T.b), ("WB", T.w)):
        dma("y", C(name), ext(t[:, :]))

    iota(C("PIN"), [[0, 1]], 0, 1, True)
    iota(C("RK"), [[64, 6]], 2 * P * r, 0)
    iota(C("TI0"), [[64, 2], [1, 32]], 0, 0)
    iota(C("OI", 0, 2), [[0, 2]], 0, 0, True)
    iota(C("OI", 2, 4), [[0, 2]], 4, 0, True)
    upper = [(2, 4, -3)]
    at, nb, na = 4, r, N - 1 - r
    for what, s0, n in (("main", 0, nb), ("rest", 0, nb), ("rest", nb, na), ("main", nb, na)):
        if what == "main" and n:
            iota(C("OI", at, at + 2 * n), [[2, n], [0, 2]], 2 * s0, 0, True)
            at += 2 * n
        elif n:
            m = (n + 1) // 2
            iota(C("OI", at, at + 2 * m), [[4, m], [0, 2]], 2 * s0 + 1, 0, True)
            if n // 2:
                upper.append((at, at + 2 * (n // 2), 2))
            if n % 2:
                upper.append((at + n - 1, at + n + 1, 16 - (2 * s0 + 1 + 4 * (m - 1))))
            at += 2 * m
    cut = 32 * (nb + (nb + 1) // 2)
    memset(C("Z0"), 0.0)
    memset(C("OC"), -9e29)
    memset(C("land1", 16, 20), -9e29)
    memset(C("C64"), 64.0)
    copy("v", C("PID"), C("PIN"))
    for k, m in enumerate((31, 15, 32, 112)):
        ts(C("PA", k, k + 1), C("PIN"), m, ALU.bitwise_and)
    copy("v", C("BITS"), C("PA"))
    IC, PM16, QO, GR = [C("BITS", k, k + 1) for k in range(4)]
    affine(C("SG"), C("PID"), -63.5, 1.0, ACT.Sign)
    affine(C("I2"), IC, 0.0, 2.0)
    affine(C("TH"), IC, 64.0, -1.0)
    affine(C("GR"), GR, 0.0, 1.0, ACT.Sign)
    affine(C("QOB"), QO, float(-4 * HW), 1.0)
    affine(C("ISC"), C("SG"), 0.0, 1.0, ACT.Relu)
    affine(C("NT"), C("PID"), C("I2"), -1.0)
    affine(C("CLA"), PM16, C("PID"), -1.0)
    affine(C("GRP"), C("GR"), 2.0, -2.0)
    affine(C("SLT"), C("TI0", 0, 32), C("QOB"), 1.0)
    affine(C("CK"), C("I2"), C("ISC"), 1.0)
    affine(C("NTB"), C("NT"), P * r * TAU, -TAU)
    affine(C("THT"), C("TI0", 0, 32), C("TH"), 0.0)
    affine(C("SLT2"), C("SLT"), 64.0, 1.0)
    affine(C("NTN"), C("RK"), C("NTB"), -0.5 * TAU)
    affine(C("KEYC"), C("RK"), C("CK"), 1.0)
    affine(U("V2C"), U("RK"), U("I2"), 1.0)
    affine(C("CLP"), C("CLA"), C("GRP"), 2.0)
    affine(C("KEYN"), C("KEYC"), 0.0, -1.0)

    for t in range(4):
        ts(part_of("UB", t, 512, 4), C("Z0"), C("U4", t, t + 1), ALU.add)
    quant("UQ", 0, 128, C("UB"))
    quant("W1", hL, hL + P, C("XB"))
    pieces = [(d, sfx) for sfx in ("S", "") for d in (r - 1, r + 1) if 0 <= d < N]
    halo(*pieces[0])
    mm(bank(1, 128), "W1", hL, "UQ", 0, 128)
    mm(bank(2, 128), "W1", hL + 64, "UQ", 0, 128)
    mm(bank(0, P), "UQ", 0, "W1", hL, hL + P)
    copy("v", C("OC", 0, 1), bank(1, 1))
    copy("v", U("OC", 1, 2), bank(2, 1, 64, 128))
    copy("v", H("OC", 1, 2), bank(2, 1, 64, 128))
    fan(C("OC", 0, 2), "land1", 0, 2, "ar1")
    arrive("ar1", arrivals(), [C("land1", 0, 14)])
    for piece in pieces[1:]:
        halo(*piece)
    want = sum(2 * len(ways(T.cores[d])) for d in (r - 1, r + 1) if 0 <= d < N)
    hq, hl, hr = _land(r)
    arrive("arh", want, [C(hq + x, a, b) for x in ("", "S") for a, b in ((hl, hl + hL), (hr, hr + hR)) if b > a])
    iota(C("OI2", 0, 4), [[16, 2], [0, 2]], 0, 0)
    iota(C("OI2", 20, 22), [[0, 2]], 32, 0)
    iota(C("CTI"), [[2 * (G2 - G1) - 2, 2], [2, 16]], 2 * (G1 + ws), 0)
    for q in range(4):
        st, sh = (96 if q % 2 == 0 else -96), (32 if q < 2 else -32)
        iota(Q("OI2", q, 4, 12), [[st, 2], [16, 2], [0, 2]], 96 * (q % 2) + 32 + 32 * (q // 2), 0)
        iota(Q("OI2", q, 12, 20), [[sh, 2], [st, 2], [16, 2]], 96 * (q % 2) + 32 + 32 * (q // 2), 0)

    copy("v", C("OU"), C("OI"))
    for c0, c1, x in upper:
        ts(U("OU", c0, c1), U("OI", c0, c1), float(x), ALU.add)
    gather("s", C("OCB"), C("OC"), C("OU", 0, 4))
    tr(C("ST0"), bank(0, P))
    for k in range(6):
        affine(C("TIE", 64 * k, 64 * k + 64), C("TI0"), C("NTN", k, k + 1), TAU)
    tr(C("TOWN"), C("OCB"))
    quant("AQ", 0, 512, C("AB"))
    for k in range(6):
        ts(C("DL", 64 * k, 64 * k + 64), C("TOWN"), C("ST0", 32 * k, 32 * k + 1), ALU.subtract)
    for k in range(6):
        tt(C("CM", CW * k + 352, CW * k + CW), C("DL", 64 * k, 64 * k + 64), C("TIE", 64 * k, 64 * k + 64), ALU.is_gt)
    quant("BQ", 0, 512, C("BB"))
    copy("s", H("V2C"), C("ST0", 0, 192, 0, 64, 32))
    affine(C("CLB"), C("ISC"), C("CLP"), 1.0)
    affine(C("CLM"), C("ISC"), C("CLP"), -1.0)
    affine(C("CN"), C("ISC"), float(272 + 6 * DUMP), 2.0)
    affine(C("BL1"), C("ISC"), C("GRP"), -2.0)
    affine(C("BL2"), C("GRP"), -2.0, 1.0)
    for k in range(NV, 6):
        scaled("s", C("NST", k - NV, k - NV + 1), C("ST0", 32 * k, 32 * k + 1), -1.0)
    affine(C("BLT", 0, 16), C("TI0", 0, 16), C("BL1"), 0.0)
    affine(C("BLT", 16, 32), C("TI0", 0, 16), C("BL2"), 0.0)

    def last(k):
        return C("SCN", HW * k + HW - 1, HW * k + HW)

    def tally(k):
        pairsum(C("SCN", HW * k, HW * k + HW), C("CM", CW * k, CW * k + HW), C("CM", CW * k + HW, CW * k + CW), float(-HW))

    def against(k):
        sc = C("ST0", 32 * k, 32 * k + 1)
        if cut > 0:
            ts(C("CM", CW * k, CW * k + cut), C("LT", 0, cut), sc, ALU.is_ge)
        if cut < 352:
            ts(C("CM", CW * k + cut, CW * k + 352), C("LT", cut, 352), sc, ALU.is_gt)

    def signs(k):
        c, i, j = CW * k, k - NV, CW * (k - NV)
        affine(C("CM", c, c + 352), C("LT"), C("NST", i, i + 1), 1.0, ACT.Sign)
        if cut > 0:
            affine(C("J1", j, j + cut), C("CM", c, c + cut), 0.0, -1.0, ACT.Relu, C("LO", i, i + 1))
        affine(C("J1", j + cut, j + CW), C("CM", c + cut, c + CW), 0.0, 1.0, ACT.Relu, C("HI", i, i + 1))

    kids("W1", hL, P, "KH1", "KH2", 3, "ssssssss", lambda: gather("s", C("LB", 192, 352), C("land1", 0, 20), C("OU", 16, 26)))
    quant("W1", Wn + hL, Wn + hL + P, C("KH1"))
    gather("v", C("LB", 0, 192), C("land1", 0, 20), C("OU", 4, 16))
    tr(C("LT", 0, 192), C("LB", 0, 192))
    tr(C("LT", 192, 352), C("LB", 192, 352))
    mm(bank(3, P), "UQ", 0, "W1", Wn + hL, Wn + hL + P)
    signs(4)
    signs(5)
    against(0)
    against(1)
    tally(0)
    quant("W1", 2 * Wn + hL, 2 * Wn + hL + P, C("KH2"))
    mm(bank(4, P), "UQ", 0, "W1", 2 * Wn + hL, 2 * Wn + hL + P)
    against(2)
    tally(1)
    against(3)
    tally(2)
    tally(3)
    for k in range(NV, 6):
        i = k - NV
        if cut > 0:
            ts(last(k), C("HI", i, i + 1), C("LO", i, i + 1), ALU.subtract, float(cut - HW), ALU.add)
        else:
            ts(last(k), C("HI", i, i + 1), float(-HW), ALU.add)
    quadsum("PZ", "PB", C("SCN", HW - 1, None, 0, 64, HW), C("SCN", HW - 1, None, 64, 128, HW), 6, lambda: tr(H("VALT"), bank(3, P, 0, 64)))
    for k in range(6):
        affine(C("AD", 32 * k, 32 * k + 32), C("SLT"), C("PZ", k, k + 1), -1.0, ACT.Abs)
    for k in range(6):
        affine(C("EV", 32 * k, 32 * k + 32), C("AD", 32 * k, 32 * k + 32), C("KEYC", k, k + 1), C("KEYN", k, k + 1), ACT.Relu)

    def slots(v):
        for k in range(6):
            val = C("V2C", k, k + 1) if v == 1 else C("VALT", 32 * k, 32 * k + 1)
            ts(C("EV", 192 * v + 32 * k, 192 * v + 32 * k + 32), C("SLT2" if v == 1 else "SLT"), C("PZ", k, k + 1), ALU.is_equal, val, ALU.mult)
    slots(1)
    tr(U("VALT"), bank(4, P, 64, 128))
    tr(C("ET", 192, 384), C("EV", 192, 384))
    slots(2)
    tr(C("ET", 0, 192), C("EV", 0, 192))
    tr(C("ET", 384, 576), C("EV", 384, 576))
    total_of("s", H("land2", 380, 381), H("ET", 192, 384), H("J3", 192, 384))
    total_of("s", U("land2", 382, 383), U("ET", 192, 384), U("J3", 192, 384))
    copy("s", U("land2", 380, 381), H("land2", 380, 381))
    copy("s", H("land2", 382, 383), U("land2", 382, 383))
    for v, at in ((0, 3), (2, 1)):
        pairsum((T.land2[:, at:384:4], "land2", 0, 128, 380 + at, 381 + at), C("ET", 192 * v, 192 * v + 96), C("ET", 192 * v + 96, 192 * v + 192))
    fan(C("land2", 380, 384), "land2", 384, 4, "ar2")
    arrive("ar2", arrivals(), [C("land2", 384, 412)])

    iota(C("RA", e0 - 8, e0 + 232), [[0, 240]], 0, 0)
    iota(C("RB", e0 - 8, e0 + 232), [[0, 240]], 0, 0)
    iota(C("INI"), [[0, 1]], 0, 0)
    iota(C("RA", e0 - 8, e0 + 232, 0, 16), [[0, 240]], -2, 0)
    iota(C("INI", 0, 1, 0, 16), [[0, 1]], 320 - 2 * (E * r - ws - 1), 0)
    for t, x in (("VA", 1), ("VB", 0)):
        iota(H(t, 0, 32), [[0, 32]], -2 * Wn, 0)
        iota(U(t, 0, 32), [[2 * G3 - 4 * Wn, 2], [0, 16]], -2 * G3 + 2 * x, 0)
    iota(C("VA", 0, 32, 0, 16), [[0, 32]], -2 * Wn - 2, 0)
    iota(H("SEC"), [[0, 32]], 0, 0)
    iota(U("SEC"), [[0, 32]], 1, 0)
    iota(C("ZT"), [[0, 32]], 0, 0)
    for k in range(3):
        iota(C("HT", k * Wn, k * Wn + Wn), [[4, Wn]], 4 * ws + 2 * (k // 2), 0)
    iota(C("HT", G3, G3 + Wn), [[4, Wn]], 4 * ws + 1, 0)
    ks, kn = (0, hL + hR) if hq == "HQ" else (0 if hL else Wn - 128, 128)
    kids(hq, ks, kn, "FH1", "FH2", 5, "ssvsvssv")
    affine(C("CT", 0, 16), C("CTI", 0, 16), C("CLM"), 1.0)
    affine(C("CT", 16, 32), C("CTI", 16, 32), C("CLB"), 1.0)
    quant("HK1", 0, kn, C("FH1", 0, 4 * kn))
    quant("HK2", 0, kn, C("FH2", 0, 4 * kn))
    if hq == "HQ":
        move("W1", 0, "HQ", 0, hL)
        move("W1", hL + P, "HQ", hL, hR)
    for k in (1, 2):
        move("W1", k * Wn, "HK%d" % k, 0, hL)
        move("W1", k * Wn + hL + P, "HK%d" % k, kn - hR, hR)
    move("W2", 0, "W1", 0, 3 * Wn)
    move("W2", G3, "W1", 2 * Wn, Wn)
    ts(C("OD"), C("OI2", 0, 20), PM16, ALU.add)
    ts(C("OV"), C("OI2", 20, 22), IC, ALU.add)
    quant("WQ", 0, 128, C("WB"))

    for k in range(2):
        total_of("s", C("VV", k + 2, k + 3), C("land2", 382 + k, 412, step=4), C("JJ", 8 * k, 8 * k + 8))
        total_of("v", C("VV", k, k + 1), C("land2", 380 + k, 412, step=4))
    for k in range(2):
        ts(C("RBS", 32 * k, 32 * k + 32), C("C64"), 0.0, ALU.mult, C("VV", k, k + 1), ALU.add)
        affine(C("RBK", 32 * k, 32 * k + 32), C("C64"), C("VV", k + 2, k + 3), 0.0)
    affine(C("TK"), C("VV", 2, 3), 0.0, TAU)
    affine(C("KB"), C("VV", 3, 4), -BIG, 1.0)
    affine(C("NB"), C("VV", 2, 3), -BIG, 1.0)
    tr(C("SC", 0, 64), C("RBS"))
    tr(C("KY", 0, 64), C("RBK"))
    swap("SC")
    swap("KY")
    pairs("SC", "vsvs")
    pairs("KY", "vsvs")
    affine(C("E1"), C("SC"), C("VV", 1, 2), -1.0)
    ts(C("NK1"), C("KY"), C("VV", 3, 4), ALU.subtract, -TAU, ALU.mult)
    affine(C("E2"), C("SC", 32, 192), C("VV", 0, 1), -1.0)
    affine(C("NK2"), C("KY", 32, 192), C("TK"), -TAU)
    tt(C("M1"), C("E1"), C("NK1"), ALU.is_lt)
    tt(C("M2"), C("E2"), C("NK2"), ALU.is_lt)
    pairsum(C("R1"), C("M1", 0, 96), C("M1", 96, 192))
    pairsum(C("R2"), C("M2", 0, 80), C("M2", 80, 160))
    R1, R2 = C("R1", 95, 96), C("R2", 79, 80)
    gathered(C("GD"), C("KY"), C("OD", 4, 12), float(-ws), 0.5, ACT.Relu)
    for f, a in ((H, 64), (U, 32)):
        affine(f("FR", 192, 224), f("KY", a, a + 32), -BIG, 1.0)
        affine(f("FR", 224, 256), f("KY", a + 96, a + 128), -BIG, 1.0)
    affine(C("GE"), C("GD"), float(Wn - 1), -1.0, ACT.Relu)
    affine(C("NKA"), C("VV", 2, 3), C("CN"), 1.0)
    affine(C("Q1", 192, 256), C("FR", 192, 256), C("KB"), -1.0, ACT.Sign, C("S1A"))
    affine(C("Q2", 192, 256), C("FR", 192, 256), C("NB"), -1.0, ACT.Sign, C("C2A"))
    affine(C("KES"), C("VV", 3, 4), C("S1A"), 1.0)
    affine(C("NKE"), C("NKA"), C("C2A"), 1.0)
    for k in range(3):
        affine(C("KE", k, k + 1), C("KES"), float(272 + 2 * k * DUMP), 1.0)
    ts(C("FB", 32, 64), C("C64"), R1, ALU.is_gt, C("KB"), ALU.mult)
    ts(C("FB", 0, 32), C("THT"), R2, ALU.is_gt, C("NB"), ALU.mult)
    ts(C("FL"), C("C64", 0, 1), R1, ALU.is_gt)
    ts(C("F2"), C("THT", 0, 1), R2, ALU.is_gt)
    tr(C("FR", 0, 64), C("FB"))
    tr(C("GT"), C("GE"))
    swap("FR")
    for k in (0, 1):
        ts(C("OFFG", 4 * k, 4 * k + 4), C("GT", 0, 128, step=32), -1.0, ALU.mult, float((2 + k) * Wn - 1), ALU.add)
    pairs("FR", "vsvs")
    affine(C("Q1", 0, 192), C("FR", 0, 192), C("KB"), -1.0, ACT.Sign, C("S1"))
    affine(C("Q2", 0, 192), C("FR", 0, 192), C("NB"), -1.0, ACT.Sign, C("C2"))
    win, off, ct = C("KY", 0, 96), C("OV"), C("CT")
    run("v", lambda: g.vector.tensor_tensor(T.VA[:, 32:64], win[0].indirect(off[0]), ct[0], ALU.subtract), [win, off, ct], [C("VA", 32, 64)])
    for k, x in enumerate((2 * DUMP - 1, -2 * DUMP - 1, 1 - 4 * DUMP)):
        ts(C("DB", k, k + 1), C("FL"), float(x), ALU.mult, C("KE", k, k + 1), ALU.add)
    ts(C("DBN"), C("F2"), -6.0 * DUMP - 1, ALU.mult, C("NKE"), ALU.add)
    tt(C("VB", 32, 64), C("VA", 32, 64), C("BLT"), ALU.add)
    pick_codes("PK", 0, 128, "W1", 3 * Wn, C("OFFG"))
    ts(C("OFF", 1, 4), C("DB"), C("S1"), ALU.add, 0.5, ALU.mult)
    ts(C("OFF", 0, 1), C("C2"), C("DBN"), ALU.add, 0.5, ALU.mult)

    scatter(C("RB"), C("OFF"), C("VB"))
    scatter(C("RA"), C("OFF"), C("VA"))
    affine(C("EB"), C("S1"), float(2 * e0 - 1), -1.0)
    affine(C("BN"), C("DBN"), float(2 * e0 - 1), -1.0)
    affine(C("JK", 0, 2), C("DB", 0, 2), C("EB"), -1.0, ACT.Sign, C("A12"))
    affine(C("SGN"), C("C2"), C("BN"), -1.0, ACT.Sign)
    affine(C("SB1"), C("DB", 2, 3), C("EB"), -1.0, ACT.Sign)
    affine(C("AN"), C("SGN"), C("A12"), 1.0)
    pick_scales("PK", 0, 128, "W1", 3 * Wn, C("OFFG"))
    scaled("s", C("RB", e0 - 1, e0), C("RB", e0 - 1, e0), 0.0)
    affine(C("XS", 224, 256), C("SEC"), C("SB1"), C("AN"))
    xa, xb, x0, xo = C("RA", e0, e0 + 224), C("RB", e0 - 1, e0 + 223), C("INI"), C("XS", 0, 224)
    run("v", lambda: g.vector.tensor_tensor_scan(xo[0], xa[0], xb[0], x0[0], ALU.add, ALU.subtract), [xa, xb, x0], [xo])
    tr(C("XT"), C("XS"))
    gathered(C("HT", G1, G1 + 128), C("KY"), C("OD", 12, 20), 0.0, 2.0, ACT.Identity)
    total_of("s", C("ZS", 7, 8), C("XT", 224, 256), C("J3", 0, 32))
    tt(C("ZS", 0, 7), C("XT", 0, 224, step=32), C("XT", 16, 224, step=32), ALU.add)
    kids("PK", 0, 128, "GH1", "GH2", 5, "ssssssss")
    quadsum("ZT", "HS", H("ZS"), U("ZS"), 8)
    tr(C("XR"), C("ZT"))
    quant("W2", G1, G1 + 128, C("GH1"))
    gather("v", C("YY"), C("XR"), C("OD", 0, 4))
    tr(C("YT"), C("YY"))
    quant("W2", G2, G2 + 128, C("GH2"))
    for h in (0, 1):
        ts(part_of("OFFL", h, 14, 2), C("YT", 32 * h, 32 * h + 7), C("ZT", 7, 8), ALU.add, -0.5, ALU.mult)
    affine(C("HT", G2, G2 + 128), C("HT", G1, G1 + 128), 1.0, 1.0)
    for c0, c1 in ((0, 128), (128, E)):
        off = C("OFFL", c0 // 16, c1 // 16)
        pick_codes("FQ", c0, c1, "W2", G3 + Wn, off)
        pick_scales("FQ", c0, c1, "W2", G3 + Wn, off)
    mm(bank(0, 128), "WQ", 0, "FQ", 0, 128)
    mm(bank(1, 128), "WQ", 0, "FQ", E - 128, E)
    dma("y", ext(T.oc[:, :]), C("FQ"), bits=2)
    gather("s", C("HR"), C("HT", 0, G3 + Wn), C("OFFL", 0, 13))
    for k in range(4):
        dma("yyss"[k], ext(T.osc[4 * k:4 * k + 4, :]), C("FQS", 0, E, 32 * k, 32 * k + 4))
    copy("v", C("YS", 0, 128), bank(0, 128))
    dma("y", ext(T.y[:, 0:128]), C("YS", 0, 128))
    copy("v", C("YS", 128, E), bank(1, 128, 0, 128, 256 - E))
    dma("y", ext(T.y[:, 128:E]), C("YS", 128, E))
    dma("s", ext(T.hs[:, :]), C("HR", 0, E, 0, 1))

    total["loc"] = loc[0]
    for sem in SEMAPHORES:
        if total.get(sem):
            need("g", sem, total[sem], {})
